import numpy as np
import ml_dtypes


def mxq(x, axis, fmt="e4m3"):
    dtype, down = {"e4m3": (ml_dtypes.float8_e4m3fn, 7), "e5m2": (ml_dtypes.float8_e5m2, 14)}[fmt]
    v = np.moveaxis(np.asarray(x, np.float32).astype(ml_dtypes.bfloat16).astype(np.float64), axis, -1)
    blocks = v.reshape(v.shape[:-1] + (-1, 32))
    amax = np.abs(blocks).max(-1, keepdims=True)
    byte = np.maximum(np.where(amax > 0, np.frexp(amax)[1] - 1 + 127, 0) - down, 1)
    scale = np.exp2(byte - 127.0)
    codes = (blocks / scale).astype(np.float32).astype(dtype).astype(np.float64)
    return np.moveaxis((codes * scale).reshape(v.shape), -1, axis)


WIDE = False


def mx_kscale(k):
    if not WIDE:
        return np.ones(k)
    levels = np.array([10, -10, 5, -5, 0])
    if k % 512:
        return np.exp2(np.random.permutation(np.resize(levels, k // 32))).repeat(32)
    a = np.empty((k // 512, 16))
    for p in range(k // 512):
        a[p, :8] = np.random.permutation(np.resize(levels, 8))
        for g in range(8):
            far = levels[np.abs(levels - a[p, g]) >= 10]
            a[p, g + 8] = far[np.random.randint(len(far))]
    return np.exp2(a.ravel()).repeat(32)


def f64(x):
    return np.asarray(x).astype(np.float64)


def striped(idx):
    return np.tile(idx.reshape(-1, 16).T, (8, 1)).astype(np.uint16)


def unstriped(offs):
    return offs[:16].T.reshape(-1).astype(np.int64)


E2M1 = np.array([0.0, 0.5, 1.0, 1.5, 2.0, 3.0, 4.0, 6.0, -0.0, -0.5, -1.0, -1.5, -2.0, -3.0, -4.0, -6.0])


def pack_weight(w, fmt):
    k, n = w.shape
    w = f64(np.asarray(w, np.float32).astype(ml_dtypes.bfloat16)).reshape(k // 32, 32, n)
    amax = np.abs(w).max(1)
    if fmt == "e4m3":
        byte = np.frexp(amax)[1] - 1 + 127 - 7
    else:
        mant, ex = np.frexp(amax / 6.0)
        byte = np.where(mant > 0.5, ex, ex - 1) + 127
    byte = np.clip(np.where(amax > 0, byte, 1), 1, 254)
    scaled = (w * np.exp2(127.0 - byte)[:, None, :]).reshape(k, n).astype(np.float32)
    by_word = np.ascontiguousarray(scaled.reshape(k // 512, 128, 4, n).transpose(0, 1, 3, 2))
    if fmt == "e4m3":
        words = by_word.astype(ml_dtypes.float8_e4m3fn).view(np.uint8)
    else:
        c = by_word.astype(ml_dtypes.float4_e2m1fn).view(np.uint8) & 0xF
        words = (c[..., 0::2] | (c[..., 1::2] << 4)).reshape(k // 512, 128, 2 * n)
    return np.ascontiguousarray(words), np.ascontiguousarray(byte.astype(np.uint8).reshape(k // 512, 16, n))


def unpack_weight(words, scales, fmt):
    g, _, n = scales.shape
    words = np.ascontiguousarray(words).reshape(g, 128, n, -1)
    if fmt == "e4m3":
        vals = words.view(ml_dtypes.float8_e4m3fn).astype(np.float64)
    else:
        nib = np.empty((g, 128, n, 4), np.uint8)
        nib[..., 0::2] = words & 0xF
        nib[..., 1::2] = words >> 4
        vals = E2M1[nib]
    vals = vals * np.repeat(np.exp2(scales.astype(np.float64) - 127.0), 8, axis=1)[..., None]
    return vals.transpose(0, 1, 3, 2).reshape(g * 512, n)


def relu(v):
    return np.maximum(v, 0.0)


def d_relu(v):
    return (v > 0).astype(np.float64)


K, T, E, C, H, N = 256, 512, 8, 256, 512, 1024
TOP = 4


def by_expert(wq, xq):
    return np.concatenate([wq[e].T @ xq[:, e * C:(e + 1) * C] for e in range(E)], axis=1)


def setup_inputs():
    n = np.random.standard_normal
    s = mx_kscale(N)[:, None]
    u = mx_kscale(H)
    deal = np.repeat(np.arange(E), C).reshape(TOP, T)[:, np.random.permutation(T)]
    deal = np.take_along_axis(deal, np.argsort(np.random.rand(TOP, T), axis=0), axis=0)
    for _ in range(8):
        s_, t_ = np.random.permutation(T).reshape(2, -1); r = np.random.randint(TOP, size=T // 2); x, y = deal[r, s_].copy(), deal[r, t_].copy()
        ok = ~((deal[:, s_] == y).any(0) | (deal[:, t_] == x).any(0)); deal[r[ok], s_[ok]] = y[ok]; deal[r[ok], t_[ok]] = x[ok]
    order = np.lexsort((np.random.rand(TOP * T), deal.reshape(-1)))
    slot_token = order % T; pos = np.empty(TOP * T, np.int64); pos[order] = np.arange(TOP * T); pos = pos.reshape(TOP, T)
    g = np.random.uniform(0.5, 1.5, (TOP, T)); g = g / g.sum(0)
    w_slot = np.empty(E * C)
    for r in range(TOP): w_slot[pos[r]] = g[r]
    dy = pack_weight(n((N, T)) * s, "e4m3")
    w2 = [pack_weight(m, "e2m1") for m in n((E, N, H)) / np.sqrt(N) / s[None] * u[None, None, :]]
    w1 = [pack_weight(m, "e2m1") for m in n((E, H, K)) / np.sqrt(H) / u[None, :, None]]
    w3 = [pack_weight(m, "e2m1") for m in n((E, H, K)) / np.sqrt(H) / u[None, :, None]]
    return {
        "dy_words": dy[0],
        "dy_scales": dy[1],
        "a1": n((H, E * C)).astype(np.float32),
        "a3": n((H, E * C)).astype(np.float32),
        "w2_words": np.stack([m[0] for m in w2]),
        "w2_scales": np.stack([m[1] for m in w2]),
        "w1_words": np.stack([m[0] for m in w1]),
        "w1_scales": np.stack([m[1] for m in w1]),
        "w3_words": np.stack([m[0] for m in w3]),
        "w3_scales": np.stack([m[1] for m in w3]),
        "gate": np.tile(w_slot, (H, 1)).astype(np.float32),
        "offs": striped(slot_token),
        "pos1": striped(pos[0]),
        "pos2": striped(pos[1]),
        "pos3": striped(pos[2]),
        "pos4": striped(pos[3]),
    }


def reference(dy_words, dy_scales, a1, a3, w2_words, w2_scales, w1_words, w1_scales, w3_words, w3_scales, gate, offs, pos1, pos2, pos3, pos4):
    idx = unstriped(offs)
    w2 = np.stack([unpack_weight(w2_words[e], w2_scales[e], "e2m1") for e in range(E)])
    w1 = np.stack([unpack_weight(w1_words[e], w1_scales[e], "e2m1") for e in range(E)])
    w3 = np.stack([unpack_weight(w3_words[e], w3_scales[e], "e2m1") for e in range(E)])
    gq = unpack_weight(dy_words, dy_scales, "e4m3")[:, idx]
    dh = f64(gate) * by_expert(w2, gq)
    da1 = dh * f64(a3) * d_relu(f64(a1))
    da3 = dh * relu(f64(a1))
    dx = by_expert(w1, mxq(da1, 0, "e4m3")) + by_expert(w3, mxq(da3, 0, "e4m3"))
    return dx[:, unstriped(pos1)] + dx[:, unstriped(pos2)] + dx[:, unstriped(pos3)] + dx[:, unstriped(pos4)]

@@ -1,0 +1,198 @@
+from contextlib import ExitStack
+
+import concourse.mybir as mybir
+from concourse.masks import make_identity
+
+K, T, E, C, H, N = 256, 512, 8, 256, 512, 1024
+S = E * C
+P = 128
+FLOPS = 2 * S * (N * H + 2 * H * K)
+BYTES = (N * T + N * T // 32 + 2 * H * S * 4 + E * (N * H + 2 * H * K) // 2 + E * (N * H + 2 * H * K) // 32
+         + S * 4 + P * (S + 4 * T) // 16 * 2 + K * T * 4)
+
+F32 = mybir.dt.float32
+BF16 = mybir.dt.bfloat16
+I32 = mybir.dt.int32
+U32 = mybir.dt.uint32
+U16 = mybir.dt.uint16
+U8 = mybir.dt.uint8
+FP8X4 = mybir.dt.float8_e4m3fn_x4
+FP4X4 = mybir.dt.float4_e2m1fn_x4
+ACT = mybir.ActivationFunctionType
+MULT = mybir.AluOpType.mult
+ADD = mybir.AluOpType.add
+
+PASSES = N // 512
+
+
+def tile_moe_bdx_glu_relu_kernel(
+        tc, dy_words, dy_scales, a1, a3, w2_words, w2_scales, w1_words, w1_scales, w3_words, w3_scales,
+        gate, offs, pos1, pos2, pos3, pos4, out):
+    nc = tc.nc
+    with ExitStack() as ctx:
+        keep = ctx.enter_context(tc.tile_pool(name="keep", bufs=1))
+        ring = ctx.enter_context(tc.tile_pool(name="ring", bufs=3))
+        psum = ctx.enter_context(tc.psum_pool(name="psum", bufs=1))
+
+        offs_sb = keep.tile([P, S // 16], U16, name="offs_sb")
+        pos_sb = [keep.tile([P, T // 16], U16, name="pos_sb%d" % r) for r in range(4)]
+        dyw = keep.tile([P, PASSES * T], I32, name="dyw", align_bytes=64)
+        share = ctx.enter_context(tc.tile_pool(name="share", bufs=1))
+        dys = share.tile([P, 2048], U8, name="dys", align_bytes=64, offset=3072)
+        gs0 = keep.tile([P, S], U8, name="gs0", align_bytes=64)
+        gs1 = keep.tile([P, S], U8, name="gs1", align_bytes=64)
+        w2s = keep.tile([P, E * PASSES * H], U8, name="w2s", align_bytes=64)
+        gate_rows = keep.tile([P, P], F32, name="gate_rows")
+        gate_col = keep.tile([P, S // P], F32, name="gate_col")
+        ident = keep.tile([P, P], F32, name="ident")
+        dx = [keep.tile([P, S], F32, name="dx%d" % kb) for kb in range(2)]
+
+        nc.gpsimd.memset(dys[:, 0:T].bitcast(I32), 0)
+        nc.vector.memset(dys[:, T:].bitcast(I32), 0)
+        make_identity(nc, ident[:])
+
+        w2w, a1_sb, a3_sb = {}, {}, {}
+
+        def load_w2(e):
+            w2w[e] = ring.tile([P, PASSES * H * 2], U8, name="w2w", align_bytes=64)
+            nc.sync.dma_start(
+                out=w2w[e][:].bitcast(I32).rearrange("p (s b) -> p s b", s=PASSES),
+                in_=w2_words[e].rearrange("s p b -> p s b").bitcast(I32))
+
+        def load_saved(e):
+            for src, dst in ((a1, a1_sb), (a3, a3_sb)):
+                dst[e] = ring.tile([P, 4, C], F32, name="saved", bufs=5)
+                nc.sync.dma_start(out=dst[e][:], in_=src[:, e * C:(e + 1) * C].rearrange("(p r) j -> p r j", r=4))
+
+        def load_expert(e):
+            load_w2(e)
+            load_saved(e)
+
+        nc.sync.dma_start(offs_sb[:], offs)
+        nc.sync.dma_start(out=gate_rows[:], in_=gate[0:8, :].rearrange("h (b p) -> (h b) p", p=P))
+        load_w2(0)
+        for q in range(4):
+            nc.sync.dma_start(out=dys[32 * q:32 * q + 8, 0:T].bitcast(I32),
+                              in_=dy_scales[:, 4 * q:4 * q + 4, :].bitcast(I32))
+        nc.sync.dma_start(out=dyw[:].rearrange("p (o t) -> p o t", o=PASSES),
+                          in_=dy_words.rearrange("o p t d -> p o (t d)").bitcast(I32))
+        for q in range(4):
+            nc.sync.dma_start(
+                out=w2s[32 * q:32 * q + 4, :].bitcast(I32).rearrange("f (g i) -> f g i", g=E * PASSES),
+                in_=w2_scales[:, :, 4 * q:4 * q + 4, :].rearrange("e s f i -> f (e s) i").bitcast(I32))
+        load_saved(0)
+        load_expert(1)
+        for r, pos in enumerate((pos1, pos2, pos3, pos4)):
+            nc.sync.dma_start(pos_sb[r][:], pos)
+        load_expert(2)
+
+        gate_ps = psum.tile([P, P], F32, name="gate_ps")
+        nc.tensor.transpose(gate_ps[:], gate_rows[:], ident[:])
+        nc.scalar.copy(gate_col[:], gate_ps[:, 0:S // P])
+
+        for half in range(2):
+            nc.vector.tensor_copy(gs0[:, half * 1024:(half + 1) * 1024],
+                                  dys[:].indirect(offs_sb[:, half * 64:(half + 1) * 64]))
+        for q in range(4):
+            nc.sync.dma_start(out=gs1[32 * q:32 * q + 4, :].bitcast(I32),
+                                in_=gs0[32 * q + 4:32 * q + 8, :].bitcast(I32))
+        g_scales = (gs0, gs1)
+
+        w13s = share.tile([P, 2 * E * K], U8, name="w13s", align_bytes=64, offset=0)
+        w13w = share.tile([P, 2 * E * K * 2], U8, name="w13w", align_bytes=64, offset=4096)
+        for m, scales in enumerate((w1_scales, w3_scales)):
+            for q in range(4):
+                nc.sync.dma_start(
+                    out=w13s[32 * q:32 * q + 4, m * E * K:(m + 1) * E * K].bitcast(I32).rearrange("f (e k) -> f e k", e=E),
+                    in_=scales[:, 0, 4 * q:4 * q + 4, :].rearrange("e f k -> f e k").bitcast(I32))
+        for m, words in enumerate((w1_words, w3_words)):
+            nc.sync.dma_start(
+                out=w13w[:, m * E * K * 2:(m + 1) * E * K * 2].bitcast(I32).rearrange("p (e b) -> p e b", e=E),
+                in_=words[:, 0].rearrange("e p b -> p e b").bitcast(I32))
+
+        g_words = {}
+
+        def gather_words(e, s):
+            if s == 0:
+                g_words[e] = ring.tile([P, PASSES * C], U32, name="g_words", align_bytes=64, bufs=8)
+            nc.vector.tensor_copy(g_words[e][:, s * C:(s + 1) * C],
+                                  dyw[:, s * T:(s + 1) * T].bitcast(U32).indirect(offs_sb[:, 16 * e:16 * (e + 1)]))
+
+        AHEAD = 8
+        for e in range(AHEAD):
+            gather_words(e, 0)
+            gather_words(e, 1)
+
+        for e in range(E):
+            relu = ring.tile([P, 4 * C], F32, name="relu", bufs=4)
+            nc.scalar.activation(out=relu[:].rearrange("p (c i r) -> p c r i", i=2, r=4),
+                                 in_=a1_sb[e][:].rearrange("p r (c i) -> p c r i", i=2), func=ACT.Relu)
+            mask = ring.tile([P, 4 * C], BF16, name="mask", bufs=4)
+            nc.scalar.activation(out=mask[:], in_=relu[:], func=ACT.Sign)
+            y1 = ring.tile([P, 4 * C], BF16, name="y1")
+            da = ring.tile([P, 2 * 4 * C], BF16, name="da", align_bytes=64)
+            for h in range(2):
+                b = 2 * e + h
+                sums = psum.tile([P, H], F32, name="sums", bufs=2)
+                for s in range(PASSES):
+                    nc.tensor.matmul_mx(
+                        out=sums[:],
+                        lhsT=g_words[e][:, s * C + h * P:s * C + (h + 1) * P].bitcast(FP8X4),
+                        lhsT_scale=g_scales[s][:, b * P:(b + 1) * P],
+                        rhs=w2w[e][:, s * H * 2:(s + 1) * H * 2].bitcast(FP4X4),
+                        rhs_scale=w2s[:, (e * PASSES + s) * H:(e * PASSES + s + 1) * H],
+                        start=(s == 0), stop=(s == PASSES - 1))
+                dh_t = ring.tile([P, 4, P], F32, name="dh_t")
+                nc.scalar.activation(out=dh_t[:], in_=sums[:].rearrange("j (p r) -> j r p", r=4),
+                                     func=ACT.Copy, scale=gate_col[:, b:b + 1])
+                dh = psum.tile([P, 4, P], F32, name="dh", bufs=3)
+                for r in range(4):
+                    nc.tensor.transpose(dh[:, r, :], dh_t[:, r, :], ident[:])
+                cols = slice(h * 4 * P, (h + 1) * 4 * P)
+                nc.vector.tensor_tensor(
+                    y1[:, cols].rearrange("p (c i r) -> p c r i", i=2, r=4),
+                    dh[:].rearrange("p r (c i) -> p c r i", i=2),
+                    a3_sb[e][:, :, h * P:(h + 1) * P].rearrange("p r (c i) -> p c r i", i=2), MULT)
+                nc.vector.tensor_tensor(
+                    da[:, 4 * C + h * 4 * P:4 * C + (h + 1) * 4 * P].rearrange("p (j r) -> p j r", r=4),
+                    dh[:].rearrange("p r j -> p j r"),
+                    relu[:, cols].rearrange("p (j r) -> p j r", r=4), MULT)
+            if e + AHEAD < E:
+                gather_words(e + AHEAD, 0)
+            nc.vector.tensor_tensor(da[:, 0:4 * C], y1[:], mask[:], MULT)
+            if e + AHEAD < E:
+                gather_words(e + AHEAD, 1)
+            if e + 3 < E:
+                load_expert(e + 3)
+            codes = ring.tile([P, 2 * C], U32, name="codes", align_bytes=64)
+            scales = ring.tile([P, 2 * C], U8, name="scales", align_bytes=64)
+            nc.vector.quantize_mx(out=codes[:].bitcast(FP8X4), scales=scales[:], in_=da[:])
+            acc = psum.tile([P, 2, C], F32, name="acc", bufs=2)
+            for kb in range(2):
+                for h in range(2):
+                    for m in range(2):
+                        nc.tensor.matmul_mx(
+                            out=acc[:, kb, h * P:(h + 1) * P],
+                            lhsT=w13w[:, ((m * E + e) * K + kb * P) * 2:((m * E + e) * K + (kb + 1) * P) * 2].bitcast(FP4X4),
+                            lhsT_scale=w13s[:, (m * E + e) * K + kb * P:(m * E + e) * K + (kb + 1) * P],
+                            rhs=codes[:, m * C + h * P:m * C + (h + 1) * P].bitcast(FP8X4),
+                            rhs_scale=scales[:, m * C + h * P:m * C + (h + 1) * P],
+                            start=(m == 0), stop=(m == 1))
+            for kb in range(2):
+                nc.scalar.copy(dx[kb][:, e * C:(e + 1) * C], acc[:, kb, :])
+
+        HALF = T // 2
+        for kb in range(2):
+            part = [[keep.tile([P, HALF], F32, name="part%d_%d_%d" % (kb, h, r)) for r in range(3)] for h in range(2)]
+            res = keep.tile([P, T], F32, name="res%d" % kb)
+            for r in range(4):
+                for h in range(2):
+                    picked = dx[kb][:].indirect(pos_sb[r][:, h * HALF // 16:(h + 1) * HALF // 16])
+                    if r == 0:
+                        nc.vector.tensor_copy(part[h][0][:], picked)
+                    else:
+                        dst = part[h][r][:] if r < 3 else res[:, h * HALF:(h + 1) * HALF]
+                        nc.vector.tensor_tensor(dst, picked, part[h][r - 1][:], ADD)
+            for h in range(2):
+                nc.sync.dma_start(out=out[kb * P:(kb + 1) * P, h * HALF:(h + 1) * HALF],
+                                  in_=res[:, h * HALF:(h + 1) * HALF])

@@ -36,7 +36,7 @@ def tile_moe_bdx_glu_relu_kernel(
 
         offs_sb = keep.tile([P, S // 16], U16, name="offs_sb")
         pos_sb = [keep.tile([P, T // 16], U16, name="pos_sb%d" % r) for r in range(4)]
-        dyw = keep.tile([P, PASSES * T], I32, name="dyw", align_bytes=64)
+        dyw = ring.tile([P, (PASSES + 1) * T], I32, name="dyw", tag="a3", align_bytes=64)
         share = ctx.enter_context(tc.tile_pool(name="share", bufs=1))
         dys = share.tile([P, 2048], U8, name="dys", align_bytes=64, offset=3072)
         gs0 = keep.tile([P, S], U8, name="gs0", align_bytes=64)
@@ -49,6 +49,7 @@ def tile_moe_bdx_glu_relu_kernel(
 
         nc.gpsimd.memset(dys[:, 0:T].bitcast(I32), 0)
         nc.vector.memset(dys[:, T:].bitcast(I32), 0)
+        nc.vector.memset(dyw[:, PASSES * T:], 0)
         make_identity(nc, ident[:])
 
         w2w, a1_sb, a3_sb = {}, {}, {}
@@ -59,14 +60,9 @@ def tile_moe_bdx_glu_relu_kernel(
                 out=w2w[e][:].bitcast(I32).rearrange("p (s b) -> p s b", s=PASSES),
                 in_=w2_words[e].rearrange("s p b -> p s b").bitcast(I32))
 
-        def load_saved(e):
-            for src, dst in ((a1, a1_sb), (a3, a3_sb)):
-                dst[e] = ring.tile([P, 4, C], F32, name="saved", bufs=5)
-                nc.sync.dma_start(out=dst[e][:], in_=src[:, e * C:(e + 1) * C].rearrange("(p r) j -> p r j", r=4))
-
-        def load_expert(e):
-            load_w2(e)
-            load_saved(e)
+        def load_saved(src, dst, tag, e):
+            dst[e] = ring.tile([P, 4, C], F32, name=tag + "_sb", tag=tag, align_bytes=64)
+            nc.sync.dma_start(out=dst[e][:], in_=src[:, e * C:(e + 1) * C].rearrange("(p r) j -> p r j", r=4))
 
         nc.sync.dma_start(offs_sb[:], offs)
         nc.sync.dma_start(out=gate_rows[:], in_=gate[0:8, :].rearrange("h (b p) -> (h b) p", p=P))
@@ -74,17 +70,21 @@ def tile_moe_bdx_glu_relu_kernel(
         for q in range(4):
             nc.sync.dma_start(out=dys[32 * q:32 * q + 8, 0:T].bitcast(I32),
                               in_=dy_scales[:, 4 * q:4 * q + 4, :].bitcast(I32))
-        nc.sync.dma_start(out=dyw[:].rearrange("p (o t) -> p o t", o=PASSES),
+        nc.sync.dma_start(out=dyw[:, 0:PASSES * T].rearrange("p (o t) -> p o t", o=PASSES),
                           in_=dy_words.rearrange("o p t d -> p o (t d)").bitcast(I32))
         for q in range(4):
             nc.sync.dma_start(
                 out=w2s[32 * q:32 * q + 4, :].bitcast(I32).rearrange("f (g i) -> f g i", g=E * PASSES),
                 in_=w2_scales[:, :, 4 * q:4 * q + 4, :].rearrange("e s f i -> f (e s) i").bitcast(I32))
-        load_saved(0)
-        load_expert(1)
+        load_saved(a1, a1_sb, "a1", 0)
+        load_w2(1)
+        load_saved(a1, a1_sb, "a1", 1)
         for r, pos in enumerate((pos1, pos2, pos3, pos4)):
             nc.sync.dma_start(pos_sb[r][:], pos)
-        load_expert(2)
+        load_saved(a1, a1_sb, "a1", 2)
+        load_saved(a3, a3_sb, "a3", 0)
+        load_w2(2)
+        load_saved(a3, a3_sb, "a3", 1)
 
         gate_ps = psum.tile([P, P], F32, name="gate_ps")
         nc.tensor.transpose(gate_ps[:], gate_rows[:], ident[:])
@@ -110,25 +110,41 @@ def tile_moe_bdx_glu_relu_kernel(
                 out=w13w[:, m * E * K * 2:(m + 1) * E * K * 2].bitcast(I32).rearrange("p (e b) -> p e b", e=E),
                 in_=words[:, 0].rearrange("e p b -> p e b").bitcast(I32))
 
-        g_words = {}
+        g_words = []
+        for pair in range(E // 2):
+            g_words.append(keep.tile([P, PASSES * 2 * C], U32, name="g_words%d" % pair, align_bytes=64))
+            for s in range(PASSES):
+                nc.vector.tensor_copy(
+                    g_words[pair][:, s * 2 * C:(s + 1) * 2 * C],
+                    dyw[:, s * T:(s + 2) * T].bitcast(U32).indirect(offs_sb[:, 32 * pair:32 * (pair + 1)]))
+        load_saved(a3, a3_sb, "a3", 2)
 
-        def gather_words(e, s):
-            if s == 0:
-                g_words[e] = ring.tile([P, PASSES * C], U32, name="g_words", align_bytes=64, bufs=8)
-            nc.vector.tensor_copy(g_words[e][:, s * C:(s + 1) * C],
-                                  dyw[:, s * T:(s + 1) * T].bitcast(U32).indirect(offs_sb[:, 16 * e:16 * (e + 1)]))
+        def second_product(e, da):
+            codes = ring.tile([P, 2 * C], U32, name="codes", align_bytes=64)
+            scales = ring.tile([P, 2 * C], U8, name="scales", align_bytes=64)
+            nc.vector.quantize_mx(out=codes[:].bitcast(FP8X4), scales=scales[:], in_=da[:])
+            for kb in range(2):
+                acc = psum.tile([P, C], F32, name="acc%d" % kb)
+                for h in range(2):
+                    for m in range(2):
+                        nc.tensor.matmul_mx(
+                            out=acc[:, h * P:(h + 1) * P],
+                            lhsT=w13w[:, ((m * E + e) * K + kb * P) * 2:((m * E + e) * K + (kb + 1) * P) * 2].bitcast(FP4X4),
+                            lhsT_scale=w13s[:, (m * E + e) * K + kb * P:(m * E + e) * K + (kb + 1) * P],
+                            rhs=codes[:, m * C + h * P:m * C + (h + 1) * P].bitcast(FP8X4),
+                            rhs_scale=scales[:, m * C + h * P:m * C + (h + 1) * P],
+                            start=(m == 0), stop=(m == 1))
+                nc.scalar.copy(dx[kb][:, e * C:(e + 1) * C], acc[:])
 
-        AHEAD = 8
-        for e in range(AHEAD):
-            gather_words(e, 0)
-            gather_words(e, 1)
-
+        waiting = None
         for e in range(E):
-            relu = ring.tile([P, 4 * C], F32, name="relu", bufs=4)
+            relu = keep.tile([P, 4 * C], F32, name="relu%d" % e)
             nc.scalar.activation(out=relu[:].rearrange("p (c i r) -> p c r i", i=2, r=4),
                                  in_=a1_sb[e][:].rearrange("p r (c i) -> p c r i", i=2), func=ACT.Relu)
-            mask = ring.tile([P, 4 * C], BF16, name="mask", bufs=4)
+            mask = keep.tile([P, 4 * C], BF16, name="mask%d" % e)
             nc.scalar.activation(out=mask[:], in_=relu[:], func=ACT.Sign)
+            if e + 3 < E:
+                load_saved(a1, a1_sb, "a1", e + 3)
             y1 = ring.tile([P, 4 * C], BF16, name="y1")
             da = ring.tile([P, 2 * 4 * C], BF16, name="da", align_bytes=64)
             for h in range(2):
@@ -137,7 +153,7 @@ def tile_moe_bdx_glu_relu_kernel(
                 for s in range(PASSES):
                     nc.tensor.matmul_mx(
                         out=sums[:],
-                        lhsT=g_words[e][:, s * C + h * P:s * C + (h + 1) * P].bitcast(FP8X4),
+                        lhsT=g_words[e // 2][:, s * 2 * C + (b % 4) * P:s * 2 * C + (b % 4 + 1) * P].bitcast(FP8X4),
                         lhsT_scale=g_scales[s][:, b * P:(b + 1) * P],
                         rhs=w2w[e][:, s * H * 2:(s + 1) * H * 2].bitcast(FP4X4),
                         rhs_scale=w2s[:, (e * PASSES + s) * H:(e * PASSES + s + 1) * H],
@@ -153,33 +169,18 @@ def tile_moe_bdx_glu_relu_kernel(
                     y1[:, cols].rearrange("p (c i r) -> p c r i", i=2, r=4),
                     dh[:].rearrange("p r (c i) -> p c r i", i=2),
                     a3_sb[e][:, :, h * P:(h + 1) * P].rearrange("p r (c i) -> p c r i", i=2), MULT)
+                if h == 0 and waiting is not None:
+                    second_product(*waiting)
                 nc.vector.tensor_tensor(
                     da[:, 4 * C + h * 4 * P:4 * C + (h + 1) * 4 * P].rearrange("p (j r) -> p j r", r=4),
                     dh[:].rearrange("p r j -> p j r"),
                     relu[:, cols].rearrange("p (j r) -> p j r", r=4), MULT)
-            if e + AHEAD < E:
-                gather_words(e + AHEAD, 0)
             nc.vector.tensor_tensor(da[:, 0:4 * C], y1[:], mask[:], MULT)
-            if e + AHEAD < E:
-                gather_words(e + AHEAD, 1)
             if e + 3 < E:
-                load_expert(e + 3)
-            codes = ring.tile([P, 2 * C], U32, name="codes", align_bytes=64)
-            scales = ring.tile([P, 2 * C], U8, name="scales", align_bytes=64)
-            nc.vector.quantize_mx(out=codes[:].bitcast(FP8X4), scales=scales[:], in_=da[:])
-            acc = psum.tile([P, 2, C], F32, name="acc", bufs=2)
-            for kb in range(2):
-                for h in range(2):
-                    for m in range(2):
-                        nc.tensor.matmul_mx(
-                            out=acc[:, kb, h * P:(h + 1) * P],
-                            lhsT=w13w[:, ((m * E + e) * K + kb * P) * 2:((m * E + e) * K + (kb + 1) * P) * 2].bitcast(FP4X4),
-                            lhsT_scale=w13s[:, (m * E + e) * K + kb * P:(m * E + e) * K + (kb + 1) * P],
-                            rhs=codes[:, m * C + h * P:m * C + (h + 1) * P].bitcast(FP8X4),
-                            rhs_scale=scales[:, m * C + h * P:m * C + (h + 1) * P],
-                            start=(m == 0), stop=(m == 1))
-            for kb in range(2):
-                nc.scalar.copy(dx[kb][:, e * C:(e + 1) * C], acc[:, kb, :])
+                load_w2(e + 3)
+                load_saved(a3, a3_sb, "a3", e + 3)
+            waiting = (e, da)
+        second_product(*waiting)
 
         HALF = T // 2
         for kb in range(2):

@@ -21,8 +21,12 @@ FP4X4 = mybir.dt.float4_e2m1fn_x4
 ACT = mybir.ActivationFunctionType
 MULT = mybir.AluOpType.mult
 ADD = mybir.AluOpType.add
+MIN = mybir.AluOpType.min
+MAX = mybir.AluOpType.max
+F32_MAX = 3.4028234663852886e38
 
 PASSES = N // 512
+EARLY = 2
 
 
 def tile_moe_bdx_glu_relu_kernel(
@@ -36,9 +40,10 @@ def tile_moe_bdx_glu_relu_kernel(
 
         offs_sb = keep.tile([P, S // 16], U16, name="offs_sb")
         pos_sb = [keep.tile([P, T // 16], U16, name="pos_sb%d" % r) for r in range(4)]
-        dyw = ring.tile([P, (PASSES + 1) * T], I32, name="dyw", tag="a3", align_bytes=64)
+        dyw = keep.tile([P, (PASSES + 1) * T], I32, name="dyw", align_bytes=64)
         share = ctx.enter_context(tc.tile_pool(name="share", bufs=1))
-        dys = share.tile([P, 2048], U8, name="dys", align_bytes=64, offset=3072)
+        late_bytes = 2 * (E - EARLY) * 4 * C * 4
+        dys = share.tile([P, 2048], U8, name="dys", align_bytes=64, offset=late_bytes - 64)
         gs0 = keep.tile([P, S], U8, name="gs0", align_bytes=64)
         gs1 = keep.tile([P, S], U8, name="gs1", align_bytes=64)
         w2s = keep.tile([P, E * PASSES * H], U8, name="w2s", align_bytes=64)
@@ -54,19 +59,26 @@ def tile_moe_bdx_glu_relu_kernel(
 
         w2w, a1_sb, a3_sb = {}, {}, {}
 
-        def load_w2(e):
-            w2w[e] = ring.tile([P, PASSES * H * 2], U8, name="w2w", align_bytes=64)
+        def load_w2(dst, e0, n):
             nc.sync.dma_start(
-                out=w2w[e][:].bitcast(I32).rearrange("p (s b) -> p s b", s=PASSES),
-                in_=w2_words[e].rearrange("s p b -> p s b").bitcast(I32))
+                out=dst.bitcast(I32).rearrange("p (g b) -> p g b", g=n * PASSES),
+                in_=w2_words[e0:e0 + n].rearrange("e s p b -> p (e s) b").bitcast(I32))
+            for e in range(n):
+                w2w[e0 + e] = dst[:, e * PASSES * H * 2:(e + 1) * PASSES * H * 2]
 
-        def load_saved(src, dst, tag, e):
-            dst[e] = ring.tile([P, 4, C], F32, name=tag + "_sb", tag=tag, align_bytes=64)
-            nc.sync.dma_start(out=dst[e][:], in_=src[:, e * C:(e + 1) * C].rearrange("(p r) j -> p r j", r=4))
+        def load_saved(src, held, dst, e0, n):
+            rows = dst.rearrange("p (r j) -> p r j", r=4)
+            nc.sync.dma_start(out=rows, in_=src[:, e0 * C:(e0 + n) * C].rearrange("(p r) j -> p r j", r=4))
+            for e in range(n):
+                held[e0 + e] = rows[:, :, e * C:(e + 1) * C]
+
+        early_w2 = [keep.tile([P, PASSES * H * 2], U8, name="early_w2_%d" % e, align_bytes=64) for e in range(EARLY)]
+        early_a1 = [keep.tile([P, 4 * C], F32, name="early_a1_%d" % e) for e in range(EARLY)]
+        early_a3 = [keep.tile([P, 4 * C], F32, name="early_a3_%d" % e) for e in range(EARLY)]
 
         nc.sync.dma_start(offs_sb[:], offs)
         nc.sync.dma_start(out=gate_rows[:], in_=gate[0:8, :].rearrange("h (b p) -> (h b) p", p=P))
-        load_w2(0)
+        load_w2(early_w2[0][:], 0, 1)
         for q in range(4):
             nc.sync.dma_start(out=dys[32 * q:32 * q + 8, 0:T].bitcast(I32),
                               in_=dy_scales[:, 4 * q:4 * q + 4, :].bitcast(I32))
@@ -76,17 +88,15 @@ def tile_moe_bdx_glu_relu_kernel(
             nc.sync.dma_start(
                 out=w2s[32 * q:32 * q + 4, :].bitcast(I32).rearrange("f (g i) -> f g i", g=E * PASSES),
                 in_=w2_scales[:, :, 4 * q:4 * q + 4, :].rearrange("e s f i -> f (e s) i").bitcast(I32))
-        load_saved(a1, a1_sb, "a1", 0)
-        load_w2(1)
-        load_saved(a1, a1_sb, "a1", 1)
+        load_saved(a1, a1_sb, early_a1[0][:], 0, 1)
+        load_saved(a3, a3_sb, early_a3[0][:], 0, 1)
+        load_w2(early_w2[1][:], 1, 1)
+        load_saved(a1, a1_sb, early_a1[1][:], 1, 1)
         for r, pos in enumerate((pos1, pos2, pos3, pos4)):
             nc.sync.dma_start(pos_sb[r][:], pos)
-        load_saved(a1, a1_sb, "a1", 2)
-        load_saved(a3, a3_sb, "a3", 0)
-        load_w2(2)
-        load_saved(a3, a3_sb, "a3", 1)
+        load_saved(a3, a3_sb, early_a3[1][:], 1, 1)
 
-        gate_ps = psum.tile([P, P], F32, name="gate_ps")
+        gate_ps = psum.tile([P, P], F32, name="gate_ps", tag="acc0")
         nc.tensor.transpose(gate_ps[:], gate_rows[:], ident[:])
         nc.scalar.copy(gate_col[:], gate_ps[:, 0:S // P])
 
@@ -98,17 +108,32 @@ def tile_moe_bdx_glu_relu_kernel(
                                 in_=gs0[32 * q + 4:32 * q + 8, :].bitcast(I32))
         g_scales = (gs0, gs1)
 
-        w13s = share.tile([P, 2 * E * K], U8, name="w13s", align_bytes=64, offset=0)
-        w13w = share.tile([P, 2 * E * K * 2], U8, name="w13w", align_bytes=64, offset=4096)
+        saved = share.tile([P, late_bytes // 4], F32, name="saved", align_bytes=64, offset=0)
+        w13s_bytes, w13w_bytes, pair_w2 = 2 * E * K, 2 * E * K * 2, 2 * PASSES * H * 2
+        weights = share.tile([P, w13s_bytes + w13w_bytes + (E - EARLY) // 2 * pair_w2], U8, name="weights",
+                             align_bytes=64, offset=late_bytes + 2048 - 128)
+        w13s = weights[:, 0:w13s_bytes]
+        w13w = weights[:, w13s_bytes:w13s_bytes + w13w_bytes]
+
+        def load_pair(e0):
+            at = (e0 - EARLY) * 2 * 4 * C
+            load_saved(a1, a1_sb, saved[:, at:at + 8 * C], e0, 2)
+            load_saved(a3, a3_sb, saved[:, at + 8 * C:at + 16 * C], e0, 2)
+            at = w13s_bytes + w13w_bytes + (e0 - EARLY) // 2 * pair_w2
+            load_w2(weights[:, at:at + pair_w2], e0, 2)
+
         for m, scales in enumerate((w1_scales, w3_scales)):
             for q in range(4):
                 nc.sync.dma_start(
                     out=w13s[32 * q:32 * q + 4, m * E * K:(m + 1) * E * K].bitcast(I32).rearrange("f (e k) -> f e k", e=E),
                     in_=scales[:, 0, 4 * q:4 * q + 4, :].rearrange("e f k -> f e k").bitcast(I32))
+        load_pair(EARLY)
         for m, words in enumerate((w1_words, w3_words)):
             nc.sync.dma_start(
                 out=w13w[:, m * E * K * 2:(m + 1) * E * K * 2].bitcast(I32).rearrange("p (e b) -> p e b", e=E),
                 in_=words[:, 0].rearrange("e p b -> p e b").bitcast(I32))
+        for e0 in range(EARLY + 2, E, 2):
+            load_pair(e0)
 
         g_words = []
         for pair in range(E // 2):
@@ -117,14 +142,13 @@ def tile_moe_bdx_glu_relu_kernel(
                 nc.vector.tensor_copy(
                     g_words[pair][:, s * 2 * C:(s + 1) * 2 * C],
                     dyw[:, s * T:(s + 2) * T].bitcast(U32).indirect(offs_sb[:, 32 * pair:32 * (pair + 1)]))
-        load_saved(a3, a3_sb, "a3", 2)
 
         def second_product(e, da):
             codes = ring.tile([P, 2 * C], U32, name="codes", align_bytes=64)
             scales = ring.tile([P, 2 * C], U8, name="scales", align_bytes=64)
             nc.vector.quantize_mx(out=codes[:].bitcast(FP8X4), scales=scales[:], in_=da[:])
             for kb in range(2):
-                acc = psum.tile([P, C], F32, name="acc%d" % kb)
+                acc = psum.tile([P, C], F32, name="acc", tag="acc%d" % kb)
                 for h in range(2):
                     for m in range(2):
                         nc.tensor.matmul_mx(
@@ -138,13 +162,18 @@ def tile_moe_bdx_glu_relu_kernel(
 
         waiting = None
         for e in range(E):
-            relu = keep.tile([P, 4 * C], F32, name="relu%d" % e)
-            nc.scalar.activation(out=relu[:].rearrange("p (c i r) -> p c r i", i=2, r=4),
-                                 in_=a1_sb[e][:].rearrange("p r (c i) -> p c r i", i=2), func=ACT.Relu)
-            mask = keep.tile([P, 4 * C], BF16, name="mask%d" % e)
+            relu = ring.tile([P, 4 * C], F32, name="relu", bufs=4)
+            a3w = ring.tile([P, 4 * C], F32, name="a3w", bufs=4)
+            for h in range(2):
+                nc.gpsimd.tensor_scalar(
+                    relu[:, h * 4 * P:(h + 1) * 4 * P].rearrange("p (j r) -> p j r", r=4),
+                    a1_sb[e][:, :, h * P:(h + 1) * P].rearrange("p r j -> p j r"), F32_MAX, 0.0, MIN, MAX)
+            for h in range(2):
+                nc.gpsimd.tensor_scalar(
+                    a3w[:, h * 4 * P:(h + 1) * 4 * P].rearrange("p (j r) -> p j r", r=4),
+                    a3_sb[e][:, :, h * P:(h + 1) * P].rearrange("p r j -> p j r"), 1.0, 0.0, MULT, ADD)
+            mask = ring.tile([P, 4 * C], BF16, name="mask", bufs=4)
             nc.scalar.activation(out=mask[:], in_=relu[:], func=ACT.Sign)
-            if e + 3 < E:
-                load_saved(a1, a1_sb, "a1", e + 3)
             y1 = ring.tile([P, 4 * C], BF16, name="y1")
             da = ring.tile([P, 2 * 4 * C], BF16, name="da", align_bytes=64)
             for h in range(2):
@@ -161,14 +190,14 @@ def tile_moe_bdx_glu_relu_kernel(
                 dh_t = ring.tile([P, 4, P], F32, name="dh_t")
                 nc.scalar.activation(out=dh_t[:], in_=sums[:].rearrange("j (p r) -> j r p", r=4),
                                      func=ACT.Copy, scale=gate_col[:, b:b + 1])
-                dh = psum.tile([P, 4, P], F32, name="dh", bufs=3)
+                dh = psum.tile([P, 4, P], F32, name="dh", bufs=4)
                 for r in range(4):
                     nc.tensor.transpose(dh[:, r, :], dh_t[:, r, :], ident[:])
                 cols = slice(h * 4 * P, (h + 1) * 4 * P)
                 nc.vector.tensor_tensor(
-                    y1[:, cols].rearrange("p (c i r) -> p c r i", i=2, r=4),
-                    dh[:].rearrange("p r (c i) -> p c r i", i=2),
-                    a3_sb[e][:, :, h * P:(h + 1) * P].rearrange("p r (c i) -> p c r i", i=2), MULT)
+                    y1[:, cols].rearrange("p (j r) -> p j r", r=4),
+                    dh[:].rearrange("p r j -> p j r"),
+                    a3w[:, cols].rearrange("p (j r) -> p j r", r=4), MULT)
                 if h == 0 and waiting is not None:
                     second_product(*waiting)
                 nc.vector.tensor_tensor(
@@ -176,9 +205,6 @@ def tile_moe_bdx_glu_relu_kernel(
                     dh[:].rearrange("p r j -> p j r"),
                     relu[:, cols].rearrange("p (j r) -> p j r", r=4), MULT)
             nc.vector.tensor_tensor(da[:, 0:4 * C], y1[:], mask[:], MULT)
-            if e + 3 < E:
-                load_w2(e + 3)
-                load_saved(a3, a3_sb, "a3", e + 3)
             waiting = (e, da)
         second_product(*waiting)
 

@@ -27,6 +27,7 @@ F32_MAX = 3.4028234663852886e38
 
 PASSES = N // 512
 EARLY = 2
+RELU_BY_SCALAR = 6
 
 
 def tile_moe_bdx_glu_relu_kernel(
@@ -40,7 +41,7 @@ def tile_moe_bdx_glu_relu_kernel(
 
         offs_sb = keep.tile([P, S // 16], U16, name="offs_sb")
         pos_sb = [keep.tile([P, T // 16], U16, name="pos_sb%d" % r) for r in range(4)]
-        dyw = keep.tile([P, (PASSES + 1) * T], I32, name="dyw", align_bytes=64)
+        dyw = ring.tile([P, (PASSES + 1) * T], I32, name="dyw", tag="a3w", align_bytes=64)
         share = ctx.enter_context(tc.tile_pool(name="share", bufs=1))
         late_bytes = 2 * (E - EARLY) * 4 * C * 4
         dys = share.tile([P, 2048], U8, name="dys", align_bytes=64, offset=late_bytes - 64)
@@ -115,25 +116,34 @@ def tile_moe_bdx_glu_relu_kernel(
         w13s = weights[:, 0:w13s_bytes]
         w13w = weights[:, w13s_bytes:w13s_bytes + w13w_bytes]
 
-        def load_pair(e0):
+        def load_a1(e0):
             at = (e0 - EARLY) * 2 * 4 * C
             load_saved(a1, a1_sb, saved[:, at:at + 8 * C], e0, 2)
+
+        def load_a3(e0):
+            at = (e0 - EARLY) * 2 * 4 * C
             load_saved(a3, a3_sb, saved[:, at + 8 * C:at + 16 * C], e0, 2)
+
+        def load_w2_pair(e0):
             at = w13s_bytes + w13w_bytes + (e0 - EARLY) // 2 * pair_w2
             load_w2(weights[:, at:at + pair_w2], e0, 2)
 
+        load_w2_pair(EARLY)
+        load_a1(EARLY)
         for m, scales in enumerate((w1_scales, w3_scales)):
             for q in range(4):
                 nc.sync.dma_start(
                     out=w13s[32 * q:32 * q + 4, m * E * K:(m + 1) * E * K].bitcast(I32).rearrange("f (e k) -> f e k", e=E),
                     in_=scales[:, 0, 4 * q:4 * q + 4, :].rearrange("e f k -> f e k").bitcast(I32))
-        load_pair(EARLY)
         for m, words in enumerate((w1_words, w3_words)):
             nc.sync.dma_start(
                 out=w13w[:, m * E * K * 2:(m + 1) * E * K * 2].bitcast(I32).rearrange("p (e b) -> p e b", e=E),
                 in_=words[:, 0].rearrange("e p b -> p e b").bitcast(I32))
+        load_a3(EARLY)
         for e0 in range(EARLY + 2, E, 2):
-            load_pair(e0)
+            load_w2_pair(e0)
+            load_a1(e0)
+            load_a3(e0)
 
         g_words = []
         for pair in range(E // 2):
@@ -160,19 +170,27 @@ def tile_moe_bdx_glu_relu_kernel(
                             start=(m == 0), stop=(m == 1))
                 nc.scalar.copy(dx[kb][:, e * C:(e + 1) * C], acc[:])
 
+        def weave(dst, rows, first, op0, op1):
+            for h in range(2):
+                nc.gpsimd.tensor_scalar(dst[:, h * 4 * P:(h + 1) * 4 * P].rearrange("p (j r) -> p j r", r=4),
+                                        rows[:, :, h * P:(h + 1) * P].rearrange("p r j -> p j r"),
+                                        first, 0.0, op0, op1)
+
         waiting = None
         for e in range(E):
-            relu = ring.tile([P, 4 * C], F32, name="relu", bufs=4)
-            a3w = ring.tile([P, 4 * C], F32, name="a3w", bufs=4)
-            for h in range(2):
-                nc.gpsimd.tensor_scalar(
-                    relu[:, h * 4 * P:(h + 1) * 4 * P].rearrange("p (j r) -> p j r", r=4),
-                    a1_sb[e][:, :, h * P:(h + 1) * P].rearrange("p r j -> p j r"), F32_MAX, 0.0, MIN, MAX)
-            for h in range(2):
-                nc.gpsimd.tensor_scalar(
-                    a3w[:, h * 4 * P:(h + 1) * 4 * P].rearrange("p (j r) -> p j r", r=4),
-                    a3_sb[e][:, :, h * P:(h + 1) * P].rearrange("p r j -> p j r"), 1.0, 0.0, MULT, ADD)
-            mask = ring.tile([P, 4 * C], BF16, name="mask", bufs=4)
+            relu = ring.tile([P, 4 * C], F32, name="relu", bufs=5)
+            a3w = ring.tile([P, 4 * C], F32, name="a3w", align_bytes=64)
+            if e < RELU_BY_SCALAR:
+                nc.scalar.activation(out=relu[:].rearrange("p (c i r) -> p c r i", i=2, r=4),
+                                     in_=a1_sb[e].rearrange("p r (c i) -> p c r i", i=2), func=ACT.Relu)
+            else:
+                weave(relu, a1_sb[e], F32_MAX, MIN, MAX)
+            if e < EARLY:
+                nc.scalar.copy(a3w[:].rearrange("p (c i r) -> p c r i", i=2, r=4),
+                               a3_sb[e].rearrange("p r (c i) -> p c r i", i=2))
+            else:
+                weave(a3w, a3_sb[e], 1.0, MULT, ADD)
+            mask = ring.tile([P, 4 * C], BF16, name="mask")
             nc.scalar.activation(out=mask[:], in_=relu[:], func=ACT.Sign)
             y1 = ring.tile([P, 4 * C], BF16, name="y1")
             da = ring.tile([P, 2 * 4 * C], BF16, name="da", align_bytes=64)
@@ -188,7 +206,8 @@ def tile_moe_bdx_glu_relu_kernel(
                         rhs_scale=w2s[:, (e * PASSES + s) * H:(e * PASSES + s + 1) * H],
                         start=(s == 0), stop=(s == PASSES - 1))
                 dh_t = ring.tile([P, 4, P], F32, name="dh_t")
-                nc.scalar.activation(out=dh_t[:], in_=sums[:].rearrange("j (p r) -> j r p", r=4),
+                nc.scalar.activation(out=dh_t[:].rearrange("j (u v) p -> j u p v", v=2),
+                                     in_=sums[:].rearrange("j (p u v) -> j u p v", u=2, v=2),
                                      func=ACT.Copy, scale=gate_col[:, b:b + 1])
                 dh = psum.tile([P, 4, P], F32, name="dh", bufs=4)
                 for r in range(4):

@@ -6,6 +6,8 @@ from concourse.masks import make_identity
 K, T, E, C, H, N = 256, 512, 8, 256, 512, 1024
 S = E * C
 P = 128
+R = 4
+PASSES = N // (P * R)
 FLOPS = 2 * S * (N * H + 2 * H * K)
 BYTES = (N * T + N * T // 32 + 2 * H * S * 4 + E * (N * H + 2 * H * K) // 2 + E * (N * H + 2 * H * K) // 32
          + S * 4 + P * (S + 4 * T) // 16 * 2 + K * T * 4)
@@ -25,9 +27,11 @@ MIN = mybir.AluOpType.min
 MAX = mybir.AluOpType.max
 F32_MAX = 3.4028234663852886e38
 
-PASSES = N // 512
 EARLY = 2
-RELU_BY_SCALAR = 6
+RELU_BY_GPSIMD = (EARLY, EARLY + 1)
+MASK_BY_GPSIMD = tuple(range(EARLY)) + tuple(range(EARLY + 1, E - 1, 2))
+SCALE_WINDOW = 2048
+OVERLAP = 64
 
 
 def tile_moe_bdx_glu_relu_kernel(
@@ -41,17 +45,17 @@ def tile_moe_bdx_glu_relu_kernel(
 
         offs_sb = keep.tile([P, S // 16], U16, name="offs_sb")
         pos_sb = [keep.tile([P, T // 16], U16, name="pos_sb%d" % r) for r in range(4)]
-        dyw = ring.tile([P, (PASSES + 1) * T], I32, name="dyw", tag="a3w", align_bytes=64)
+        dyw = keep.tile([P, (PASSES + 1) * T], I32, name="dyw", align_bytes=64)
         share = ctx.enter_context(tc.tile_pool(name="share", bufs=1))
-        late_bytes = 2 * (E - EARLY) * 4 * C * 4
-        dys = share.tile([P, 2048], U8, name="dys", align_bytes=64, offset=late_bytes - 64)
+        late_bytes = (2 * (E - EARLY) + 1) * R * C * 4
+        dys = share.tile([P, SCALE_WINDOW], U8, name="dys", align_bytes=64, offset=late_bytes - OVERLAP)
         gs0 = keep.tile([P, S], U8, name="gs0", align_bytes=64)
         gs1 = keep.tile([P, S], U8, name="gs1", align_bytes=64)
         w2s = keep.tile([P, E * PASSES * H], U8, name="w2s", align_bytes=64)
         gate_rows = keep.tile([P, P], F32, name="gate_rows")
         gate_col = keep.tile([P, S // P], F32, name="gate_col")
         ident = keep.tile([P, P], F32, name="ident")
-        dx = [keep.tile([P, S], F32, name="dx%d" % kb) for kb in range(2)]
+        dx = [keep.tile([P, S], F32, name="dx%d" % kb) for kb in range(K // P)]
 
         nc.gpsimd.memset(dys[:, 0:T].bitcast(I32), 0)
         nc.vector.memset(dys[:, T:].bitcast(I32), 0)
@@ -59,29 +63,30 @@ def tile_moe_bdx_glu_relu_kernel(
         make_identity(nc, ident[:])
 
         w2w, a1_sb, a3_sb = {}, {}, {}
+        w2_bytes = PASSES * H * 2
 
         def load_w2(dst, e0, n):
             nc.sync.dma_start(
                 out=dst.bitcast(I32).rearrange("p (g b) -> p g b", g=n * PASSES),
                 in_=w2_words[e0:e0 + n].rearrange("e s p b -> p (e s) b").bitcast(I32))
             for e in range(n):
-                w2w[e0 + e] = dst[:, e * PASSES * H * 2:(e + 1) * PASSES * H * 2]
+                w2w[e0 + e] = dst[:, e * w2_bytes:(e + 1) * w2_bytes]
 
         def load_saved(src, held, dst, e0, n):
-            rows = dst.rearrange("p (r j) -> p r j", r=4)
-            nc.sync.dma_start(out=rows, in_=src[:, e0 * C:(e0 + n) * C].rearrange("(p r) j -> p r j", r=4))
+            rows = dst.rearrange("p (r j) -> p r j", r=R)
+            nc.sync.dma_start(out=rows, in_=src[:, e0 * C:(e0 + n) * C].rearrange("(p r) j -> p r j", r=R))
             for e in range(n):
                 held[e0 + e] = rows[:, :, e * C:(e + 1) * C]
 
-        early_w2 = [keep.tile([P, PASSES * H * 2], U8, name="early_w2_%d" % e, align_bytes=64) for e in range(EARLY)]
-        early_a1 = [keep.tile([P, 4 * C], F32, name="early_a1_%d" % e) for e in range(EARLY)]
-        early_a3 = [keep.tile([P, 4 * C], F32, name="early_a3_%d" % e) for e in range(EARLY)]
+        early_w2 = [keep.tile([P, w2_bytes], U8, name="early_w2_%d" % e, align_bytes=64) for e in range(EARLY)]
+        early_a1 = [keep.tile([P, R * C], F32, name="early_a1_%d" % e) for e in range(EARLY)]
+        early_a3 = keep.tile([P, R * C], F32, name="early_a3")
 
         nc.sync.dma_start(offs_sb[:], offs)
-        nc.sync.dma_start(out=gate_rows[:], in_=gate[0:8, :].rearrange("h (b p) -> (h b) p", p=P))
+        nc.sync.dma_start(out=gate_rows[:], in_=gate[0:P * P // S, :].rearrange("h (b p) -> (h b) p", p=P))
         load_w2(early_w2[0][:], 0, 1)
         for q in range(4):
-            nc.sync.dma_start(out=dys[32 * q:32 * q + 8, 0:T].bitcast(I32),
+            nc.sync.dma_start(out=dys[32 * q:32 * q + 4 * PASSES, 0:T].bitcast(I32),
                               in_=dy_scales[:, 4 * q:4 * q + 4, :].bitcast(I32))
         nc.sync.dma_start(out=dyw[:, 0:PASSES * T].rearrange("p (o t) -> p o t", o=PASSES),
                           in_=dy_words.rearrange("o p t d -> p o (t d)").bitcast(I32))
@@ -90,60 +95,61 @@ def tile_moe_bdx_glu_relu_kernel(
                 out=w2s[32 * q:32 * q + 4, :].bitcast(I32).rearrange("f (g i) -> f g i", g=E * PASSES),
                 in_=w2_scales[:, :, 4 * q:4 * q + 4, :].rearrange("e s f i -> f (e s) i").bitcast(I32))
         load_saved(a1, a1_sb, early_a1[0][:], 0, 1)
-        load_saved(a3, a3_sb, early_a3[0][:], 0, 1)
+        load_saved(a3, a3_sb, early_a3[:], 0, 1)
         load_w2(early_w2[1][:], 1, 1)
         load_saved(a1, a1_sb, early_a1[1][:], 1, 1)
         for r, pos in enumerate((pos1, pos2, pos3, pos4)):
             nc.sync.dma_start(pos_sb[r][:], pos)
-        load_saved(a3, a3_sb, early_a3[1][:], 1, 1)
 
         gate_ps = psum.tile([P, P], F32, name="gate_ps", tag="acc0")
         nc.tensor.transpose(gate_ps[:], gate_rows[:], ident[:])
         nc.scalar.copy(gate_col[:], gate_ps[:, 0:S // P])
 
         for half in range(2):
-            nc.vector.tensor_copy(gs0[:, half * 1024:(half + 1) * 1024],
-                                  dys[:].indirect(offs_sb[:, half * 64:(half + 1) * 64]))
+            nc.vector.tensor_copy(gs0[:, half * S // 2:(half + 1) * S // 2],
+                                  dys[:].indirect(offs_sb[:, half * S // 32:(half + 1) * S // 32]))
         for q in range(4):
             nc.sync.dma_start(out=gs1[32 * q:32 * q + 4, :].bitcast(I32),
-                                in_=gs0[32 * q + 4:32 * q + 8, :].bitcast(I32))
+                              in_=gs0[32 * q + 4:32 * q + 8, :].bitcast(I32))
         g_scales = (gs0, gs1)
 
         saved = share.tile([P, late_bytes // 4], F32, name="saved", align_bytes=64, offset=0)
-        w13s_bytes, w13w_bytes, pair_w2 = 2 * E * K, 2 * E * K * 2, 2 * PASSES * H * 2
-        weights = share.tile([P, w13s_bytes + w13w_bytes + (E - EARLY) // 2 * pair_w2], U8, name="weights",
-                             align_bytes=64, offset=late_bytes + 2048 - 128)
+        w13s_bytes, w13w_bytes = 2 * E * K, 2 * E * K * 2
+        weights = share.tile([P, w13s_bytes + w13w_bytes + (E - EARLY) * w2_bytes], U8, name="weights",
+                             align_bytes=64, offset=late_bytes + SCALE_WINDOW - 2 * OVERLAP)
         w13s = weights[:, 0:w13s_bytes]
         w13w = weights[:, w13s_bytes:w13s_bytes + w13w_bytes]
 
-        def load_a1(e0):
-            at = (e0 - EARLY) * 2 * 4 * C
-            load_saved(a1, a1_sb, saved[:, at:at + 8 * C], e0, 2)
+        def load_a1_pair(e0):
+            at = (e0 - EARLY) * 2 * R * C
+            load_saved(a1, a1_sb, saved[:, at:at + 2 * R * C], e0, 2)
 
-        def load_a3(e0):
-            at = (e0 - EARLY) * 2 * 4 * C
-            load_saved(a3, a3_sb, saved[:, at + 8 * C:at + 16 * C], e0, 2)
+        def load_a3_pair(e0):
+            at = (e0 - EARLY + 1) * 2 * R * C
+            load_saved(a3, a3_sb, saved[:, at:at + 2 * R * C], e0, 2)
 
         def load_w2_pair(e0):
-            at = w13s_bytes + w13w_bytes + (e0 - EARLY) // 2 * pair_w2
-            load_w2(weights[:, at:at + pair_w2], e0, 2)
+            at = w13s_bytes + w13w_bytes + (e0 - EARLY) * w2_bytes
+            load_w2(weights[:, at:at + 2 * w2_bytes], e0, 2)
 
+        load_saved(a3, a3_sb, saved[:, (E - EARLY) * 2 * R * C:], 1, 1)
         load_w2_pair(EARLY)
-        load_a1(EARLY)
-        for m, scales in enumerate((w1_scales, w3_scales)):
+        load_a1_pair(EARLY)
+        for m, w_scales in enumerate((w1_scales, w3_scales)):
             for q in range(4):
                 nc.sync.dma_start(
-                    out=w13s[32 * q:32 * q + 4, m * E * K:(m + 1) * E * K].bitcast(I32).rearrange("f (e k) -> f e k", e=E),
-                    in_=scales[:, 0, 4 * q:4 * q + 4, :].rearrange("e f k -> f e k").bitcast(I32))
-        for m, words in enumerate((w1_words, w3_words)):
+                    out=w13s[32 * q:32 * q + 4, m * E * K:(m + 1) * E * K].bitcast(I32).rearrange(
+                        "f (e k) -> f e k", e=E),
+                    in_=w_scales[:, 0, 4 * q:4 * q + 4, :].rearrange("e f k -> f e k").bitcast(I32))
+        for m, w_words in enumerate((w1_words, w3_words)):
             nc.sync.dma_start(
                 out=w13w[:, m * E * K * 2:(m + 1) * E * K * 2].bitcast(I32).rearrange("p (e b) -> p e b", e=E),
-                in_=words[:, 0].rearrange("e p b -> p e b").bitcast(I32))
-        load_a3(EARLY)
+                in_=w_words[:, 0].rearrange("e p b -> p e b").bitcast(I32))
+        load_a3_pair(EARLY)
         for e0 in range(EARLY + 2, E, 2):
+            load_a1_pair(e0)
             load_w2_pair(e0)
-            load_a1(e0)
-            load_a3(e0)
+            load_a3_pair(e0)
 
         g_words = []
         for pair in range(E // 2):
@@ -151,94 +157,103 @@ def tile_moe_bdx_glu_relu_kernel(
             for s in range(PASSES):
                 nc.vector.tensor_copy(
                     g_words[pair][:, s * 2 * C:(s + 1) * 2 * C],
-                    dyw[:, s * T:(s + 2) * T].bitcast(U32).indirect(offs_sb[:, 32 * pair:32 * (pair + 1)]))
+                    dyw[:, s * T:(s + 2) * T].bitcast(U32).indirect(
+                        offs_sb[:, pair * 2 * C // 16:(pair + 1) * 2 * C // 16]))
 
         def second_product(e, da):
             codes = ring.tile([P, 2 * C], U32, name="codes", align_bytes=64)
             scales = ring.tile([P, 2 * C], U8, name="scales", align_bytes=64)
             nc.vector.quantize_mx(out=codes[:].bitcast(FP8X4), scales=scales[:], in_=da[:])
-            for kb in range(2):
+            for kb in range(K // P):
                 acc = psum.tile([P, C], F32, name="acc", tag="acc%d" % kb)
-                for h in range(2):
+                for h in range(C // P):
                     for m in range(2):
+                        col = (m * E + e) * K + kb * P
                         nc.tensor.matmul_mx(
                             out=acc[:, h * P:(h + 1) * P],
-                            lhsT=w13w[:, ((m * E + e) * K + kb * P) * 2:((m * E + e) * K + (kb + 1) * P) * 2].bitcast(FP4X4),
-                            lhsT_scale=w13s[:, (m * E + e) * K + kb * P:(m * E + e) * K + (kb + 1) * P],
+                            lhsT=w13w[:, col * 2:(col + P) * 2].bitcast(FP4X4),
+                            lhsT_scale=w13s[:, col:col + P],
                             rhs=codes[:, m * C + h * P:m * C + (h + 1) * P].bitcast(FP8X4),
                             rhs_scale=scales[:, m * C + h * P:m * C + (h + 1) * P],
                             start=(m == 0), stop=(m == 1))
                 nc.scalar.copy(dx[kb][:, e * C:(e + 1) * C], acc[:])
 
-        def weave(dst, rows, first, op0, op1):
-            for h in range(2):
-                nc.gpsimd.tensor_scalar(dst[:, h * 4 * P:(h + 1) * 4 * P].rearrange("p (j r) -> p j r", r=4),
-                                        rows[:, :, h * P:(h + 1) * P].rearrange("p r j -> p j r"),
-                                        first, 0.0, op0, op1)
+        def woven(ap):
+            return ap.rearrange("p (j r) -> p j r", r=R)
+
+        def rows_by_slot(ap):
+            return ap.rearrange("p r j -> p j r")
+
+        def woven_pairs(ap):
+            return ap.rearrange("p (c i r) -> p c r i", i=2, r=R)
+
+        def rows_by_pairs(ap):
+            return ap.rearrange("p r (c i) -> p c r i", i=2)
 
         waiting = None
         for e in range(E):
-            relu = ring.tile([P, 4 * C], F32, name="relu", bufs=5)
-            a3w = ring.tile([P, 4 * C], F32, name="a3w", align_bytes=64)
-            if e < RELU_BY_SCALAR:
-                nc.scalar.activation(out=relu[:].rearrange("p (c i r) -> p c r i", i=2, r=4),
-                                     in_=a1_sb[e].rearrange("p r (c i) -> p c r i", i=2), func=ACT.Relu)
+            halves = [(slice(h * P, (h + 1) * P), slice(h * R * P, (h + 1) * R * P)) for h in range(C // P)]
+            relu = ring.tile([P, R * C], F32, name="relu", bufs=5)
+            if e in RELU_BY_GPSIMD:
+                for slots, cols in halves:
+                    nc.gpsimd.tensor_scalar(woven(relu[:, cols]), rows_by_slot(a1_sb[e][:, :, slots]),
+                                            F32_MAX, 0.0, MIN, MAX)
             else:
-                weave(relu, a1_sb[e], F32_MAX, MIN, MAX)
-            if e < EARLY:
-                nc.scalar.copy(a3w[:].rearrange("p (c i r) -> p c r i", i=2, r=4),
-                               a3_sb[e].rearrange("p r (c i) -> p c r i", i=2))
-            else:
-                weave(a3w, a3_sb[e], 1.0, MULT, ADD)
-            mask = ring.tile([P, 4 * C], BF16, name="mask")
+                nc.scalar.activation(out=woven_pairs(relu[:]), in_=rows_by_pairs(a1_sb[e]), func=ACT.Relu)
+            mask = ring.tile([P, R * C], F32 if e in MASK_BY_GPSIMD else BF16, name="mask")
             nc.scalar.activation(out=mask[:], in_=relu[:], func=ACT.Sign)
-            y1 = ring.tile([P, 4 * C], BF16, name="y1")
-            da = ring.tile([P, 2 * 4 * C], BF16, name="da", align_bytes=64)
-            for h in range(2):
-                b = 2 * e + h
+            if e in MASK_BY_GPSIMD:
+                a3_masked = ring.tile([P, R * C], F32, name="a3_masked")
+                for slots, cols in halves:
+                    nc.gpsimd.tensor_tensor(woven(a3_masked[:, cols]), rows_by_slot(a3_sb[e][:, :, slots]),
+                                            woven(mask[:, cols]), MULT)
+            else:
+                unmasked = ring.tile([P, R * C], BF16, name="unmasked", bufs=2)
+            da = ring.tile([P, 2 * R * C], BF16, name="da", align_bytes=64)
+            for h, (slots, cols) in enumerate(halves):
+                b = e * C // P + h
+                in_pair = (e % 2) * C + h * P
                 sums = psum.tile([P, H], F32, name="sums", bufs=2)
                 for s in range(PASSES):
                     nc.tensor.matmul_mx(
                         out=sums[:],
-                        lhsT=g_words[e // 2][:, s * 2 * C + (b % 4) * P:s * 2 * C + (b % 4 + 1) * P].bitcast(FP8X4),
+                        lhsT=g_words[e // 2][:, s * 2 * C + in_pair:s * 2 * C + in_pair + P].bitcast(FP8X4),
                         lhsT_scale=g_scales[s][:, b * P:(b + 1) * P],
                         rhs=w2w[e][:, s * H * 2:(s + 1) * H * 2].bitcast(FP4X4),
                         rhs_scale=w2s[:, (e * PASSES + s) * H:(e * PASSES + s + 1) * H],
                         start=(s == 0), stop=(s == PASSES - 1))
-                dh_t = ring.tile([P, 4, P], F32, name="dh_t")
+                dh_t = ring.tile([P, R, P], F32, name="dh_t")
                 nc.scalar.activation(out=dh_t[:].rearrange("j (u v) p -> j u p v", v=2),
                                      in_=sums[:].rearrange("j (p u v) -> j u p v", u=2, v=2),
                                      func=ACT.Copy, scale=gate_col[:, b:b + 1])
-                dh = psum.tile([P, 4, P], F32, name="dh", bufs=4)
-                for r in range(4):
+                dh = psum.tile([P, R, P], F32, name="dh", bufs=4)
+                for r in range(R):
                     nc.tensor.transpose(dh[:, r, :], dh_t[:, r, :], ident[:])
-                cols = slice(h * 4 * P, (h + 1) * 4 * P)
-                nc.vector.tensor_tensor(
-                    y1[:, cols].rearrange("p (j r) -> p j r", r=4),
-                    dh[:].rearrange("p r j -> p j r"),
-                    a3w[:, cols].rearrange("p (j r) -> p j r", r=4), MULT)
+                if e in MASK_BY_GPSIMD:
+                    nc.vector.tensor_tensor(woven(da[:, cols]), rows_by_slot(dh[:]), woven(a3_masked[:, cols]), MULT)
+                else:
+                    nc.vector.tensor_tensor(woven_pairs(unmasked[:, cols]), rows_by_pairs(dh[:]),
+                                            rows_by_pairs(a3_sb[e][:, :, slots]), MULT)
                 if h == 0 and waiting is not None:
                     second_product(*waiting)
-                nc.vector.tensor_tensor(
-                    da[:, 4 * C + h * 4 * P:4 * C + (h + 1) * 4 * P].rearrange("p (j r) -> p j r", r=4),
-                    dh[:].rearrange("p r j -> p j r"),
-                    relu[:, cols].rearrange("p (j r) -> p j r", r=4), MULT)
-            nc.vector.tensor_tensor(da[:, 0:4 * C], y1[:], mask[:], MULT)
+                nc.vector.tensor_tensor(woven(da[:, R * C:][:, cols]), rows_by_slot(dh[:]), woven(relu[:, cols]), MULT)
+            if e not in MASK_BY_GPSIMD:
+                nc.vector.tensor_tensor(da[:, 0:R * C], unmasked[:], mask[:], MULT)
             waiting = (e, da)
         second_product(*waiting)
 
-        HALF = T // 2
-        for kb in range(2):
-            part = [[keep.tile([P, HALF], F32, name="part%d_%d_%d" % (kb, h, r)) for r in range(3)] for h in range(2)]
+        half_t = T // 2
+        for kb in range(K // P):
+            part = [[keep.tile([P, half_t], F32, name="part%d_%d_%d" % (kb, h, r)) for r in range(3)] for h in range(2)]
             res = keep.tile([P, T], F32, name="res%d" % kb)
             for r in range(4):
                 for h in range(2):
-                    picked = dx[kb][:].indirect(pos_sb[r][:, h * HALF // 16:(h + 1) * HALF // 16])
+                    picked = dx[kb][:].indirect(pos_sb[r][:, h * half_t // 16:(h + 1) * half_t // 16])
                     if r == 0:
                         nc.vector.tensor_copy(part[h][0][:], picked)
                     else:
-                        dst = part[h][r][:] if r < 3 else res[:, h * HALF:(h + 1) * HALF]
+                        dst = part[h][r][:] if r < 3 else res[:, h * half_t:(h + 1) * half_t]
                         nc.vector.tensor_tensor(dst, picked, part[h][r - 1][:], ADD)
             for h in range(2):
-                nc.sync.dma_start(out=out[kb * P:(kb + 1) * P, h * HALF:(h + 1) * HALF],
-                                  in_=res[:, h * HALF:(h + 1) * HALF])
+                nc.sync.dma_start(out=out[kb * P:(kb + 1) * P, h * half_t:(h + 1) * half_t],
+                                  in_=res[:, h * half_t:(h + 1) * half_t])

@@ -28,8 +28,8 @@ MAX = mybir.AluOpType.max
 F32_MAX = 3.4028234663852886e38
 
 EARLY = 2
-RELU_BY_GPSIMD = (EARLY, EARLY + 1)
-MASK_BY_GPSIMD = tuple(range(EARLY)) + tuple(range(EARLY + 1, E - 1, 2))
+RELU_BY_GPSIMD = ()
+MASK_BY_GPSIMD = ()
 SCALE_WINDOW = 2048
 OVERLAP = 64
 
@@ -47,7 +47,7 @@ def tile_moe_bdx_glu_relu_kernel(
         pos_sb = [keep.tile([P, T // 16], U16, name="pos_sb%d" % r) for r in range(4)]
         dyw = keep.tile([P, (PASSES + 1) * T], I32, name="dyw", align_bytes=64)
         share = ctx.enter_context(tc.tile_pool(name="share", bufs=1))
-        late_bytes = (2 * (E - EARLY) + 1) * R * C * 4
+        late_bytes = 2 * (E - EARLY) * R * C * 4
         dys = share.tile([P, SCALE_WINDOW], U8, name="dys", align_bytes=64, offset=late_bytes - OVERLAP)
         gs0 = keep.tile([P, S], U8, name="gs0", align_bytes=64)
         gs1 = keep.tile([P, S], U8, name="gs1", align_bytes=64)
@@ -78,9 +78,15 @@ def tile_moe_bdx_glu_relu_kernel(
             for e in range(n):
                 held[e0 + e] = rows[:, :, e * C:(e + 1) * C]
 
+        def load_scales(plane, rows, groups):
+            for r in range(4):
+                nc.sync.dma_start(
+                    out=plane[r:P:32, :].bitcast(I32).rearrange("q (g i) -> q g i", g=groups),
+                    in_=rows[r:16:4].bitcast(I32))
+
         early_w2 = [keep.tile([P, w2_bytes], U8, name="early_w2_%d" % e, align_bytes=64) for e in range(EARLY)]
-        early_a1 = [keep.tile([P, R * C], F32, name="early_a1_%d" % e) for e in range(EARLY)]
-        early_a3 = keep.tile([P, R * C], F32, name="early_a3")
+        early_a1 = keep.tile([P, EARLY * R * C], F32, name="early_a1")
+        early_a3 = keep.tile([P, EARLY * R * C], F32, name="early_a3")
 
         nc.sync.dma_start(offs_sb[:], offs)
         nc.sync.dma_start(out=gate_rows[:], in_=gate[0:P * P // S, :].rearrange("h (b p) -> (h b) p", p=P))
@@ -90,27 +96,22 @@ def tile_moe_bdx_glu_relu_kernel(
                               in_=dy_scales[:, 4 * q:4 * q + 4, :].bitcast(I32))
         nc.sync.dma_start(out=dyw[:, 0:PASSES * T].rearrange("p (o t) -> p o t", o=PASSES),
                           in_=dy_words.rearrange("o p t d -> p o (t d)").bitcast(I32))
-        for q in range(4):
-            nc.sync.dma_start(
-                out=w2s[32 * q:32 * q + 4, :].bitcast(I32).rearrange("f (g i) -> f g i", g=E * PASSES),
-                in_=w2_scales[:, :, 4 * q:4 * q + 4, :].rearrange("e s f i -> f (e s) i").bitcast(I32))
-        load_saved(a1, a1_sb, early_a1[0][:], 0, 1)
-        load_saved(a3, a3_sb, early_a3[:], 0, 1)
+        load_saved(a1, a1_sb, early_a1[:], 0, EARLY)
         load_w2(early_w2[1][:], 1, 1)
-        load_saved(a1, a1_sb, early_a1[1][:], 1, 1)
+        load_scales(w2s, w2_scales.rearrange("e s f i -> f (e s) i"), E * PASSES)
         for r, pos in enumerate((pos1, pos2, pos3, pos4)):
             nc.sync.dma_start(pos_sb[r][:], pos)
+        load_saved(a3, a3_sb, early_a3[:], 0, EARLY)
 
-        gate_ps = psum.tile([P, P], F32, name="gate_ps", tag="acc0")
+        gate_ps = psum.tile([P, P], F32, name="gate_ps", tag="acc", bufs=2)
         nc.tensor.transpose(gate_ps[:], gate_rows[:], ident[:])
         nc.scalar.copy(gate_col[:], gate_ps[:, 0:S // P])
 
         for half in range(2):
             nc.vector.tensor_copy(gs0[:, half * S // 2:(half + 1) * S // 2],
                                   dys[:].indirect(offs_sb[:, half * S // 32:(half + 1) * S // 32]))
-        for q in range(4):
-            nc.sync.dma_start(out=gs1[32 * q:32 * q + 4, :].bitcast(I32),
-                              in_=gs0[32 * q + 4:32 * q + 8, :].bitcast(I32))
+        for r in range(4):
+            nc.sync.dma_start(out=gs1[r:P:32, :].bitcast(I32), in_=gs0[4 + r:P:32, :].bitcast(I32))
         g_scales = (gs0, gs1)
 
         saved = share.tile([P, late_bytes // 4], F32, name="saved", align_bytes=64, offset=0)
@@ -120,36 +121,40 @@ def tile_moe_bdx_glu_relu_kernel(
         w13s = weights[:, 0:w13s_bytes]
         w13w = weights[:, w13s_bytes:w13s_bytes + w13w_bytes]
 
-        def load_a1_pair(e0):
-            at = (e0 - EARLY) * 2 * R * C
-            load_saved(a1, a1_sb, saved[:, at:at + 2 * R * C], e0, 2)
+        def load_a1(e0, n):
+            at = (e0 - EARLY) * R * C
+            load_saved(a1, a1_sb, saved[:, at:at + n * R * C], e0, n)
 
-        def load_a3_pair(e0):
-            at = (e0 - EARLY + 1) * 2 * R * C
-            load_saved(a3, a3_sb, saved[:, at:at + 2 * R * C], e0, 2)
+        def load_a3(e0, n):
+            at = (E - EARLY + e0 - EARLY) * R * C
+            load_saved(a3, a3_sb, saved[:, at:at + n * R * C], e0, n)
 
         def load_w2_pair(e0):
             at = w13s_bytes + w13w_bytes + (e0 - EARLY) * w2_bytes
             load_w2(weights[:, at:at + 2 * w2_bytes], e0, 2)
 
-        load_saved(a3, a3_sb, saved[:, (E - EARLY) * 2 * R * C:], 1, 1)
-        load_w2_pair(EARLY)
-        load_a1_pair(EARLY)
-        for m, w_scales in enumerate((w1_scales, w3_scales)):
-            for q in range(4):
-                nc.sync.dma_start(
-                    out=w13s[32 * q:32 * q + 4, m * E * K:(m + 1) * E * K].bitcast(I32).rearrange(
-                        "f (e k) -> f e k", e=E),
-                    in_=w_scales[:, 0, 4 * q:4 * q + 4, :].rearrange("e f k -> f e k").bitcast(I32))
-        for m, w_words in enumerate((w1_words, w3_words)):
+        def load_w13_scales(m, w_scales):
+            load_scales(w13s[:, m * E * K:(m + 1) * E * K], w_scales[:, 0].rearrange("e f k -> f e k"), E)
+
+        def load_w13_words(m, w_words):
             nc.sync.dma_start(
                 out=w13w[:, m * E * K * 2:(m + 1) * E * K * 2].bitcast(I32).rearrange("p (e b) -> p e b", e=E),
                 in_=w_words[:, 0].rearrange("e p b -> p e b").bitcast(I32))
-        load_a3_pair(EARLY)
-        for e0 in range(EARLY + 2, E, 2):
-            load_a1_pair(e0)
-            load_w2_pair(e0)
-            load_a3_pair(e0)
+
+        load_w2_pair(2)
+        load_a1(2, 2)
+        load_w13_scales(0, w1_scales)
+        load_a3(2, 2)
+        load_w2_pair(4)
+        load_a1(4, 2)
+        load_w13_scales(1, w3_scales)
+        load_a3(4, 2)
+        load_w2_pair(6)
+        load_a1(6, 2)
+        load_a3(6, 1)
+        load_w13_words(0, w1_words)
+        load_w13_words(1, w3_words)
+        load_a3(7, 1)
 
         g_words = []
         for pair in range(E // 2):
@@ -161,22 +166,22 @@ def tile_moe_bdx_glu_relu_kernel(
                         offs_sb[:, pair * 2 * C // 16:(pair + 1) * 2 * C // 16]))
 
         def second_product(e, da):
-            codes = ring.tile([P, 2 * C], U32, name="codes", align_bytes=64)
-            scales = ring.tile([P, 2 * C], U8, name="scales", align_bytes=64)
+            codes = ring.tile([P, 2 * C], U32, name="codes", align_bytes=64, bufs=E)
+            scales = ring.tile([P, 2 * C], U8, name="scales", align_bytes=64, bufs=E)
             nc.vector.quantize_mx(out=codes[:].bitcast(FP8X4), scales=scales[:], in_=da[:])
+            acc = psum.tile([P, K // P, C], F32, name="acc", bufs=2)
             for kb in range(K // P):
-                acc = psum.tile([P, C], F32, name="acc", tag="acc%d" % kb)
-                for h in range(C // P):
-                    for m in range(2):
-                        col = (m * E + e) * K + kb * P
-                        nc.tensor.matmul_mx(
-                            out=acc[:, h * P:(h + 1) * P],
-                            lhsT=w13w[:, col * 2:(col + P) * 2].bitcast(FP4X4),
-                            lhsT_scale=w13s[:, col:col + P],
-                            rhs=codes[:, m * C + h * P:m * C + (h + 1) * P].bitcast(FP8X4),
-                            rhs_scale=scales[:, m * C + h * P:m * C + (h + 1) * P],
-                            start=(m == 0), stop=(m == 1))
-                nc.scalar.copy(dx[kb][:, e * C:(e + 1) * C], acc[:])
+                for m in range(2):
+                    col = (m * E + e) * K + kb * P
+                    nc.tensor.matmul_mx(
+                        out=acc[:, kb, :],
+                        lhsT=w13w[:, col * 2:(col + P) * 2].bitcast(FP4X4),
+                        lhsT_scale=w13s[:, col:col + P],
+                        rhs=codes[:, m * C:(m + 1) * C].bitcast(FP8X4),
+                        rhs_scale=scales[:, m * C:(m + 1) * C],
+                        start=(m == 0), stop=(m == 1))
+            for kb in range(K // P):
+                nc.scalar.copy(dx[kb][:, e * C:(e + 1) * C], acc[:, kb, :])
 
         def woven(ap):
             return ap.rearrange("p (j r) -> p j r", r=R)
@@ -244,16 +249,14 @@ def tile_moe_bdx_glu_relu_kernel(
 
         half_t = T // 2
         for kb in range(K // P):
-            part = [[keep.tile([P, half_t], F32, name="part%d_%d_%d" % (kb, h, r)) for r in range(3)] for h in range(2)]
-            res = keep.tile([P, T], F32, name="res%d" % kb)
-            for r in range(4):
-                for h in range(2):
-                    picked = dx[kb][:].indirect(pos_sb[r][:, h * half_t // 16:(h + 1) * half_t // 16])
-                    if r == 0:
-                        nc.vector.tensor_copy(part[h][0][:], picked)
-                    else:
-                        dst = part[h][r][:] if r < 3 else res[:, h * half_t:(h + 1) * half_t]
-                        nc.vector.tensor_tensor(dst, picked, part[h][r - 1][:], ADD)
             for h in range(2):
-                nc.sync.dma_start(out=out[kb * P:(kb + 1) * P, h * half_t:(h + 1) * half_t],
-                                  in_=res[:, h * half_t:(h + 1) * half_t])
+                part = [share.tile([P, half_t], F32, name="part%d_%d_%d" % (kb, h, r),
+                                   offset=((kb * 2 + h) * 4 + r) * half_t * 4) for r in range(4)]
+                res = keep.tile([P, half_t], F32, name="res%d_%d" % (kb, h))
+                picked = [dx[kb][:].indirect(pos_sb[r][:, h * half_t // 16:(h + 1) * half_t // 16]) for r in range(4)]
+                for r in range(2):
+                    nc.scalar.activation(out=part[r][:], in_=picked[r], func=ACT.Copy)
+                for r in range(2):
+                    nc.vector.tensor_tensor(part[2 + r][:], picked[2 + r], part[r][:], ADD)
+                nc.vector.tensor_tensor(res[:], part[2][:], part[3][:], ADD)
+                nc.sync.dma_start(out=out[kb * P:(kb + 1) * P, h * half_t:(h + 1) * half_t], in_=res[:])

@@ -23,13 +23,11 @@ FP4X4 = mybir.dt.float4_e2m1fn_x4
 ACT = mybir.ActivationFunctionType
 MULT = mybir.AluOpType.mult
 ADD = mybir.AluOpType.add
-MIN = mybir.AluOpType.min
-MAX = mybir.AluOpType.max
-F32_MAX = 3.4028234663852886e38
+IS_GT = mybir.AluOpType.is_gt
 
 EARLY = 2
-RELU_BY_GPSIMD = ()
-MASK_BY_GPSIMD = ()
+BY_GPSIMD = (0, 1, 2)
+LAG = 3
 SCALE_WINDOW = 2048
 OVERLAP = 64
 
@@ -52,7 +50,9 @@ def tile_moe_bdx_glu_relu_kernel(
         gs0 = keep.tile([P, S], U8, name="gs0", align_bytes=64)
         gs1 = keep.tile([P, S], U8, name="gs1", align_bytes=64)
         w2s = keep.tile([P, E * PASSES * H], U8, name="w2s", align_bytes=64)
-        gate_rows = keep.tile([P, P], F32, name="gate_rows")
+        share_gate = ctx.enter_context(tc.tile_pool(name="share_gate", bufs=1))
+        w13s_bytes, w13w_bytes = 2 * E * K, 2 * E * K * 2
+        gate_rows = share_gate.tile([P, P], F32, name="gate_rows", align_bytes=64, offset=w13s_bytes - OVERLAP)
         gate_col = keep.tile([P, S // P], F32, name="gate_col")
         ident = keep.tile([P, P], F32, name="ident")
         dx = [keep.tile([P, S], F32, name="dx%d" % kb) for kb in range(K // P)]
@@ -115,11 +115,11 @@ def tile_moe_bdx_glu_relu_kernel(
         g_scales = (gs0, gs1)
 
         saved = share.tile([P, late_bytes // 4], F32, name="saved", align_bytes=64, offset=0)
-        w13s_bytes, w13w_bytes = 2 * E * K, 2 * E * K * 2
-        weights = share.tile([P, w13s_bytes + w13w_bytes + (E - EARLY) * w2_bytes], U8, name="weights",
+        weights = share.tile([P, (E - EARLY) * w2_bytes], U8, name="weights",
                              align_bytes=64, offset=late_bytes + SCALE_WINDOW - 2 * OVERLAP)
-        w13s = weights[:, 0:w13s_bytes]
-        w13w = weights[:, w13s_bytes:w13s_bytes + w13w_bytes]
+        w13s = share_gate.tile([P, w13s_bytes], U8, name="w13s", align_bytes=64, offset=0)
+        w13w = share_gate.tile([P, w13w_bytes], U8, name="w13w", align_bytes=64,
+                               offset=w13s_bytes + P * 4 - 2 * OVERLAP)
 
         def load_a1(e0, n):
             at = (e0 - EARLY) * R * C
@@ -130,7 +130,7 @@ def tile_moe_bdx_glu_relu_kernel(
             load_saved(a3, a3_sb, saved[:, at:at + n * R * C], e0, n)
 
         def load_w2_pair(e0):
-            at = w13s_bytes + w13w_bytes + (e0 - EARLY) * w2_bytes
+            at = (e0 - EARLY) * w2_bytes
             load_w2(weights[:, at:at + 2 * w2_bytes], e0, 2)
 
         def load_w13_scales(m, w_scales):
@@ -156,17 +156,24 @@ def tile_moe_bdx_glu_relu_kernel(
         load_w13_words(1, w3_words)
         load_a3(7, 1)
 
-        g_words = []
-        for pair in range(E // 2):
-            g_words.append(keep.tile([P, PASSES * 2 * C], U32, name="g_words%d" % pair, align_bytes=64))
+        g_words = {}
+
+        def gather_words(pair):
+            g_words[pair] = ring.tile([P, PASSES * 2 * C], U32, name="g_words", align_bytes=64)
             for s in range(PASSES):
                 nc.vector.tensor_copy(
                     g_words[pair][:, s * 2 * C:(s + 1) * 2 * C],
                     dyw[:, s * T:(s + 2) * T].bitcast(U32).indirect(
                         offs_sb[:, pair * 2 * C // 16:(pair + 1) * 2 * C // 16]))
 
+        for pair in range(E // 2 - 1):
+            gather_words(pair)
+
         def second_product(e, da):
-            codes = ring.tile([P, 2 * C], U32, name="codes", align_bytes=64, bufs=E)
+            if e in BY_GPSIMD:
+                codes = ring.tile([P, 2 * C], U32, name="codes", tag="held%d" % e, align_bytes=64, bufs=1)
+            else:
+                codes = ring.tile([P, 2 * C], U32, name="codes", align_bytes=64, bufs=E - len(BY_GPSIMD))
             scales = ring.tile([P, 2 * C], U8, name="scales", align_bytes=64, bufs=E)
             nc.vector.quantize_mx(out=codes[:].bitcast(FP8X4), scales=scales[:], in_=da[:])
             acc = psum.tile([P, K // P, C], F32, name="acc", bufs=2)
@@ -196,25 +203,24 @@ def tile_moe_bdx_glu_relu_kernel(
             return ap.rearrange("p r (c i) -> p c r i", i=2)
 
         waiting = None
+        held = {}
         for e in range(E):
             halves = [(slice(h * P, (h + 1) * P), slice(h * R * P, (h + 1) * R * P)) for h in range(C // P)]
-            relu = ring.tile([P, R * C], F32, name="relu", bufs=5)
-            if e in RELU_BY_GPSIMD:
-                for slots, cols in halves:
-                    nc.gpsimd.tensor_scalar(woven(relu[:, cols]), rows_by_slot(a1_sb[e][:, :, slots]),
-                                            F32_MAX, 0.0, MIN, MAX)
+            if e == 2:
+                gather_words(E // 2 - 1)
+            relu = ring.tile([P, R * C], F32, name="relu", tag="relu_held" if e in BY_GPSIMD else "relu")
+            nc.scalar.activation(out=woven_pairs(relu[:]), in_=rows_by_pairs(a1_sb[e]), func=ACT.Relu)
+            if e in BY_GPSIMD:
+                dh_masked = ring.tile([P, R * C], F32, name="dh_masked")
             else:
-                nc.scalar.activation(out=woven_pairs(relu[:]), in_=rows_by_pairs(a1_sb[e]), func=ACT.Relu)
-            mask = ring.tile([P, R * C], F32 if e in MASK_BY_GPSIMD else BF16, name="mask")
-            nc.scalar.activation(out=mask[:], in_=relu[:], func=ACT.Sign)
-            if e in MASK_BY_GPSIMD:
-                a3_masked = ring.tile([P, R * C], F32, name="a3_masked")
-                for slots, cols in halves:
-                    nc.gpsimd.tensor_tensor(woven(a3_masked[:, cols]), rows_by_slot(a3_sb[e][:, :, slots]),
-                                            woven(mask[:, cols]), MULT)
-            else:
-                unmasked = ring.tile([P, R * C], BF16, name="unmasked", bufs=2)
-            da = ring.tile([P, 2 * R * C], BF16, name="da", align_bytes=64)
+                mask = ring.tile([P, R * C], BF16, name="mask")
+                nc.scalar.activation(out=mask[:], in_=relu[:], func=ACT.Sign)
+                if e - LAG in BY_GPSIMD:
+                    unmasked = ring.tile([P, R * C], BF16, name="unmasked", tag="held%d" % (e - LAG),
+                                         align_bytes=64, bufs=1)
+                else:
+                    unmasked = ring.tile([P, R * C], BF16, name="unmasked", bufs=2)
+            da = ring.tile([P, 2 * R * C], BF16, name="da", align_bytes=64, bufs=5)
             for h, (slots, cols) in enumerate(halves):
                 b = e * C // P + h
                 in_pair = (e % 2) * C + h * P
@@ -234,17 +240,29 @@ def tile_moe_bdx_glu_relu_kernel(
                 dh = psum.tile([P, R, P], F32, name="dh", bufs=4)
                 for r in range(R):
                     nc.tensor.transpose(dh[:, r, :], dh_t[:, r, :], ident[:])
-                if e in MASK_BY_GPSIMD:
-                    nc.vector.tensor_tensor(woven(da[:, cols]), rows_by_slot(dh[:]), woven(a3_masked[:, cols]), MULT)
+                if e in BY_GPSIMD:
+                    nc.vector.scalar_tensor_tensor(woven(dh_masked[:, cols]), woven(relu[:, cols]), 0.0,
+                                                   rows_by_slot(dh[:]), IS_GT, MULT)
+                    nc.gpsimd.tensor_tensor(da[:, R * C:][:, cols], dh_masked[:, cols], relu[:, cols], MULT)
+                    nc.gpsimd.tensor_tensor(woven(da[:, cols]), woven(dh_masked[:, cols]),
+                                            rows_by_slot(a3_sb[e][:, :, slots]), MULT)
                 else:
                     nc.vector.tensor_tensor(woven_pairs(unmasked[:, cols]), rows_by_pairs(dh[:]),
                                             rows_by_pairs(a3_sb[e][:, :, slots]), MULT)
                 if h == 0 and waiting is not None:
                     second_product(*waiting)
-                nc.vector.tensor_tensor(woven(da[:, R * C:][:, cols]), rows_by_slot(dh[:]), woven(relu[:, cols]), MULT)
-            if e not in MASK_BY_GPSIMD:
+                    waiting = None
+                if e not in BY_GPSIMD:
+                    nc.vector.tensor_tensor(woven(da[:, R * C:][:, cols]), rows_by_slot(dh[:]),
+                                            woven(relu[:, cols]), MULT)
+            if e not in BY_GPSIMD:
                 nc.vector.tensor_tensor(da[:, 0:R * C], unmasked[:], mask[:], MULT)
-            waiting = (e, da)
+            if e - LAG in BY_GPSIMD:
+                second_product(e - LAG, held[e - LAG])
+            if e in BY_GPSIMD:
+                held[e] = da
+            else:
+                waiting = (e, da)
         second_product(*waiting)
 
         half_t = T // 2

@@ -26,7 +26,7 @@ ADD = mybir.AluOpType.add
 IS_GT = mybir.AluOpType.is_gt
 
 EARLY = 2
-BY_GPSIMD = (0, 1, 2)
+BY_GPSIMD = ()
 LAG = 3
 SCALE_WINDOW = 2048
 OVERLAP = 64

@@ -26,8 +26,7 @@ ADD = mybir.AluOpType.add
 IS_GT = mybir.AluOpType.is_gt
 
 EARLY = 2
-BY_GPSIMD = ()
-LAG = 3
+BY_GPSIMD = (0, 3)
 SCALE_WINDOW = 2048
 OVERLAP = 64
 
@@ -43,16 +42,19 @@ def tile_moe_bdx_glu_relu_kernel(
 
         offs_sb = keep.tile([P, S // 16], U16, name="offs_sb")
         pos_sb = [keep.tile([P, T // 16], U16, name="pos_sb%d" % r) for r in range(4)]
-        dyw = keep.tile([P, (PASSES + 1) * T], I32, name="dyw", align_bytes=64)
+        share_words = ctx.enter_context(tc.tile_pool(name="share_words", bufs=1))
+        dyw = share_words.tile([P, (PASSES + 1) * T], I32, name="dyw", align_bytes=64, offset=0)
         share = ctx.enter_context(tc.tile_pool(name="share", bufs=1))
         late_bytes = 2 * (E - EARLY) * R * C * 4
-        dys = share.tile([P, SCALE_WINDOW], U8, name="dys", align_bytes=64, offset=late_bytes - OVERLAP)
+        w13s_bytes = 2 * E * K
+        dys_tile = share.tile([P, w13s_bytes + 2 * OVERLAP], U8, name="dys", align_bytes=64,
+                              offset=late_bytes - OVERLAP)
+        dys = dys_tile[:, 0:SCALE_WINDOW]
         gs0 = keep.tile([P, S], U8, name="gs0", align_bytes=64)
         gs1 = keep.tile([P, S], U8, name="gs1", align_bytes=64)
         w2s = keep.tile([P, E * PASSES * H], U8, name="w2s", align_bytes=64)
-        share_gate = ctx.enter_context(tc.tile_pool(name="share_gate", bufs=1))
-        w13s_bytes, w13w_bytes = 2 * E * K, 2 * E * K * 2
-        gate_rows = share_gate.tile([P, P], F32, name="gate_rows", align_bytes=64, offset=w13s_bytes - OVERLAP)
+        w13w_bytes = 2 * E * K * 2
+        gate_rows = keep.tile([P, P], F32, name="gate_rows")
         gate_col = keep.tile([P, S // P], F32, name="gate_col")
         ident = keep.tile([P, P], F32, name="ident")
         dx = [keep.tile([P, S], F32, name="dx%d" % kb) for kb in range(K // P)]
@@ -84,7 +86,8 @@ def tile_moe_bdx_glu_relu_kernel(
                     out=plane[r:P:32, :].bitcast(I32).rearrange("q (g i) -> q g i", g=groups),
                     in_=rows[r:16:4].bitcast(I32))
 
-        early_w2 = [keep.tile([P, w2_bytes], U8, name="early_w2_%d" % e, align_bytes=64) for e in range(EARLY)]
+        early_w2 = [keep.tile([P, w2_bytes], U8, name="early_w2", tag="early%d" % e, align_bytes=64)
+                    for e in range(EARLY)]
         early_a1 = keep.tile([P, EARLY * R * C], F32, name="early_a1")
         early_a3 = keep.tile([P, EARLY * R * C], F32, name="early_a3")
 
@@ -103,23 +106,22 @@ def tile_moe_bdx_glu_relu_kernel(
             nc.sync.dma_start(pos_sb[r][:], pos)
         load_saved(a3, a3_sb, early_a3[:], 0, EARLY)
 
-        gate_ps = psum.tile([P, P], F32, name="gate_ps", tag="acc", bufs=2)
+        gate_ps = psum.tile([P, P], F32, name="gate_ps", tag="bank5")
         nc.tensor.transpose(gate_ps[:], gate_rows[:], ident[:])
         nc.scalar.copy(gate_col[:], gate_ps[:, 0:S // P])
 
         for half in range(2):
             nc.vector.tensor_copy(gs0[:, half * S // 2:(half + 1) * S // 2],
-                                  dys[:].indirect(offs_sb[:, half * S // 32:(half + 1) * S // 32]))
+                                  dys.indirect(offs_sb[:, half * S // 32:(half + 1) * S // 32]))
         for r in range(4):
             nc.sync.dma_start(out=gs1[r:P:32, :].bitcast(I32), in_=gs0[4 + r:P:32, :].bitcast(I32))
         g_scales = (gs0, gs1)
 
         saved = share.tile([P, late_bytes // 4], F32, name="saved", align_bytes=64, offset=0)
-        weights = share.tile([P, (E - EARLY) * w2_bytes], U8, name="weights",
-                             align_bytes=64, offset=late_bytes + SCALE_WINDOW - 2 * OVERLAP)
-        w13s = share_gate.tile([P, w13s_bytes], U8, name="w13s", align_bytes=64, offset=0)
-        w13w = share_gate.tile([P, w13w_bytes], U8, name="w13w", align_bytes=64,
-                               offset=w13s_bytes + P * 4 - 2 * OVERLAP)
+        weights = share.tile([P, w13w_bytes + (E - EARLY) * w2_bytes], U8, name="weights",
+                             align_bytes=64, offset=late_bytes + w13s_bytes)
+        w13w = weights[:, 0:w13w_bytes]
+        w13s = share.tile([P, w13s_bytes], U8, name="w13s", align_bytes=64, offset=late_bytes)
 
         def load_a1(e0, n):
             at = (e0 - EARLY) * R * C
@@ -130,7 +132,7 @@ def tile_moe_bdx_glu_relu_kernel(
             load_saved(a3, a3_sb, saved[:, at:at + n * R * C], e0, n)
 
         def load_w2_pair(e0):
-            at = (e0 - EARLY) * w2_bytes
+            at = w13w_bytes + (e0 - EARLY) * w2_bytes
             load_w2(weights[:, at:at + 2 * w2_bytes], e0, 2)
 
         def load_w13_scales(m, w_scales):
@@ -141,52 +143,53 @@ def tile_moe_bdx_glu_relu_kernel(
                 out=w13w[:, m * E * K * 2:(m + 1) * E * K * 2].bitcast(I32).rearrange("p (e b) -> p e b", e=E),
                 in_=w_words[:, 0].rearrange("e p b -> p e b").bitcast(I32))
 
-        load_w2_pair(2)
-        load_a1(2, 2)
+        for e0 in range(EARLY, E, 2):
+            load_w2_pair(e0)
+            load_a1(e0, 2)
+            if e0 < E - 2:
+                load_a3(e0, 2)
         load_w13_scales(0, w1_scales)
-        load_a3(2, 2)
-        load_w2_pair(4)
-        load_a1(4, 2)
-        load_w13_scales(1, w3_scales)
-        load_a3(4, 2)
-        load_w2_pair(6)
-        load_a1(6, 2)
-        load_a3(6, 1)
         load_w13_words(0, w1_words)
+        load_w13_scales(1, w3_scales)
         load_w13_words(1, w3_words)
+        load_a3(6, 1)
         load_a3(7, 1)
 
         g_words = {}
 
         def gather_words(pair):
-            g_words[pair] = ring.tile([P, PASSES * 2 * C], U32, name="g_words", align_bytes=64)
+            g_words[pair] = ring.tile([P, PASSES * 2 * C], U32, name="g_words", align_bytes=64, bufs=4)
             for s in range(PASSES):
                 nc.vector.tensor_copy(
                     g_words[pair][:, s * 2 * C:(s + 1) * 2 * C],
                     dyw[:, s * T:(s + 2) * T].bitcast(U32).indirect(
                         offs_sb[:, pair * 2 * C // 16:(pair + 1) * 2 * C // 16]))
 
-        for pair in range(E // 2 - 1):
+        for pair in range(4):
             gather_words(pair)
 
-        def second_product(e, da):
-            if e in BY_GPSIMD:
-                codes = ring.tile([P, 2 * C], U32, name="codes", tag="held%d" % e, align_bytes=64, bufs=1)
-            else:
-                codes = ring.tile([P, 2 * C], U32, name="codes", align_bytes=64, bufs=E - len(BY_GPSIMD))
+        done = []
+
+        def quantise(codes, da):
             scales = ring.tile([P, 2 * C], U8, name="scales", align_bytes=64, bufs=E)
             nc.vector.quantize_mx(out=codes[:].bitcast(FP8X4), scales=scales[:], in_=da[:])
-            acc = psum.tile([P, K // P, C], F32, name="acc", bufs=2)
+            return [(codes[:, part * C:(part + 1) * C], scales[:, part * C:(part + 1) * C]) for part in range(2)]
+
+        def multiply(acc, e, kb, m, operand, start):
+            col = (m * E + e) * K + kb * P
+            nc.tensor.matmul_mx(
+                out=acc,
+                lhsT=w13w[:, col * 2:(col + P) * 2].bitcast(FP4X4),
+                lhsT_scale=w13s[:, col:col + P],
+                rhs=operand[0].bitcast(FP8X4), rhs_scale=operand[1],
+                start=start, stop=not start)
+
+        def second_product(e, operands):
+            acc = psum.tile([P, K // P, C], F32, name="acc", tag="bank%d" % (4 + len(done) % 2))
+            done.append(e)
             for kb in range(K // P):
                 for m in range(2):
-                    col = (m * E + e) * K + kb * P
-                    nc.tensor.matmul_mx(
-                        out=acc[:, kb, :],
-                        lhsT=w13w[:, col * 2:(col + P) * 2].bitcast(FP4X4),
-                        lhsT_scale=w13s[:, col:col + P],
-                        rhs=codes[:, m * C:(m + 1) * C].bitcast(FP8X4),
-                        rhs_scale=scales[:, m * C:(m + 1) * C],
-                        start=(m == 0), stop=(m == 1))
+                    multiply(acc[:, kb, :], e, kb, m, operands[m], m == 0)
             for kb in range(K // P):
                 nc.scalar.copy(dx[kb][:, e * C:(e + 1) * C], acc[:, kb, :])
 
@@ -202,79 +205,140 @@ def tile_moe_bdx_glu_relu_kernel(
         def rows_by_pairs(ap):
             return ap.rearrange("p r (c i) -> p c r i", i=2)
 
-        waiting = None
-        held = {}
-        for e in range(E):
-            halves = [(slice(h * P, (h + 1) * P), slice(h * R * P, (h + 1) * R * P)) for h in range(C // P)]
-            if e == 2:
-                gather_words(E // 2 - 1)
-            relu = ring.tile([P, R * C], F32, name="relu", tag="relu_held" if e in BY_GPSIMD else "relu")
-            nc.scalar.activation(out=woven_pairs(relu[:]), in_=rows_by_pairs(a1_sb[e]), func=ACT.Relu)
-            if e in BY_GPSIMD:
-                dh_masked = ring.tile([P, R * C], F32, name="dh_masked")
-            else:
-                mask = ring.tile([P, R * C], BF16, name="mask")
-                nc.scalar.activation(out=mask[:], in_=relu[:], func=ACT.Sign)
-                if e - LAG in BY_GPSIMD:
-                    unmasked = ring.tile([P, R * C], BF16, name="unmasked", tag="held%d" % (e - LAG),
-                                         align_bytes=64, bufs=1)
-                else:
-                    unmasked = ring.tile([P, R * C], BF16, name="unmasked", bufs=2)
-            da = ring.tile([P, 2 * R * C], BF16, name="da", align_bytes=64, bufs=5)
+        def first_product(e, h):
+            b = e * C // P + h
+            in_pair = (e % 2) * C + h * P
+            sums = psum.tile([P, H], F32, name="sums", bufs=2)
+            for s in range(PASSES):
+                nc.tensor.matmul_mx(
+                    out=sums[:],
+                    lhsT=g_words[e // 2][:, s * 2 * C + in_pair:s * 2 * C + in_pair + P].bitcast(FP8X4),
+                    lhsT_scale=g_scales[s][:, b * P:(b + 1) * P],
+                    rhs=w2w[e][:, s * H * 2:(s + 1) * H * 2].bitcast(FP4X4),
+                    rhs_scale=w2s[:, (e * PASSES + s) * H:(e * PASSES + s + 1) * H],
+                    start=(s == 0), stop=(s == PASSES - 1))
+            dh_t = ring.tile([P, R, P], F32, name="dh_t")
+            nc.scalar.activation(out=dh_t[:].rearrange("j (u v) p -> j u p v", v=2),
+                                 in_=sums[:].rearrange("j (p u v) -> j u p v", u=2, v=2),
+                                 func=ACT.Copy, scale=gate_col[:, b:b + 1])
+            dh = psum.tile([P, R, P], F32, name="dh", tag="bank%d" % (b % 4))
+            for r in range(R):
+                nc.tensor.transpose(dh[:, r, :], dh_t[:, r, :], ident[:])
+            return dh
+
+        halves = [(slice(h * P, (h + 1) * P), slice(h * R * P, (h + 1) * R * P)) for h in range(C // P)]
+        dh = {}
+        last = E - 1
+        wide = R * C
+
+        def single(shape, dtype, tag):
+            return ring.tile(shape, dtype, name=tag, tag=tag, align_bytes=64, bufs=1)
+
+        turns = ctx.enter_context(tc.tile_pool(name="turns", bufs=1))
+
+        def in_turn(shape, dtype, name, at):
+            return turns.tile(shape, dtype, name=name, align_bytes=64, offset=at * wide * 2)
+
+        def make_relu(e, relu):
+            nc.scalar.activation(out=woven_pairs(relu), in_=rows_by_pairs(a1_sb[e]), func=ACT.Relu)
+
+        def make_mask(e, mask):
+            relu = ring.tile([P, wide], F32, name="relu", bufs=4)
+            make_relu(e, relu[:])
+            nc.scalar.activation(out=mask, in_=relu[:], func=ACT.Sign)
+            return relu
+
+        def ahead(b):
+            if b + 4 < S // P:
+                dh[b + 4] = first_product((b + 4) // 2, b % 2)
+
+        def times_relu(e, h, da3, relu):
+            cols = halves[h][1]
+            nc.vector.tensor_tensor(woven(da3[:, cols]), rows_by_slot(dh[2 * e + h][:]), woven(relu[:, cols]), MULT)
+
+        def times_a3(e, h, unmasked):
+            slots, cols = halves[h]
+            nc.vector.tensor_tensor(woven_pairs(unmasked[:, cols]), rows_by_pairs(dh[2 * e + h][:]),
+                                    rows_by_pairs(a3_sb[e][:, :, slots]), MULT)
+            ahead(2 * e + h)
+
+        for b in range(4):
+            dh[b] = first_product(b // 2, b % 2)
+        for period, g in enumerate(BY_GPSIMD):
+            at = 4 * period
+            relu = in_turn([P, wide], F32, "relu%d" % g, at)
+            make_relu(g, relu[:])
+            dh_masked = in_turn([P, wide], F32, "dh_masked%d" % g, at + 2)
+            da = single([P, 2 * wide], BF16, "da%d" % g)
             for h, (slots, cols) in enumerate(halves):
-                b = e * C // P + h
-                in_pair = (e % 2) * C + h * P
-                sums = psum.tile([P, H], F32, name="sums", bufs=2)
-                for s in range(PASSES):
-                    nc.tensor.matmul_mx(
-                        out=sums[:],
-                        lhsT=g_words[e // 2][:, s * 2 * C + in_pair:s * 2 * C + in_pair + P].bitcast(FP8X4),
-                        lhsT_scale=g_scales[s][:, b * P:(b + 1) * P],
-                        rhs=w2w[e][:, s * H * 2:(s + 1) * H * 2].bitcast(FP4X4),
-                        rhs_scale=w2s[:, (e * PASSES + s) * H:(e * PASSES + s + 1) * H],
-                        start=(s == 0), stop=(s == PASSES - 1))
-                dh_t = ring.tile([P, R, P], F32, name="dh_t")
-                nc.scalar.activation(out=dh_t[:].rearrange("j (u v) p -> j u p v", v=2),
-                                     in_=sums[:].rearrange("j (p u v) -> j u p v", u=2, v=2),
-                                     func=ACT.Copy, scale=gate_col[:, b:b + 1])
-                dh = psum.tile([P, R, P], F32, name="dh", bufs=4)
-                for r in range(R):
-                    nc.tensor.transpose(dh[:, r, :], dh_t[:, r, :], ident[:])
-                if e in BY_GPSIMD:
-                    nc.vector.scalar_tensor_tensor(woven(dh_masked[:, cols]), woven(relu[:, cols]), 0.0,
-                                                   rows_by_slot(dh[:]), IS_GT, MULT)
-                    nc.gpsimd.tensor_tensor(da[:, R * C:][:, cols], dh_masked[:, cols], relu[:, cols], MULT)
-                    nc.gpsimd.tensor_tensor(woven(da[:, cols]), woven(dh_masked[:, cols]),
-                                            rows_by_slot(a3_sb[e][:, :, slots]), MULT)
-                else:
-                    nc.vector.tensor_tensor(woven_pairs(unmasked[:, cols]), rows_by_pairs(dh[:]),
-                                            rows_by_pairs(a3_sb[e][:, :, slots]), MULT)
-                if h == 0 and waiting is not None:
-                    second_product(*waiting)
-                    waiting = None
-                if e not in BY_GPSIMD:
-                    nc.vector.tensor_tensor(woven(da[:, R * C:][:, cols]), rows_by_slot(dh[:]),
-                                            woven(relu[:, cols]), MULT)
-            if e not in BY_GPSIMD:
-                nc.vector.tensor_tensor(da[:, 0:R * C], unmasked[:], mask[:], MULT)
-            if e - LAG in BY_GPSIMD:
-                second_product(e - LAG, held[e - LAG])
-            if e in BY_GPSIMD:
-                held[e] = da
-            else:
-                waiting = (e, da)
-        second_product(*waiting)
+                nc.vector.scalar_tensor_tensor(woven(dh_masked[:, cols]), woven(relu[:, cols]), 0.0,
+                                               rows_by_slot(dh[2 * g + h][:]), IS_GT, MULT)
+                nc.gpsimd.tensor_tensor(da[:, wide:][:, cols], dh_masked[:, cols], relu[:, cols], MULT)
+                nc.gpsimd.tensor_tensor(woven(da[:, cols]), woven(dh_masked[:, cols]),
+                                        rows_by_slot(a3_sb[g][:, :, slots]), MULT)
+                ahead(2 * g + h)
+            mask = single([P, 2 * wide], BF16, "mask%d" % g)
+            da3 = single([P, 2 * wide], BF16, "da3_%d" % g)
+            unmasked = in_turn([P, 2 * wide], BF16, "unmasked%d" % g, at + 6)
+            for i in range(2):
+                relu = make_mask(g + 1 + i, mask[:, i * wide:(i + 1) * wide])
+                for h in range(2):
+                    times_relu(g + 1 + i, h, da3[:, i * wide:(i + 1) * wide], relu)
+                    times_a3(g + 1 + i, h, unmasked[:, i * wide:(i + 1) * wide])
+            by_w3 = quantise(in_turn([P, 2 * C], U32, "codes3_%d" % g, at), da3)
+            da1 = in_turn([P, 2 * wide], BF16, "da1_%d" % g, at + 2)
+            nc.vector.tensor_tensor(da1[:], unmasked[:], mask[:], MULT)
+            second_product(g, quantise(single([P, 2 * C], U32, "mask%d" % g), da))
+            by_w1 = quantise(in_turn([P, 2 * C], U32, "codes1_%d" % g, at + 1), da1)
+            for i in range(2):
+                second_product(g + 1 + i, (by_w1[i], by_w3[i]))
+
+        mask = single([P, 2 * wide], BF16, "mask6")
+        unmasked = single([P, 2 * wide], BF16, "unmasked6")
+        relu = [make_mask(6 + i, mask[:, i * wide:(i + 1) * wide]) for i in range(2)]
+        da = [single([P, 2 * wide], BF16, "da%d" % g) for g in BY_GPSIMD]
+        for h in range(2):
+            times_relu(6, h, da[0][:, wide:], relu[0])
+            times_a3(6, h, unmasked[:, 0:wide])
+        nc.vector.tensor_tensor(da[0][:, 0:wide], unmasked[:, 0:wide], mask[:, 0:wide], MULT)
+        times_relu(last, 0, da[1][:, wide:], relu[1])
+        second_product(6, quantise(single([P, 2 * C], U32, "codes6"), da[0]))
+        times_relu(last, 1, da[1][:, wide:], relu[1])
+        for h in range(2):
+            times_a3(last, h, unmasked[:, wide:])
+        codes = single([P, 2 * C], U32, "codes7")
+        scales = ring.tile([P, 2 * C], U8, name="scales", align_bytes=64, bufs=E)
+        acc = [psum.tile([P, C], F32, name="acc", tag="bank%d" % kb) for kb in range(K // P)]
+        for m in (1, 0):
+            cols = halves[1 - m][1]
+            nc.vector.tensor_tensor(da[1][:, cols], unmasked[:, wide:][:, cols], mask[:, wide:][:, cols], MULT)
+            operand = (codes[:, m * C:(m + 1) * C], scales[:, m * C:(m + 1) * C])
+            nc.vector.quantize_mx(out=operand[0].bitcast(FP8X4), scales=operand[1],
+                                  in_=da[1][:, m * wide:(m + 1) * wide])
+            for kb in range(K // P):
+                multiply(acc[kb][:], last, kb, m, operand, m == 1)
+        nc.vector.tensor_copy(dx[0][:, last * C:], acc[0][:])
+        nc.scalar.copy(dx[1][:, last * C:], acc[1][:])
 
         half_t = T // 2
-        for kb in range(K // P):
-            for h in range(2):
-                part = [share.tile([P, half_t], F32, name="part%d_%d_%d" % (kb, h, r),
-                                   offset=((kb * 2 + h) * 4 + r) * half_t * 4) for r in range(4)]
-                res = keep.tile([P, half_t], F32, name="res%d_%d" % (kb, h))
-                picked = [dx[kb][:].indirect(pos_sb[r][:, h * half_t // 16:(h + 1) * half_t // 16]) for r in range(4)]
+        pieces = [(kb, h) for kb in range(K // P) for h in range(2)]
+        for g, (kb, h) in enumerate(pieces):
+            part = [share.tile([P, half_t], F32, name="part%d_%d" % (g, r), offset=(g * 6 + r) * half_t * 4)
+                    for r in range(6)]
+            picked = [dx[kb][:].indirect(pos_sb[r][:, h * half_t // 16:(h + 1) * half_t // 16]) for r in range(4)]
+            if g == 0:
+                nc.vector.tensor_copy(part[1][:], picked[1])
+                nc.scalar.activation(out=part[0][:], in_=picked[0], func=ACT.Copy)
+            else:
                 for r in range(2):
                     nc.scalar.activation(out=part[r][:], in_=picked[r], func=ACT.Copy)
+            if g == len(pieces) - 1:
+                nc.scalar.activation(out=part[4][:], in_=picked[2], func=ACT.Copy)
+                nc.vector.tensor_tensor(part[3][:], picked[3], part[0][:], ADD)
+                nc.vector.tensor_tensor(part[2][:], part[1][:], part[3][:], ADD)
+                nc.vector.tensor_tensor(part[5][:], part[2][:], part[4][:], ADD)
+            else:
                 for r in range(2):
                     nc.vector.tensor_tensor(part[2 + r][:], picked[2 + r], part[r][:], ADD)
-                nc.vector.tensor_tensor(res[:], part[2][:], part[3][:], ADD)
-                nc.sync.dma_start(out=out[kb * P:(kb + 1) * P, h * half_t:(h + 1) * half_t], in_=res[:])
+                nc.vector.tensor_tensor(part[5][:], part[2][:], part[3][:], ADD)
+            nc.sync.dma_start(out=out[kb * P:(kb + 1) * P, h * half_t:(h + 1) * half_t], in_=part[5][:])

@@ -27,6 +27,7 @@ IS_GT = mybir.AluOpType.is_gt
 
 EARLY = 2
 BY_GPSIMD = (0, 3)
+WORD_WINDOW = 2048
 SCALE_WINDOW = 2048
 OVERLAP = 64
 
@@ -42,8 +43,7 @@ def tile_moe_bdx_glu_relu_kernel(
 
         offs_sb = keep.tile([P, S // 16], U16, name="offs_sb")
         pos_sb = [keep.tile([P, T // 16], U16, name="pos_sb%d" % r) for r in range(4)]
-        share_words = ctx.enter_context(tc.tile_pool(name="share_words", bufs=1))
-        dyw = share_words.tile([P, (PASSES + 1) * T], I32, name="dyw", align_bytes=64, offset=0)
+        dyw = keep.tile([P, T + WORD_WINDOW], I32, name="dyw", align_bytes=64)
         share = ctx.enter_context(tc.tile_pool(name="share", bufs=1))
         late_bytes = 2 * (E - EARLY) * R * C * 4
         w13s_bytes = 2 * E * K
@@ -65,6 +65,12 @@ def tile_moe_bdx_glu_relu_kernel(
         make_identity(nc, ident[:])
 
         w2w, a1_sb, a3_sb = {}, {}, {}
+        wide = R * C
+        turns = ctx.enter_context(tc.tile_pool(name="turns", bufs=1))
+
+        def in_turn(shape, dtype, name, at):
+            return turns.tile(shape, dtype, name=name, align_bytes=64, offset=at * wide * 2)
+
         w2_bytes = PASSES * H * 2
 
         def load_w2(dst, e0, n):
@@ -86,21 +92,19 @@ def tile_moe_bdx_glu_relu_kernel(
                     out=plane[r:P:32, :].bitcast(I32).rearrange("q (g i) -> q g i", g=groups),
                     in_=rows[r:16:4].bitcast(I32))
 
-        early_w2 = [keep.tile([P, w2_bytes], U8, name="early_w2", tag="early%d" % e, align_bytes=64)
-                    for e in range(EARLY)]
-        early_a1 = keep.tile([P, EARLY * R * C], F32, name="early_a1")
+        early_w2 = keep.tile([P, EARLY * w2_bytes], U8, name="early_w2", align_bytes=64)
+        early_a1 = in_turn([P, EARLY * wide], F32, "early_a1", 12)
         early_a3 = keep.tile([P, EARLY * R * C], F32, name="early_a3")
 
         nc.sync.dma_start(offs_sb[:], offs)
         nc.sync.dma_start(out=gate_rows[:], in_=gate[0:P * P // S, :].rearrange("h (b p) -> (h b) p", p=P))
-        load_w2(early_w2[0][:], 0, 1)
         for q in range(4):
             nc.sync.dma_start(out=dys[32 * q:32 * q + 4 * PASSES, 0:T].bitcast(I32),
                               in_=dy_scales[:, 4 * q:4 * q + 4, :].bitcast(I32))
         nc.sync.dma_start(out=dyw[:, 0:PASSES * T].rearrange("p (o t) -> p o t", o=PASSES),
                           in_=dy_words.rearrange("o p t d -> p o (t d)").bitcast(I32))
         load_saved(a1, a1_sb, early_a1[:], 0, EARLY)
-        load_w2(early_w2[1][:], 1, 1)
+        load_w2(early_w2[:], 0, EARLY)
         load_scales(w2s, w2_scales.rearrange("e s f i -> f (e s) i"), E * PASSES)
         for r, pos in enumerate((pos1, pos2, pos3, pos4)):
             nc.sync.dma_start(pos_sb[r][:], pos)
@@ -155,18 +159,14 @@ def tile_moe_bdx_glu_relu_kernel(
         load_a3(6, 1)
         load_a3(7, 1)
 
-        g_words = {}
-
-        def gather_words(pair):
-            g_words[pair] = ring.tile([P, PASSES * 2 * C], U32, name="g_words", align_bytes=64, bufs=4)
+        g_words = []
+        for half in range(2):
+            g_words.append(keep.tile([P, PASSES * S // 2], U32, name="g_words%d" % half, align_bytes=64))
             for s in range(PASSES):
                 nc.vector.tensor_copy(
-                    g_words[pair][:, s * 2 * C:(s + 1) * 2 * C],
-                    dyw[:, s * T:(s + 2) * T].bitcast(U32).indirect(
-                        offs_sb[:, pair * 2 * C // 16:(pair + 1) * 2 * C // 16]))
-
-        for pair in range(4):
-            gather_words(pair)
+                    g_words[half][:, s * S // 2:(s + 1) * S // 2],
+                    dyw[:, s * T:s * T + WORD_WINDOW].bitcast(U32).indirect(
+                        offs_sb[:, half * S // 32:(half + 1) * S // 32]))
 
         done = []
 
@@ -207,12 +207,12 @@ def tile_moe_bdx_glu_relu_kernel(
 
         def first_product(e, h):
             b = e * C // P + h
-            in_pair = (e % 2) * C + h * P
+            in_half = b * P % (S // 2)
             sums = psum.tile([P, H], F32, name="sums", bufs=2)
             for s in range(PASSES):
                 nc.tensor.matmul_mx(
                     out=sums[:],
-                    lhsT=g_words[e // 2][:, s * 2 * C + in_pair:s * 2 * C + in_pair + P].bitcast(FP8X4),
+                    lhsT=g_words[2 * e // E][:, s * S // 2 + in_half:s * S // 2 + in_half + P].bitcast(FP8X4),
                     lhsT_scale=g_scales[s][:, b * P:(b + 1) * P],
                     rhs=w2w[e][:, s * H * 2:(s + 1) * H * 2].bitcast(FP4X4),
                     rhs_scale=w2s[:, (e * PASSES + s) * H:(e * PASSES + s + 1) * H],
@@ -229,15 +229,9 @@ def tile_moe_bdx_glu_relu_kernel(
         halves = [(slice(h * P, (h + 1) * P), slice(h * R * P, (h + 1) * R * P)) for h in range(C // P)]
         dh = {}
         last = E - 1
-        wide = R * C
 
         def single(shape, dtype, tag):
             return ring.tile(shape, dtype, name=tag, tag=tag, align_bytes=64, bufs=1)
-
-        turns = ctx.enter_context(tc.tile_pool(name="turns", bufs=1))
-
-        def in_turn(shape, dtype, name, at):
-            return turns.tile(shape, dtype, name=name, align_bytes=64, offset=at * wide * 2)
 
         def make_relu(e, relu):
             nc.scalar.activation(out=woven_pairs(relu), in_=rows_by_pairs(a1_sb[e]), func=ACT.Relu)
@@ -332,11 +326,11 @@ def tile_moe_bdx_glu_relu_kernel(
             else:
                 for r in range(2):
                     nc.scalar.activation(out=part[r][:], in_=picked[r], func=ACT.Copy)
-            if g == len(pieces) - 1:
+            if g >= len(pieces) - 2:
                 nc.scalar.activation(out=part[4][:], in_=picked[2], func=ACT.Copy)
                 nc.vector.tensor_tensor(part[3][:], picked[3], part[0][:], ADD)
-                nc.vector.tensor_tensor(part[2][:], part[1][:], part[3][:], ADD)
-                nc.vector.tensor_tensor(part[5][:], part[2][:], part[4][:], ADD)
+                nc.vector.tensor_tensor(part[2][:], part[1][:], part[4][:], ADD)
+                nc.vector.tensor_tensor(part[5][:], part[2][:], part[3][:], ADD)
             else:
                 for r in range(2):
                     nc.vector.tensor_tensor(part[2 + r][:], picked[2 + r], part[r][:], ADD)

@@ -142,10 +142,11 @@ def tile_moe_bdx_glu_relu_kernel(
         def load_w13_scales(m, w_scales):
             load_scales(w13s[:, m * E * K:(m + 1) * E * K], w_scales[:, 0].rearrange("e f k -> f e k"), E)
 
-        def load_w13_words(m, w_words):
+        def load_w13_words(m, w_words, e0, n):
+            at = (m * E + e0) * K * 2
             nc.sync.dma_start(
-                out=w13w[:, m * E * K * 2:(m + 1) * E * K * 2].bitcast(I32).rearrange("p (e b) -> p e b", e=E),
-                in_=w_words[:, 0].rearrange("e p b -> p e b").bitcast(I32))
+                out=w13w[:, at:at + n * K * 2].bitcast(I32).rearrange("p (e b) -> p e b", e=n),
+                in_=w_words[e0:e0 + n, 0].rearrange("e p b -> p e b").bitcast(I32))
 
         for e0 in range(EARLY, E, 2):
             load_w2_pair(e0)
@@ -153,11 +154,13 @@ def tile_moe_bdx_glu_relu_kernel(
             if e0 < E - 2:
                 load_a3(e0, 2)
         load_w13_scales(0, w1_scales)
-        load_w13_words(0, w1_words)
+        load_w13_words(0, w1_words, 0, E - 2)
         load_w13_scales(1, w3_scales)
-        load_w13_words(1, w3_words)
+        load_w13_words(1, w3_words, 0, E - 2)
         load_a3(6, 1)
         load_a3(7, 1)
+        load_w13_words(1, w3_words, E - 2, 2)
+        load_w13_words(0, w1_words, E - 2, 2)
 
         g_words = []
         for half in range(2):
@@ -237,9 +240,9 @@ def tile_moe_bdx_glu_relu_kernel(
             nc.scalar.activation(out=woven_pairs(relu), in_=rows_by_pairs(a1_sb[e]), func=ACT.Relu)
 
         def make_mask(e, mask):
-            relu = ring.tile([P, wide], F32, name="relu", bufs=4)
-            make_relu(e, relu[:])
-            nc.scalar.activation(out=mask, in_=relu[:], func=ACT.Sign)
+            relu = ring.tile([P, R, C], F32, name="relu", bufs=4)
+            nc.scalar.activation(out=relu[:], in_=a1_sb[e], func=ACT.Relu)
+            nc.scalar.activation(out=woven_pairs(mask), in_=rows_by_pairs(relu[:]), func=ACT.Sign)
             return relu
 
         def ahead(b):
@@ -247,8 +250,9 @@ def tile_moe_bdx_glu_relu_kernel(
                 dh[b + 4] = first_product((b + 4) // 2, b % 2)
 
         def times_relu(e, h, da3, relu):
-            cols = halves[h][1]
-            nc.vector.tensor_tensor(woven(da3[:, cols]), rows_by_slot(dh[2 * e + h][:]), woven(relu[:, cols]), MULT)
+            slots, cols = halves[h]
+            nc.vector.tensor_tensor(woven_pairs(da3[:, cols]), rows_by_pairs(dh[2 * e + h][:]),
+                                    rows_by_pairs(relu[:, :, slots]), MULT)
 
         def times_a3(e, h, unmasked):
             slots, cols = halves[h]

@@ -27,8 +27,9 @@ IS_GT = mybir.AluOpType.is_gt
 
 EARLY = 2
 BY_GPSIMD = (0, 3)
-WORD_WINDOW = 2048
-SCALE_WINDOW = 2048
+WIDE = R * C
+DH_BANKS = 4
+WINDOW = 2048
 OVERLAP = 64
 
 
@@ -43,17 +44,13 @@ def tile_moe_bdx_glu_relu_kernel(
 
         offs_sb = keep.tile([P, S // 16], U16, name="offs_sb")
         pos_sb = [keep.tile([P, T // 16], U16, name="pos_sb%d" % r) for r in range(4)]
-        dyw = keep.tile([P, T + WORD_WINDOW], I32, name="dyw", align_bytes=64)
+        dyw = keep.tile([P, T + WINDOW], I32, name="dyw", align_bytes=64)
         share = ctx.enter_context(tc.tile_pool(name="share", bufs=1))
-        late_bytes = 2 * (E - EARLY) * R * C * 4
-        w13s_bytes = 2 * E * K
-        dys_tile = share.tile([P, w13s_bytes + 2 * OVERLAP], U8, name="dys", align_bytes=64,
-                              offset=late_bytes - OVERLAP)
-        dys = dys_tile[:, 0:SCALE_WINDOW]
+        late_bytes = 2 * (E - EARLY) * WIDE * 4
+        dys = share.tile([P, WINDOW], U8, name="dys", align_bytes=64, offset=late_bytes - OVERLAP)
         gs0 = keep.tile([P, S], U8, name="gs0", align_bytes=64)
         gs1 = keep.tile([P, S], U8, name="gs1", align_bytes=64)
         w2s = keep.tile([P, E * PASSES * H], U8, name="w2s", align_bytes=64)
-        w13w_bytes = 2 * E * K * 2
         gate_rows = keep.tile([P, P], F32, name="gate_rows")
         gate_col = keep.tile([P, S // P], F32, name="gate_col")
         ident = keep.tile([P, P], F32, name="ident")
@@ -65,13 +62,12 @@ def tile_moe_bdx_glu_relu_kernel(
         make_identity(nc, ident[:])
 
         w2w, a1_sb, a3_sb = {}, {}, {}
-        wide = R * C
+        w2_bytes = PASSES * H * 2
+        w13w_bytes = 2 * E * K * 2
         turns = ctx.enter_context(tc.tile_pool(name="turns", bufs=1))
 
-        def in_turn(shape, dtype, name, at):
-            return turns.tile(shape, dtype, name=name, align_bytes=64, offset=at * wide * 2)
-
-        w2_bytes = PASSES * H * 2
+        def in_turn(shape, dtype, name, place):
+            return turns.tile(shape, dtype, name=name, align_bytes=64, offset=place * WIDE * 2)
 
         def load_w2(dst, e0, n):
             nc.sync.dma_start(
@@ -92,9 +88,9 @@ def tile_moe_bdx_glu_relu_kernel(
                     out=plane[r:P:32, :].bitcast(I32).rearrange("q (g i) -> q g i", g=groups),
                     in_=rows[r:16:4].bitcast(I32))
 
-        early_w2 = keep.tile([P, EARLY * w2_bytes], U8, name="early_w2", align_bytes=64)
-        early_a1 = in_turn([P, EARLY * wide], F32, "early_a1", 12)
-        early_a3 = keep.tile([P, EARLY * R * C], F32, name="early_a3")
+        early_w2 = keep.tile([P, EARLY * w2_bytes], U8, name="early_w2", tag="early_w2", align_bytes=64)
+        early_a1 = in_turn([P, EARLY * WIDE], F32, "early_a1", 12)
+        early_a3 = keep.tile([P, EARLY * WIDE], F32, name="early_a3")
 
         nc.sync.dma_start(offs_sb[:], offs)
         nc.sync.dma_start(out=gate_rows[:], in_=gate[0:P * P // S, :].rearrange("h (b p) -> (h b) p", p=P))
@@ -110,57 +106,45 @@ def tile_moe_bdx_glu_relu_kernel(
             nc.sync.dma_start(pos_sb[r][:], pos)
         load_saved(a3, a3_sb, early_a3[:], 0, EARLY)
 
-        gate_ps = psum.tile([P, P], F32, name="gate_ps", tag="bank5")
+        gate_ps = psum.tile([P, P], F32, name="gate_ps", tag="bank%d" % (DH_BANKS + 1))
         nc.tensor.transpose(gate_ps[:], gate_rows[:], ident[:])
         nc.scalar.copy(gate_col[:], gate_ps[:, 0:S // P])
 
         for half in range(2):
             nc.vector.tensor_copy(gs0[:, half * S // 2:(half + 1) * S // 2],
-                                  dys.indirect(offs_sb[:, half * S // 32:(half + 1) * S // 32]))
+                                  dys[:].indirect(offs_sb[:, half * S // 32:(half + 1) * S // 32]))
         for r in range(4):
             nc.sync.dma_start(out=gs1[r:P:32, :].bitcast(I32), in_=gs0[4 + r:P:32, :].bitcast(I32))
         g_scales = (gs0, gs1)
 
         saved = share.tile([P, late_bytes // 4], F32, name="saved", align_bytes=64, offset=0)
         weights = share.tile([P, w13w_bytes + (E - EARLY) * w2_bytes], U8, name="weights",
-                             align_bytes=64, offset=late_bytes + w13s_bytes)
+                             align_bytes=64, offset=late_bytes + WINDOW - 2 * OVERLAP)
         w13w = weights[:, 0:w13w_bytes]
-        w13s = share.tile([P, w13s_bytes], U8, name="w13s", align_bytes=64, offset=late_bytes)
 
         def load_a1(e0, n):
-            at = (e0 - EARLY) * R * C
-            load_saved(a1, a1_sb, saved[:, at:at + n * R * C], e0, n)
+            at = (e0 - EARLY) * WIDE
+            load_saved(a1, a1_sb, saved[:, at:at + n * WIDE], e0, n)
 
         def load_a3(e0, n):
-            at = (E - EARLY + e0 - EARLY) * R * C
-            load_saved(a3, a3_sb, saved[:, at:at + n * R * C], e0, n)
+            at = (E - EARLY + e0 - EARLY) * WIDE
+            load_saved(a3, a3_sb, saved[:, at:at + n * WIDE], e0, n)
 
         def load_w2_pair(e0):
             at = w13w_bytes + (e0 - EARLY) * w2_bytes
             load_w2(weights[:, at:at + 2 * w2_bytes], e0, 2)
 
-        def load_w13_scales(m, w_scales):
-            load_scales(w13s[:, m * E * K:(m + 1) * E * K], w_scales[:, 0].rearrange("e f k -> f e k"), E)
-
-        def load_w13_words(m, w_words, e0, n):
+        def load_w13_words(m, e0, n):
             at = (m * E + e0) * K * 2
             nc.sync.dma_start(
                 out=w13w[:, at:at + n * K * 2].bitcast(I32).rearrange("p (e b) -> p e b", e=n),
-                in_=w_words[e0:e0 + n, 0].rearrange("e p b -> p e b").bitcast(I32))
+                in_=(w1_words, w3_words)[m][e0:e0 + n, 0].rearrange("e p b -> p e b").bitcast(I32))
 
         for e0 in range(EARLY, E, 2):
             load_w2_pair(e0)
             load_a1(e0, 2)
             if e0 < E - 2:
                 load_a3(e0, 2)
-        load_w13_scales(0, w1_scales)
-        load_w13_words(0, w1_words, 0, E - 2)
-        load_w13_scales(1, w3_scales)
-        load_w13_words(1, w3_words, 0, E - 2)
-        load_a3(6, 1)
-        load_a3(7, 1)
-        load_w13_words(1, w3_words, E - 2, 2)
-        load_w13_words(0, w1_words, E - 2, 2)
 
         g_words = []
         for half in range(2):
@@ -168,15 +152,15 @@ def tile_moe_bdx_glu_relu_kernel(
             for s in range(PASSES):
                 nc.vector.tensor_copy(
                     g_words[half][:, s * S // 2:(s + 1) * S // 2],
-                    dyw[:, s * T:s * T + WORD_WINDOW].bitcast(U32).indirect(
+                    dyw[:, s * T:s * T + WINDOW].bitcast(U32).indirect(
                         offs_sb[:, half * S // 32:(half + 1) * S // 32]))
 
-        done = []
+        multiplied = []
 
         def quantise(codes, da):
             scales = ring.tile([P, 2 * C], U8, name="scales", align_bytes=64, bufs=E)
             nc.vector.quantize_mx(out=codes[:].bitcast(FP8X4), scales=scales[:], in_=da[:])
-            return [(codes[:, part * C:(part + 1) * C], scales[:, part * C:(part + 1) * C]) for part in range(2)]
+            return [(codes[:, i * C:(i + 1) * C], scales[:, i * C:(i + 1) * C]) for i in range(2)]
 
         def multiply(acc, e, kb, m, operand, start):
             col = (m * E + e) * K + kb * P
@@ -188,8 +172,8 @@ def tile_moe_bdx_glu_relu_kernel(
                 start=start, stop=not start)
 
         def second_product(e, operands):
-            acc = psum.tile([P, K // P, C], F32, name="acc", tag="bank%d" % (4 + len(done) % 2))
-            done.append(e)
+            acc = psum.tile([P, K // P, C], F32, name="acc", tag="bank%d" % (DH_BANKS + len(multiplied) % 2))
+            multiplied.append(e)
             for kb in range(K // P):
                 for m in range(2):
                     multiply(acc[:, kb, :], e, kb, m, operands[m], m == 0)
@@ -208,14 +192,16 @@ def tile_moe_bdx_glu_relu_kernel(
         def rows_by_pairs(ap):
             return ap.rearrange("p r (c i) -> p c r i", i=2)
 
-        def first_product(e, h):
-            b = e * C // P + h
-            in_half = b * P % (S // 2)
+        dh = {}
+
+        def first_product(b):
+            e = b // 2
+            half, in_half = divmod(b * P, S // 2)
             sums = psum.tile([P, H], F32, name="sums", bufs=2)
             for s in range(PASSES):
                 nc.tensor.matmul_mx(
                     out=sums[:],
-                    lhsT=g_words[2 * e // E][:, s * S // 2 + in_half:s * S // 2 + in_half + P].bitcast(FP8X4),
+                    lhsT=g_words[half][:, s * S // 2 + in_half:s * S // 2 + in_half + P].bitcast(FP8X4),
                     lhsT_scale=g_scales[s][:, b * P:(b + 1) * P],
                     rhs=w2w[e][:, s * H * 2:(s + 1) * H * 2].bitcast(FP4X4),
                     rhs_scale=w2s[:, (e * PASSES + s) * H:(e * PASSES + s + 1) * H],
@@ -224,119 +210,141 @@ def tile_moe_bdx_glu_relu_kernel(
             nc.scalar.activation(out=dh_t[:].rearrange("j (u v) p -> j u p v", v=2),
                                  in_=sums[:].rearrange("j (p u v) -> j u p v", u=2, v=2),
                                  func=ACT.Copy, scale=gate_col[:, b:b + 1])
-            dh = psum.tile([P, R, P], F32, name="dh", tag="bank%d" % (b % 4))
+            dh[b] = psum.tile([P, R, P], F32, name="dh", tag="bank%d" % (b % DH_BANKS))
             for r in range(R):
-                nc.tensor.transpose(dh[:, r, :], dh_t[:, r, :], ident[:])
-            return dh
+                nc.tensor.transpose(dh[b][:, r, :], dh_t[:, r, :], ident[:])
 
-        halves = [(slice(h * P, (h + 1) * P), slice(h * R * P, (h + 1) * R * P)) for h in range(C // P)]
-        dh = {}
-        last = E - 1
+        blocks = [(slice(h * P, (h + 1) * P), slice(h * R * P, (h + 1) * R * P)) for h in range(C // P)]
 
         def single(shape, dtype, tag):
             return ring.tile(shape, dtype, name=tag, tag=tag, align_bytes=64, bufs=1)
 
-        def make_relu(e, relu):
-            nc.scalar.activation(out=woven_pairs(relu), in_=rows_by_pairs(a1_sb[e]), func=ACT.Relu)
-
-        def make_mask(e, mask):
+        def relu_and_mask(e, mask):
             relu = ring.tile([P, R, C], F32, name="relu", bufs=4)
             nc.scalar.activation(out=relu[:], in_=a1_sb[e], func=ACT.Relu)
             nc.scalar.activation(out=woven_pairs(mask), in_=rows_by_pairs(relu[:]), func=ACT.Sign)
             return relu
 
-        def ahead(b):
-            if b + 4 < S // P:
-                dh[b + 4] = first_product((b + 4) // 2, b % 2)
+        def leave_bank(b):
+            if b + DH_BANKS < S // P:
+                first_product(b + DH_BANKS)
 
-        def times_relu(e, h, da3, relu):
-            slots, cols = halves[h]
-            nc.vector.tensor_tensor(woven_pairs(da3[:, cols]), rows_by_pairs(dh[2 * e + h][:]),
-                                    rows_by_pairs(relu[:, :, slots]), MULT)
+        def times_dh(e, h, product, rows):
+            slots, cols = blocks[h]
+            nc.vector.tensor_tensor(woven_pairs(product[:, cols]), rows_by_pairs(dh[2 * e + h][:]),
+                                    rows_by_pairs(rows[:, :, slots]), MULT)
 
-        def times_a3(e, h, unmasked):
-            slots, cols = halves[h]
-            nc.vector.tensor_tensor(woven_pairs(unmasked[:, cols]), rows_by_pairs(dh[2 * e + h][:]),
-                                    rows_by_pairs(a3_sb[e][:, :, slots]), MULT)
-            ahead(2 * e + h)
+        def part(tile, i):
+            return tile[:, i * WIDE:(i + 1) * WIDE]
 
-        for b in range(4):
-            dh[b] = first_product(b // 2, b % 2)
+        for b in range(DH_BANKS):
+            first_product(b)
+
+        w13s = keep.tile([P, 2 * E * K], U8, name="w13s", tag="early_w2", align_bytes=64)
+        for m, w_scales in enumerate((w1_scales, w3_scales)):
+            load_scales(w13s[:, m * E * K:(m + 1) * E * K], w_scales[:, 0].rearrange("e f k -> f e k"), E)
+            load_w13_words(m, 0, E - 2)
+        for e in (E - 2, E - 1):
+            load_a3(e, 1)
+        for m in (1, 0):
+            load_w13_words(m, E - 2, 2)
+
         for period, g in enumerate(BY_GPSIMD):
-            at = 4 * period
-            relu = in_turn([P, wide], F32, "relu%d" % g, at)
-            make_relu(g, relu[:])
-            dh_masked = in_turn([P, wide], F32, "dh_masked%d" % g, at + 2)
-            da = single([P, 2 * wide], BF16, "da%d" % g)
-            for h, (slots, cols) in enumerate(halves):
-                nc.vector.scalar_tensor_tensor(woven(dh_masked[:, cols]), woven(relu[:, cols]), 0.0,
+            place = 4 * period
+            relu_woven = in_turn([P, WIDE], F32, "relu_woven%d" % g, place)
+            nc.scalar.activation(out=woven_pairs(relu_woven[:]), in_=rows_by_pairs(a1_sb[g]), func=ACT.Relu)
+            dh_masked = in_turn([P, WIDE], F32, "dh_masked%d" % g, place + 2)
+            da = single([P, 2 * WIDE], BF16, "da%d" % g)
+            for h, (slots, cols) in enumerate(blocks):
+                nc.vector.scalar_tensor_tensor(woven(dh_masked[:, cols]), woven(relu_woven[:, cols]), 0.0,
                                                rows_by_slot(dh[2 * g + h][:]), IS_GT, MULT)
-                nc.gpsimd.tensor_tensor(da[:, wide:][:, cols], dh_masked[:, cols], relu[:, cols], MULT)
+                nc.gpsimd.tensor_tensor(part(da, 1)[:, cols], dh_masked[:, cols], relu_woven[:, cols], MULT)
                 nc.gpsimd.tensor_tensor(woven(da[:, cols]), woven(dh_masked[:, cols]),
                                         rows_by_slot(a3_sb[g][:, :, slots]), MULT)
-                ahead(2 * g + h)
-            mask = single([P, 2 * wide], BF16, "mask%d" % g)
-            da3 = single([P, 2 * wide], BF16, "da3_%d" % g)
-            unmasked = in_turn([P, 2 * wide], BF16, "unmasked%d" % g, at + 6)
-            for i in range(2):
-                relu = make_mask(g + 1 + i, mask[:, i * wide:(i + 1) * wide])
+                leave_bank(2 * g + h)
+            mask = single([P, 2 * WIDE], BF16, "mask%d" % g)
+            da3 = single([P, 2 * WIDE], BF16, "da3_%d" % g)
+            unmasked = in_turn([P, 2 * WIDE], BF16, "unmasked%d" % g, place + 6)
+            for i, e in enumerate((g + 1, g + 2)):
+                relu = relu_and_mask(e, part(mask, i))
                 for h in range(2):
-                    times_relu(g + 1 + i, h, da3[:, i * wide:(i + 1) * wide], relu)
-                    times_a3(g + 1 + i, h, unmasked[:, i * wide:(i + 1) * wide])
-            by_w3 = quantise(in_turn([P, 2 * C], U32, "codes3_%d" % g, at), da3)
-            da1 = in_turn([P, 2 * wide], BF16, "da1_%d" % g, at + 2)
+                    times_dh(e, h, part(da3, i), relu)
+                    times_dh(e, h, part(unmasked, i), a3_sb[e])
+                    leave_bank(2 * e + h)
+            for_w3 = quantise(in_turn([P, 2 * C], U32, "codes3_%d" % g, place), da3)
+            da1 = in_turn([P, 2 * WIDE], BF16, "da1_%d" % g, place + 2)
             nc.vector.tensor_tensor(da1[:], unmasked[:], mask[:], MULT)
             second_product(g, quantise(single([P, 2 * C], U32, "mask%d" % g), da))
-            by_w1 = quantise(in_turn([P, 2 * C], U32, "codes1_%d" % g, at + 1), da1)
-            for i in range(2):
-                second_product(g + 1 + i, (by_w1[i], by_w3[i]))
+            for_w1 = quantise(in_turn([P, 2 * C], U32, "codes1_%d" % g, place + 1), da1)
+            for i, e in enumerate((g + 1, g + 2)):
+                second_product(e, (for_w1[i], for_w3[i]))
 
-        mask = single([P, 2 * wide], BF16, "mask6")
-        unmasked = single([P, 2 * wide], BF16, "unmasked6")
-        relu = [make_mask(6 + i, mask[:, i * wide:(i + 1) * wide]) for i in range(2)]
-        da = [single([P, 2 * wide], BF16, "da%d" % g) for g in BY_GPSIMD]
+        before, last = E - 2, E - 1
+        mask = single([P, 2 * WIDE], BF16, "mask_last")
+        unmasked = single([P, 2 * WIDE], BF16, "unmasked_last")
+        relu_before, relu_last = [relu_and_mask(e, part(mask, i)) for i, e in enumerate((before, last))]
+        da_before, da_last = [single([P, 2 * WIDE], BF16, "da%d" % g) for g in BY_GPSIMD]
         for h in range(2):
-            times_relu(6, h, da[0][:, wide:], relu[0])
-            times_a3(6, h, unmasked[:, 0:wide])
-        nc.vector.tensor_tensor(da[0][:, 0:wide], unmasked[:, 0:wide], mask[:, 0:wide], MULT)
-        times_relu(last, 0, da[1][:, wide:], relu[1])
-        second_product(6, quantise(single([P, 2 * C], U32, "codes6"), da[0]))
-        times_relu(last, 1, da[1][:, wide:], relu[1])
+            times_dh(before, h, part(da_before, 1), relu_before)
+            times_dh(before, h, part(unmasked, 0), a3_sb[before])
+        nc.vector.tensor_tensor(part(da_before, 0), part(unmasked, 0), part(mask, 0), MULT)
+        times_dh(last, 0, part(da_last, 1), relu_last)
+        second_product(before, quantise(single([P, 2 * C], U32, "codes_before"), da_before))
+        times_dh(last, 1, part(da_last, 1), relu_last)
         for h in range(2):
-            times_a3(last, h, unmasked[:, wide:])
-        codes = single([P, 2 * C], U32, "codes7")
+            times_dh(last, h, part(unmasked, 1), a3_sb[last])
+        codes = single([P, 2 * C], U32, "codes_last")
         scales = ring.tile([P, 2 * C], U8, name="scales", align_bytes=64, bufs=E)
         acc = [psum.tile([P, C], F32, name="acc", tag="bank%d" % kb) for kb in range(K // P)]
-        for m in (1, 0):
-            cols = halves[1 - m][1]
-            nc.vector.tensor_tensor(da[1][:, cols], unmasked[:, wide:][:, cols], mask[:, wide:][:, cols], MULT)
+        for (slots, cols), m in zip(blocks, (1, 0)):
+            nc.vector.tensor_tensor(da_last[:, cols], part(unmasked, 1)[:, cols], part(mask, 1)[:, cols], MULT)
             operand = (codes[:, m * C:(m + 1) * C], scales[:, m * C:(m + 1) * C])
-            nc.vector.quantize_mx(out=operand[0].bitcast(FP8X4), scales=operand[1],
-                                  in_=da[1][:, m * wide:(m + 1) * wide])
+            nc.vector.quantize_mx(out=operand[0].bitcast(FP8X4), scales=operand[1], in_=part(da_last, m))
             for kb in range(K // P):
                 multiply(acc[kb][:], last, kb, m, operand, m == 1)
         nc.vector.tensor_copy(dx[0][:, last * C:], acc[0][:])
         nc.scalar.copy(dx[1][:, last * C:], acc[1][:])
 
         half_t = T // 2
-        pieces = [(kb, h) for kb in range(K // P) for h in range(2)]
-        for g, (kb, h) in enumerate(pieces):
-            part = [share.tile([P, half_t], F32, name="part%d_%d" % (g, r), offset=(g * 6 + r) * half_t * 4)
-                    for r in range(6)]
-            picked = [dx[kb][:].indirect(pos_sb[r][:, h * half_t // 16:(h + 1) * half_t // 16]) for r in range(4)]
-            if g == 0:
-                nc.vector.tensor_copy(part[1][:], picked[1])
-                nc.scalar.activation(out=part[0][:], in_=picked[0], func=ACT.Copy)
-            else:
-                for r in range(2):
-                    nc.scalar.activation(out=part[r][:], in_=picked[r], func=ACT.Copy)
-            if g >= len(pieces) - 2:
-                nc.scalar.activation(out=part[4][:], in_=picked[2], func=ACT.Copy)
-                nc.vector.tensor_tensor(part[3][:], picked[3], part[0][:], ADD)
-                nc.vector.tensor_tensor(part[2][:], part[1][:], part[4][:], ADD)
-                nc.vector.tensor_tensor(part[5][:], part[2][:], part[3][:], ADD)
-            else:
-                for r in range(2):
-                    nc.vector.tensor_tensor(part[2 + r][:], picked[2 + r], part[r][:], ADD)
-                nc.vector.tensor_tensor(part[5][:], part[2][:], part[3][:], ADD)
-            nc.sync.dma_start(out=out[kb * P:(kb + 1) * P, h * half_t:(h + 1) * half_t], in_=part[5][:])
+        used = []
+
+        def fresh():
+            used.append(share.tile([P, half_t], F32, name="value%d" % len(used), offset=len(used) * half_t * 4))
+            return used[-1][:]
+
+        def picked(piece, r):
+            kb, h = divmod(piece, 2)
+            return dx[kb][:].indirect(pos_sb[r][:, h * half_t // 16:(h + 1) * half_t // 16])
+
+        def fetch(piece, r):
+            value = fresh()
+            nc.scalar.activation(out=value, in_=picked(piece, r), func=ACT.Copy)
+            return value
+
+        def add(first, second):
+            value = fresh()
+            nc.vector.tensor_tensor(value, first, second, ADD)
+            return value
+
+        def store(piece, value):
+            kb, h = divmod(piece, 2)
+            nc.sync.dma_start(out=out[kb * P:(kb + 1) * P, h * half_t:(h + 1) * half_t], in_=value)
+
+        fetched = {(0, 1): fresh()}
+        nc.vector.tensor_copy(fetched[0, 1], picked(0, 1))
+        fetched[0, 0] = fetch(0, 0)
+        for r in range(2):
+            fetched[1, r] = fetch(1, r)
+        for r in range(3):
+            for piece in (2, 3):
+                fetched[piece, r] = fetch(piece, r)
+        sums0 = [add(picked(0, 2 + r), fetched[0, r]) for r in range(2)]
+        sums1 = [add(picked(1, 2), fetched[1, 0])]
+        store(0, add(*sums0))
+        sums1.append(add(picked(1, 3), fetched[1, 1]))
+        running = [add(picked(2, 3), fetched[2, 0])]
+        store(1, add(*sums1))
+        running.append(add(picked(3, 3), fetched[3, 0]))
+        running = [add(running[h], fetched[2 + h, 1]) for h in range(2)]
+        for h in range(2):
+            store(2 + h, add(running[h], fetched[2 + h, 2]))

@@ -46,7 +46,7 @@ def tile_moe_bdx_glu_relu_kernel(
         pos_sb = [keep.tile([P, T // 16], U16, name="pos_sb%d" % r) for r in range(4)]
         dyw = keep.tile([P, T + WINDOW], I32, name="dyw", align_bytes=64)
         share = ctx.enter_context(tc.tile_pool(name="share", bufs=1))
-        late_bytes = 2 * (E - EARLY) * WIDE * 4
+        late_bytes = (2 * E - EARLY) * WIDE * 4
         dys = share.tile([P, WINDOW], U8, name="dys", align_bytes=64, offset=late_bytes - OVERLAP)
         gs0 = keep.tile([P, S], U8, name="gs0", align_bytes=64)
         gs1 = keep.tile([P, S], U8, name="gs1", align_bytes=64)
@@ -89,8 +89,6 @@ def tile_moe_bdx_glu_relu_kernel(
                     in_=rows[r:16:4].bitcast(I32))
 
         early_w2 = keep.tile([P, EARLY * w2_bytes], U8, name="early_w2", tag="early_w2", align_bytes=64)
-        early_a1 = in_turn([P, EARLY * WIDE], F32, "early_a1", 12)
-        early_a3 = keep.tile([P, EARLY * WIDE], F32, name="early_a3")
 
         nc.sync.dma_start(offs_sb[:], offs)
         nc.sync.dma_start(out=gate_rows[:], in_=gate[0:P * P // S, :].rearrange("h (b p) -> (h b) p", p=P))
@@ -99,12 +97,11 @@ def tile_moe_bdx_glu_relu_kernel(
                               in_=dy_scales[:, 4 * q:4 * q + 4, :].bitcast(I32))
         nc.sync.dma_start(out=dyw[:, 0:PASSES * T].rearrange("p (o t) -> p o t", o=PASSES),
                           in_=dy_words.rearrange("o p t d -> p o (t d)").bitcast(I32))
-        load_saved(a1, a1_sb, early_a1[:], 0, EARLY)
+        load_saved(a1, a1_sb, keep.tile([P, EARLY * WIDE], F32, name="early_a1")[:], 0, EARLY)
         load_w2(early_w2[:], 0, EARLY)
-        load_scales(w2s, w2_scales.rearrange("e s f i -> f (e s) i"), E * PASSES)
         for r, pos in enumerate((pos1, pos2, pos3, pos4)):
             nc.sync.dma_start(pos_sb[r][:], pos)
-        load_saved(a3, a3_sb, early_a3[:], 0, EARLY)
+        load_scales(w2s, w2_scales.rearrange("e s f i -> f (e s) i"), E * PASSES)
 
         gate_ps = psum.tile([P, P], F32, name="gate_ps", tag="bank%d" % (DH_BANKS + 1))
         nc.tensor.transpose(gate_ps[:], gate_rows[:], ident[:])
@@ -127,7 +124,7 @@ def tile_moe_bdx_glu_relu_kernel(
             load_saved(a1, a1_sb, saved[:, at:at + n * WIDE], e0, n)
 
         def load_a3(e0, n):
-            at = (E - EARLY + e0 - EARLY) * WIDE
+            at = (E - EARLY + e0) * WIDE
             load_saved(a3, a3_sb, saved[:, at:at + n * WIDE], e0, n)
 
         def load_w2_pair(e0):
@@ -140,22 +137,27 @@ def tile_moe_bdx_glu_relu_kernel(
                 out=w13w[:, at:at + n * K * 2].bitcast(I32).rearrange("p (e b) -> p e b", e=n),
                 in_=(w1_words, w3_words)[m][e0:e0 + n, 0].rearrange("e p b -> p e b").bitcast(I32))
 
-        for e0 in range(EARLY, E, 2):
-            load_w2_pair(e0)
-            load_a1(e0, 2)
-            if e0 < E - 2:
-                load_a3(e0, 2)
+        load_w2_pair(2)
+        load_a1(2, 2)
+        load_a3(0, 2)
+        load_a3(2, 2)
+        load_w2_pair(4)
+        load_a1(4, 2)
+        load_w2_pair(6)
+        load_a3(4, 2)
+        load_a1(6, 2)
+        load_a3(6, 2)
 
-        g_words = []
-        for half in range(2):
-            g_words.append(keep.tile([P, PASSES * S // 2], U32, name="g_words%d" % half, align_bytes=64))
+        g_words = {}
+        for e0, n in ((0, 2), (2, 2), (4, 4)):
             for s in range(PASSES):
-                nc.vector.tensor_copy(
-                    g_words[half][:, s * S // 2:(s + 1) * S // 2],
-                    dyw[:, s * T:s * T + WINDOW].bitcast(U32).indirect(
-                        offs_sb[:, half * S // 32:(half + 1) * S // 32]))
+                words = keep.tile([P, n * C], U32, name="g_words%d_%d" % (e0, s), align_bytes=64)
+                nc.vector.tensor_copy(words[:], dyw[:, s * T:s * T + WINDOW].bitcast(U32).indirect(
+                    offs_sb[:, e0 * C // 16:(e0 + n) * C // 16]))
+                for e in range(n):
+                    g_words[e0 + e, s] = words[:, e * C:(e + 1) * C]
 
-        multiplied = []
+        operands = {}
 
         def quantise(codes, da):
             scales = ring.tile([P, 2 * C], U8, name="scales", align_bytes=64, bufs=E)
@@ -172,8 +174,7 @@ def tile_moe_bdx_glu_relu_kernel(
                 start=start, stop=not start)
 
         def second_product(e, operands):
-            acc = psum.tile([P, K // P, C], F32, name="acc", tag="bank%d" % (DH_BANKS + len(multiplied) % 2))
-            multiplied.append(e)
+            acc = psum.tile([P, K // P, C], F32, name="acc%d" % e, tag="bank%d" % (6, 7, 2, 3)[e % 4])
             for kb in range(K // P):
                 for m in range(2):
                     multiply(acc[:, kb, :], e, kb, m, operands[m], m == 0)
@@ -192,25 +193,29 @@ def tile_moe_bdx_glu_relu_kernel(
         def rows_by_pairs(ap):
             return ap.rearrange("p r (c i) -> p c r i", i=2)
 
-        dh = {}
+        dh, turned = {}, {}
+        AHEAD = 6
 
         def first_product(b):
-            e = b // 2
-            half, in_half = divmod(b * P, S // 2)
-            sums = psum.tile([P, H], F32, name="sums", bufs=2)
+            e, h = divmod(b, 2)
+            sums = psum.tile([P, H], F32, name="sums%d" % b, tag="bank%d" % (7 - b % (4 if b < 8 else 2)))
             for s in range(PASSES):
                 nc.tensor.matmul_mx(
                     out=sums[:],
-                    lhsT=g_words[half][:, s * S // 2 + in_half:s * S // 2 + in_half + P].bitcast(FP8X4),
+                    lhsT=g_words[e, s][:, h * P:(h + 1) * P].bitcast(FP8X4),
                     lhsT_scale=g_scales[s][:, b * P:(b + 1) * P],
                     rhs=w2w[e][:, s * H * 2:(s + 1) * H * 2].bitcast(FP4X4),
                     rhs_scale=w2s[:, (e * PASSES + s) * H:(e * PASSES + s + 1) * H],
                     start=(s == 0), stop=(s == PASSES - 1))
-            dh_t = ring.tile([P, R, P], F32, name="dh_t")
+            dh_t = ring.tile([P, R, P], F32, name="dh_t%d" % b, tag="dh_t", bufs=6)
             nc.scalar.activation(out=dh_t[:].rearrange("j (u v) p -> j u p v", v=2),
                                  in_=sums[:].rearrange("j (p u v) -> j u p v", u=2, v=2),
                                  func=ACT.Copy, scale=gate_col[:, b:b + 1])
-            dh[b] = psum.tile([P, R, P], F32, name="dh", tag="bank%d" % (b % DH_BANKS))
+            turned[b] = dh_t
+
+        def turn(b):
+            dh_t = turned[b]
+            dh[b] = psum.tile([P, R, P], F32, name="dh%d" % b, tag="bank%d" % (b % 4 if b < 12 else (b - 8) % 6))
             for r in range(R):
                 nc.tensor.transpose(dh[b][:, r, :], dh_t[:, r, :], ident[:])
 
@@ -220,14 +225,18 @@ def tile_moe_bdx_glu_relu_kernel(
             return ring.tile(shape, dtype, name=tag, tag=tag, align_bytes=64, bufs=1)
 
         def relu_and_mask(e, mask):
-            relu = ring.tile([P, R, C], F32, name="relu", bufs=4)
+            relu = ring.tile([P, R, C], F32, name="relu%d" % e, tag="relu", bufs=4)
             nc.scalar.activation(out=relu[:], in_=a1_sb[e], func=ACT.Relu)
             nc.scalar.activation(out=woven_pairs(mask), in_=rows_by_pairs(relu[:]), func=ACT.Sign)
             return relu
 
         def leave_bank(b):
-            if b + DH_BANKS < S // P:
-                first_product(b + DH_BANKS)
+            if b < 8:
+                turn(b + DH_BANKS)
+            if b in (6, 7, 8, 9):
+                turn(b + 6)
+            if b + DH_BANKS + AHEAD < S // P:
+                first_product(b + DH_BANKS + AHEAD)
 
         def times_dh(e, h, product, rows):
             slots, cols = blocks[h]
@@ -239,15 +248,16 @@ def tile_moe_bdx_glu_relu_kernel(
 
         for b in range(DH_BANKS):
             first_product(b)
+            turn(b)
+        for b in range(DH_BANKS, DH_BANKS + AHEAD):
+            first_product(b)
 
         w13s = keep.tile([P, 2 * E * K], U8, name="w13s", tag="early_w2", align_bytes=64)
         for m, w_scales in enumerate((w1_scales, w3_scales)):
             load_scales(w13s[:, m * E * K:(m + 1) * E * K], w_scales[:, 0].rearrange("e f k -> f e k"), E)
-            load_w13_words(m, 0, E - 2)
-        for e in (E - 2, E - 1):
-            load_a3(e, 1)
-        for m in (1, 0):
-            load_w13_words(m, E - 2, 2)
+        for e0 in (0, E // 2):
+            for m in range(2):
+                load_w13_words(m, e0, E // 2)
 
         for period, g in enumerate(BY_GPSIMD):
             place = 4 * period
@@ -274,15 +284,17 @@ def tile_moe_bdx_glu_relu_kernel(
             for_w3 = quantise(in_turn([P, 2 * C], U32, "codes3_%d" % g, place), da3)
             da1 = in_turn([P, 2 * WIDE], BF16, "da1_%d" % g, place + 2)
             nc.vector.tensor_tensor(da1[:], unmasked[:], mask[:], MULT)
-            second_product(g, quantise(single([P, 2 * C], U32, "mask%d" % g), da))
+            operands[g] = quantise(single([P, 2 * C], U32, "mask%d" % g), da)
             for_w1 = quantise(in_turn([P, 2 * C], U32, "codes1_%d" % g, place + 1), da1)
             for i, e in enumerate((g + 1, g + 2)):
-                second_product(e, (for_w1[i], for_w3[i]))
+                operands[e] = (for_w1[i], for_w3[i])
 
         before, last = E - 2, E - 1
         mask = single([P, 2 * WIDE], BF16, "mask_last")
-        unmasked = single([P, 2 * WIDE], BF16, "unmasked_last")
+        unmasked = in_turn([P, 2 * WIDE], BF16, "unmasked_last", 10)
         relu_before, relu_last = [relu_and_mask(e, part(mask, i)) for i, e in enumerate((before, last))]
+        for e in range(before):
+            second_product(e, operands[e])
         da_before, da_last = [single([P, 2 * WIDE], BF16, "da%d" % g) for g in BY_GPSIMD]
         for h in range(2):
             times_dh(before, h, part(da_before, 1), relu_before)
@@ -295,7 +307,7 @@ def tile_moe_bdx_glu_relu_kernel(
             times_dh(last, h, part(unmasked, 1), a3_sb[last])
         codes = single([P, 2 * C], U32, "codes_last")
         scales = ring.tile([P, 2 * C], U8, name="scales", align_bytes=64, bufs=E)
-        acc = [psum.tile([P, C], F32, name="acc", tag="bank%d" % kb) for kb in range(K // P)]
+        acc = [psum.tile([P, C], F32, name="acc", tag="bank%d" % bank) for bank in (3, 6)]
         for (slots, cols), m in zip(blocks, (1, 0)):
             nc.vector.tensor_tensor(da_last[:, cols], part(unmasked, 1)[:, cols], part(mask, 1)[:, cols], MULT)
             operand = (codes[:, m * C:(m + 1) * C], scales[:, m * C:(m + 1) * C])

@@ -25,6 +25,7 @@ MULT = mybir.AluOpType.mult
 ADD = mybir.AluOpType.add
 IS_GT = mybir.AluOpType.is_gt
 
+HELD_AT = (0, 4, 9)
 EARLY = 2
 BY_GPSIMD = (0, 3)
 WIDE = R * C
@@ -259,28 +260,43 @@ def tile_moe_bdx_glu_relu_kernel(
             for m in range(2):
                 load_w13_words(m, e0, E // 2)
 
+        relu_woven, dh_masked = {}, {}
+
+        def weave_relu(g, place):
+            relu_woven[g] = in_turn([P, WIDE], F32, "relu_woven%d" % g, place)
+            nc.scalar.activation(out=woven_pairs(relu_woven[g][:]), in_=rows_by_pairs(a1_sb[g]), func=ACT.Relu)
+
+        def mask_dh(g, place):
+            dh_masked[g] = in_turn([P, WIDE], F32, "dh_masked%d" % g, place + 2)
+            for h, (slots, cols) in enumerate(blocks):
+                nc.vector.scalar_tensor_tensor(woven(dh_masked[g][:, cols]), woven(relu_woven[g][:, cols]), 0.0,
+                                               rows_by_slot(dh[2 * g + h][:]), IS_GT, MULT)
+                if g < E - 2:
+                    leave_bank(2 * g + h)
+
+        def da1_on_gpsimd(g, da, slots, cols):
+            nc.gpsimd.tensor_tensor(woven(da[:, cols]), woven(dh_masked[g][:, cols]),
+                                    rows_by_slot(a3_sb[g][:, :, slots]), MULT)
+
+        for period in range(3):
+            weave_relu(3 * period, HELD_AT[period])
+        mask_dh(0, 0)
+        da = single([P, 2 * WIDE], BF16, "da0")
         for period, g in enumerate(BY_GPSIMD):
             place = 4 * period
-            relu_woven = in_turn([P, WIDE], F32, "relu_woven%d" % g, place)
-            nc.scalar.activation(out=woven_pairs(relu_woven[:]), in_=rows_by_pairs(a1_sb[g]), func=ACT.Relu)
-            dh_masked = in_turn([P, WIDE], F32, "dh_masked%d" % g, place + 2)
-            da = single([P, 2 * WIDE], BF16, "da%d" % g)
-            for h, (slots, cols) in enumerate(blocks):
-                nc.vector.scalar_tensor_tensor(woven(dh_masked[:, cols]), woven(relu_woven[:, cols]), 0.0,
-                                               rows_by_slot(dh[2 * g + h][:]), IS_GT, MULT)
-                nc.gpsimd.tensor_tensor(part(da, 1)[:, cols], dh_masked[:, cols], relu_woven[:, cols], MULT)
-                nc.gpsimd.tensor_tensor(woven(da[:, cols]), woven(dh_masked[:, cols]),
-                                        rows_by_slot(a3_sb[g][:, :, slots]), MULT)
-                leave_bank(2 * g + h)
+            for slots, cols in (blocks if period == 0 else [(slice(0, C), slice(0, WIDE))]):
+                nc.gpsimd.tensor_tensor(part(da, 1)[:, cols], dh_masked[g][:, cols], relu_woven[g][:, cols], MULT)
+                da1_on_gpsimd(g, da, slots, cols)
             mask = single([P, 2 * WIDE], BF16, "mask%d" % g)
-            da3 = single([P, 2 * WIDE], BF16, "da3_%d" % g)
-            unmasked = in_turn([P, 2 * WIDE], BF16, "unmasked%d" % g, place + 6)
+            da3 = in_turn([P, 2 * WIDE], BF16, "da3_%d" % g, 15)
+            unmasked = in_turn([P, 2 * WIDE], BF16, "unmasked%d" % g, 13)
             for i, e in enumerate((g + 1, g + 2)):
                 relu = relu_and_mask(e, part(mask, i))
                 for h in range(2):
                     times_dh(e, h, part(da3, i), relu)
                     times_dh(e, h, part(unmasked, i), a3_sb[e])
                     leave_bank(2 * e + h)
+            mask_dh(g + 3, HELD_AT[period + 1])
             for_w3 = quantise(in_turn([P, 2 * C], U32, "codes3_%d" % g, place), da3)
             da1 = in_turn([P, 2 * WIDE], BF16, "da1_%d" % g, place + 2)
             nc.vector.tensor_tensor(da1[:], unmasked[:], mask[:], MULT)
@@ -288,34 +304,44 @@ def tile_moe_bdx_glu_relu_kernel(
             for_w1 = quantise(in_turn([P, 2 * C], U32, "codes1_%d" % g, place + 1), da1)
             for i, e in enumerate((g + 1, g + 2)):
                 operands[e] = (for_w1[i], for_w3[i])
+            if period == 0:
+                da = in_turn([P, 2 * WIDE], BF16, "da%d" % (g + 3), place + 2)
 
         before, last = E - 2, E - 1
-        mask = single([P, 2 * WIDE], BF16, "mask_last")
-        unmasked = in_turn([P, 2 * WIDE], BF16, "unmasked_last", 10)
-        relu_before, relu_last = [relu_and_mask(e, part(mask, i)) for i, e in enumerate((before, last))]
+        da1_before = in_turn([P, WIDE], BF16, "da1_before", 6)
+        da1_on_gpsimd(before, da1_before, slice(0, C), slice(0, WIDE))
+        mask = single([P, WIDE], BF16, "mask_last")
+        relu_last = relu_and_mask(last, mask[:])
         for e in range(before):
             second_product(e, operands[e])
-        da_before, da_last = [single([P, 2 * WIDE], BF16, "da%d" % g) for g in BY_GPSIMD]
+        da3 = in_turn([P, 2 * WIDE], BF16, "da3_last", 7)
+        unmasked = in_turn([P, WIDE], BF16, "unmasked_last", 13)
+        for h, (slots, cols) in enumerate(blocks):
+            nc.vector.tensor_tensor(woven(da3[:, cols]), rows_by_slot(dh[2 * before + h][:]),
+                                    woven(relu_woven[before][:, cols]), MULT)
         for h in range(2):
-            times_dh(before, h, part(da_before, 1), relu_before)
-            times_dh(before, h, part(unmasked, 0), a3_sb[before])
-        nc.vector.tensor_tensor(part(da_before, 0), part(unmasked, 0), part(mask, 0), MULT)
-        times_dh(last, 0, part(da_last, 1), relu_last)
-        second_product(before, quantise(single([P, 2 * C], U32, "codes_before"), da_before))
-        times_dh(last, 1, part(da_last, 1), relu_last)
+            times_dh(last, h, part(da3, 1), relu_last)
         for h in range(2):
-            times_dh(last, h, part(unmasked, 1), a3_sb[last])
-        codes = single([P, 2 * C], U32, "codes_last")
-        scales = ring.tile([P, 2 * C], U8, name="scales", align_bytes=64, bufs=E)
-        acc = [psum.tile([P, C], F32, name="acc", tag="bank%d" % bank) for bank in (3, 6)]
-        for (slots, cols), m in zip(blocks, (1, 0)):
-            nc.vector.tensor_tensor(da_last[:, cols], part(unmasked, 1)[:, cols], part(mask, 1)[:, cols], MULT)
-            operand = (codes[:, m * C:(m + 1) * C], scales[:, m * C:(m + 1) * C])
-            nc.vector.quantize_mx(out=operand[0].bitcast(FP8X4), scales=operand[1], in_=part(da_last, m))
+            times_dh(last, h, unmasked, a3_sb[last])
+        acc = {(e, kb): psum.tile([P, C], F32, name="acc", tag="bank%d" % (2 + 4 * (e - before) + kb))
+               for e in (before, last) for kb in range(K // P)}
+        for_w3 = quantise(in_turn([P, 2 * C], U32, "codes3_last", 11), da3)
+        for i, e in enumerate((before, last)):
             for kb in range(K // P):
-                multiply(acc[kb][:], last, kb, m, operand, m == 1)
-        nc.vector.tensor_copy(dx[0][:, last * C:], acc[0][:])
-        nc.scalar.copy(dx[1][:, last * C:], acc[1][:])
+                multiply(acc[e, kb][:], e, kb, 1, for_w3[i], True)
+        da1_last = single([P, WIDE], BF16, "da1_last")
+        nc.vector.tensor_tensor(da1_last[:], unmasked[:], mask[:], MULT)
+        codes = single([P, 2 * C], U32, "codes1_last")
+        scales = ring.tile([P, 2 * C], U8, name="scales", align_bytes=64, bufs=E)
+        for i, (e, da1) in enumerate(((before, da1_before), (last, da1_last))):
+            operand = (codes[:, i * C:(i + 1) * C], scales[:, i * C:(i + 1) * C])
+            nc.vector.quantize_mx(out=operand[0].bitcast(FP8X4), scales=operand[1], in_=da1[:])
+            for kb in range(K // P):
+                multiply(acc[e, kb][:], e, kb, 0, operand, False)
+        for kb in range(K // P):
+            nc.scalar.copy(dx[kb][:, before * C:last * C], acc[before, kb][:])
+        for kb in range(K // P):
+            nc.vector.tensor_copy(dx[kb][:, last * C:], acc[last, kb][:])
 
         half_t = T // 2
         used = []

@@ -209,8 +209,8 @@ def tile_moe_bdx_glu_relu_kernel(
                     rhs_scale=w2s[:, (e * PASSES + s) * H:(e * PASSES + s + 1) * H],
                     start=(s == 0), stop=(s == PASSES - 1))
             dh_t = ring.tile([P, R, P], F32, name="dh_t%d" % b, tag="dh_t", bufs=6)
-            nc.scalar.activation(out=dh_t[:].rearrange("j (u v) p -> j u p v", v=2),
-                                 in_=sums[:].rearrange("j (p u v) -> j u p v", u=2, v=2),
+            nc.scalar.activation(out=dh_t[:],
+                                 in_=sums[:].rearrange("j (p r) -> j r p", r=R),
                                  func=ACT.Copy, scale=gate_col[:, b:b + 1])
             turned[b] = dh_t
 

@@ -57,7 +57,7 @@ def tile_moe_bdx_glu_relu_kernel(
         ident = keep.tile([P, P], F32, name="ident")
         dx = [keep.tile([P, S], F32, name="dx%d" % kb) for kb in range(K // P)]
 
-        nc.gpsimd.memset(dys[:, 0:T].bitcast(I32), 0)
+        nc.vector.memset(dys[:, 0:T].bitcast(I32), 0)
         nc.vector.memset(dys[:, T:].bitcast(I32), 0)
         nc.vector.memset(dyw[:, PASSES * T:], 0)
         make_identity(nc, ident[:])
@@ -175,7 +175,7 @@ def tile_moe_bdx_glu_relu_kernel(
                 start=start, stop=not start)
 
         def second_product(e, operands):
-            acc = psum.tile([P, K // P, C], F32, name="acc%d" % e, tag="bank%d" % (6, 7, 2, 3)[e % 4])
+            acc = psum.tile([P, K // P, C], F32, name="acc%d" % e, tag="bank%d" % (6, 7, 2, 3, 4, 5)[e])
             for kb in range(K // P):
                 for m in range(2):
                     multiply(acc[:, kb, :], e, kb, m, operands[m], m == 0)

@@ -26,6 +26,7 @@ ADD = mybir.AluOpType.add
 IS_GT = mybir.AluOpType.is_gt
 
 HELD_AT = (0, 4, 9)
+SCALES = 10
 EARLY = 2
 BY_GPSIMD = (0, 3)
 WIDE = R * C
@@ -161,7 +162,7 @@ def tile_moe_bdx_glu_relu_kernel(
         operands = {}
 
         def quantise(codes, da):
-            scales = ring.tile([P, 2 * C], U8, name="scales", align_bytes=64, bufs=E)
+            scales = ring.tile([P, 2 * C], U8, name="scales", align_bytes=64, bufs=SCALES)
             nc.vector.quantize_mx(out=codes[:].bitcast(FP8X4), scales=scales[:], in_=da[:])
             return [(codes[:, i * C:(i + 1) * C], scales[:, i * C:(i + 1) * C]) for i in range(2)]
 
@@ -175,7 +176,7 @@ def tile_moe_bdx_glu_relu_kernel(
                 start=start, stop=not start)
 
         def second_product(e, operands):
-            acc = psum.tile([P, K // P, C], F32, name="acc%d" % e, tag="bank%d" % (6, 7, 2, 3, 4, 5)[e])
+            acc = psum.tile([P, K // P, C], F32, name="acc%d" % e, tag="bank%d" % (6, 7, 2, 3, 7, 6)[e])
             for kb in range(K // P):
                 for m in range(2):
                     multiply(acc[:, kb, :], e, kb, m, operands[m], m == 0)
@@ -271,71 +272,92 @@ def tile_moe_bdx_glu_relu_kernel(
             for h, (slots, cols) in enumerate(blocks):
                 nc.vector.scalar_tensor_tensor(woven(dh_masked[g][:, cols]), woven(relu_woven[g][:, cols]), 0.0,
                                                rows_by_slot(dh[2 * g + h][:]), IS_GT, MULT)
-                if g < E - 2:
+                if g in BY_GPSIMD:
                     leave_bank(2 * g + h)
 
         def da1_on_gpsimd(g, da, slots, cols):
             nc.gpsimd.tensor_tensor(woven(da[:, cols]), woven(dh_masked[g][:, cols]),
                                     rows_by_slot(a3_sb[g][:, :, slots]), MULT)
 
-        for period in range(3):
-            weave_relu(3 * period, HELD_AT[period])
+        for g, place in zip((0, 3), HELD_AT):
+            weave_relu(g, place)
         mask_dh(0, 0)
         da = single([P, 2 * WIDE], BF16, "da0")
-        for period, g in enumerate(BY_GPSIMD):
-            place = 4 * period
-            for slots, cols in (blocks if period == 0 else [(slice(0, C), slice(0, WIDE))]):
-                nc.gpsimd.tensor_tensor(part(da, 1)[:, cols], dh_masked[g][:, cols], relu_woven[g][:, cols], MULT)
-                da1_on_gpsimd(g, da, slots, cols)
-            mask = single([P, 2 * WIDE], BF16, "mask%d" % g)
-            da3 = in_turn([P, 2 * WIDE], BF16, "da3_%d" % g, 15)
-            unmasked = in_turn([P, 2 * WIDE], BF16, "unmasked%d" % g, 13)
-            for i, e in enumerate((g + 1, g + 2)):
-                relu = relu_and_mask(e, part(mask, i))
-                for h in range(2):
-                    times_dh(e, h, part(da3, i), relu)
-                    times_dh(e, h, part(unmasked, i), a3_sb[e])
-                    leave_bank(2 * e + h)
-            mask_dh(g + 3, HELD_AT[period + 1])
-            for_w3 = quantise(in_turn([P, 2 * C], U32, "codes3_%d" % g, place), da3)
-            da1 = in_turn([P, 2 * WIDE], BF16, "da1_%d" % g, place + 2)
-            nc.vector.tensor_tensor(da1[:], unmasked[:], mask[:], MULT)
-            operands[g] = quantise(single([P, 2 * C], U32, "mask%d" % g), da)
-            for_w1 = quantise(in_turn([P, 2 * C], U32, "codes1_%d" % g, place + 1), da1)
-            for i, e in enumerate((g + 1, g + 2)):
-                operands[e] = (for_w1[i], for_w3[i])
-            if period == 0:
-                da = in_turn([P, 2 * WIDE], BF16, "da%d" % (g + 3), place + 2)
+        whole = (slice(0, C), slice(0, WIDE))
 
-        before, last = E - 2, E - 1
-        da1_before = in_turn([P, WIDE], BF16, "da1_before", 6)
-        da1_on_gpsimd(before, da1_before, slice(0, C), slice(0, WIDE))
-        mask = single([P, WIDE], BF16, "mask_last")
-        relu_last = relu_and_mask(last, mask[:])
-        for e in range(before):
-            second_product(e, operands[e])
-        da3 = in_turn([P, 2 * WIDE], BF16, "da3_last", 7)
-        unmasked = in_turn([P, WIDE], BF16, "unmasked_last", 13)
+        def da3_on_gpsimd(g, da, slots, cols):
+            nc.gpsimd.tensor_tensor(part(da, 1)[:, cols], dh_masked[g][:, cols], relu_woven[g][:, cols], MULT)
+
+        def products(e, mask, da3, unmasked):
+            relu = relu_and_mask(e, mask)
+            for h in range(2):
+                times_dh(e, h, da3, relu)
+                times_dh(e, h, unmasked, a3_sb[e])
+                leave_bank(2 * e + h)
+
+        def pair_of_products(e0, da3_at, unmasked_at):
+            mask = single([P, 2 * WIDE], BF16, "mask%d" % e0)
+            da3 = in_turn([P, 2 * WIDE], BF16, "da3_%d" % e0, da3_at)
+            unmasked = in_turn([P, 2 * WIDE], BF16, "unmasked%d" % e0, unmasked_at)
+            for i in range(2):
+                products(e0 + i, part(mask, i), part(da3, i), part(unmasked, i))
+            return mask, da3, unmasked
+
+        def quantise_one(codes, da_one):
+            scales = ring.tile([P, C], U8, name="scales", align_bytes=64, bufs=SCALES)
+            nc.vector.quantize_mx(out=codes.bitcast(FP8X4), scales=scales[:], in_=da_one)
+            return codes, scales[:]
+
+        for block in blocks:
+            da3_on_gpsimd(0, da, *block)
+            da1_on_gpsimd(0, da, *block)
+        mask, da3, unmasked = pair_of_products(1, 16, 14)
+        mask_dh(3, HELD_AT[1])
+        for_w3 = quantise(in_turn([P, 2 * C], U32, "codes3_1", 0), da3)
+        da1 = in_turn([P, 2 * WIDE], BF16, "da1_1", 2)
+        nc.vector.tensor_tensor(da1[:], unmasked[:], mask[:], MULT)
+        operands[0] = quantise(single([P, 2 * C], U32, "mask1"), da)
+        for_w1 = quantise(in_turn([P, 2 * C], U32, "codes1_1", 1), da1)
+        for i in range(2):
+            operands[1 + i] = (for_w1[i], for_w3[i])
+
+        da = in_turn([P, 2 * WIDE], BF16, "da3", 2)
+        da3_on_gpsimd(3, da, *whole)
+        da1_on_gpsimd(3, da, *whole)
+        mask4 = single([P, WIDE], BF16, "mask4")
+        da3 = in_turn([P, 2 * WIDE], BF16, "da3_4", 16)
+        unmasked4 = in_turn([P, WIDE], BF16, "unmasked4", 14)
+        products(4, mask4[:], part(da3, 0), unmasked4)
+        weave_relu(5, HELD_AT[2])
+        mask_dh(5, HELD_AT[2])
+        da1_5 = in_turn([P, WIDE], BF16, "da1_5", 8)
+        da1_on_gpsimd(5, da1_5, *whole)
         for h, (slots, cols) in enumerate(blocks):
-            nc.vector.tensor_tensor(woven(da3[:, cols]), rows_by_slot(dh[2 * before + h][:]),
-                                    woven(relu_woven[before][:, cols]), MULT)
-        for h in range(2):
-            times_dh(last, h, part(da3, 1), relu_last)
-        for h in range(2):
-            times_dh(last, h, unmasked, a3_sb[last])
-        acc = {(e, kb): psum.tile([P, C], F32, name="acc", tag="bank%d" % (2 + 4 * (e - before) + kb))
+            nc.vector.tensor_tensor(woven(part(da3, 1)[:, cols]), rows_by_slot(dh[10 + h][:]),
+                                    woven(relu_woven[5][:, cols]), MULT)
+        before, last = E - 2, E - 1
+        mask, da3_last, unmasked = pair_of_products(before, 18, 20)
+
+        operands[3] = quantise(in_turn([P, 2 * C], U32, "codes3", 11), da)
+        for e in range(4):
+            second_product(e, operands[e])
+        for_w3 = quantise(in_turn([P, 2 * C], U32, "codes3_4", 2), da3)
+        da1_4 = in_turn([P, WIDE], BF16, "da1_4", 12)
+        nc.vector.tensor_tensor(da1_4[:], unmasked4[:], mask4[:], MULT)
+        codes = in_turn([P, 2 * C], U32, "codes1_4", 13)
+        for e, da1_one in ((5, da1_5), (4, da1_4)):
+            second_product(e, (quantise_one(codes[:, (e - 4) * C:(e - 3) * C], da1_one[:]), for_w3[e - 4]))
+        da1 = in_turn([P, 2 * WIDE], BF16, "da1_last", 16)
+        nc.vector.tensor_tensor(da1[:], unmasked[:], mask[:], MULT)
+        acc = {(e, kb): psum.tile([P, C], F32, name="acc", tag="bank%d" % (4 * (last - e) + kb))
                for e in (before, last) for kb in range(K // P)}
-        for_w3 = quantise(in_turn([P, 2 * C], U32, "codes3_last", 11), da3)
+        for_w3 = quantise(in_turn([P, 2 * C], U32, "codes3_last", 14), da3_last)
         for i, e in enumerate((before, last)):
             for kb in range(K // P):
                 multiply(acc[e, kb][:], e, kb, 1, for_w3[i], True)
-        da1_last = single([P, WIDE], BF16, "da1_last")
-        nc.vector.tensor_tensor(da1_last[:], unmasked[:], mask[:], MULT)
-        codes = single([P, 2 * C], U32, "codes1_last")
-        scales = ring.tile([P, 2 * C], U8, name="scales", align_bytes=64, bufs=E)
-        for i, (e, da1) in enumerate(((before, da1_before), (last, da1_last))):
-            operand = (codes[:, i * C:(i + 1) * C], scales[:, i * C:(i + 1) * C])
-            nc.vector.quantize_mx(out=operand[0].bitcast(FP8X4), scales=operand[1], in_=da1[:])
+        codes = in_turn([P, 2 * C], U32, "codes1_last", 4)
+        for i, e in enumerate((before, last)):
+            operand = quantise_one(codes[:, i * C:(i + 1) * C], part(da1, i))
             for kb in range(K // P):
                 multiply(acc[e, kb][:], e, kb, 0, operand, False)
         for kb in range(K // P):

@@ -146,8 +146,8 @@ def tile_moe_bdx_glu_relu_kernel(
         load_w2_pair(4)
         load_a1(4, 2)
         load_w2_pair(6)
-        load_a3(4, 2)
         load_a1(6, 2)
+        load_a3(4, 2)
         load_a3(6, 2)
 
         g_words = {}
@@ -176,7 +176,7 @@ def tile_moe_bdx_glu_relu_kernel(
                 start=start, stop=not start)
 
         def second_product(e, operands):
-            acc = psum.tile([P, K // P, C], F32, name="acc%d" % e, tag="bank%d" % (6, 7, 2, 3, 7, 6)[e])
+            acc = psum.tile([P, K // P, C], F32, name="acc%d" % e, tag="bank%d" % (2, 3, 0, 1, 3, 2)[e])
             for kb in range(K // P):
                 for m in range(2):
                     multiply(acc[:, kb, :], e, kb, m, operands[m], m == 0)
@@ -214,10 +214,12 @@ def tile_moe_bdx_glu_relu_kernel(
                                  in_=sums[:].rearrange("j (p r) -> j r p", r=R),
                                  func=ACT.Copy, scale=gate_col[:, b:b + 1])
             turned[b] = dh_t
+            if b >= 14:
+                turn(b)
 
         def turn(b):
             dh_t = turned[b]
-            dh[b] = psum.tile([P, R, P], F32, name="dh%d" % b, tag="bank%d" % (b % 4 if b < 12 else (b - 8) % 6))
+            dh[b] = psum.tile([P, R, P], F32, name="dh%d" % b, tag="bank%d" % (b % 4 if b < 12 else 4 + b % 2 if b < 14 else 7 - b % 2))
             for r in range(R):
                 nc.tensor.transpose(dh[b][:, r, :], dh_t[:, r, :], ident[:])
 
@@ -226,16 +228,25 @@ def tile_moe_bdx_glu_relu_kernel(
         def single(shape, dtype, tag):
             return ring.tile(shape, dtype, name=tag, tag=tag, align_bytes=64, bufs=1)
 
-        def relu_and_mask(e, mask):
+        relus = {}
+
+        def make_relu(e):
             relu = ring.tile([P, R, C], F32, name="relu%d" % e, tag="relu", bufs=4)
             nc.scalar.activation(out=relu[:], in_=a1_sb[e], func=ACT.Relu)
+            return relu
+
+        def make_mask(mask, relu):
             nc.scalar.activation(out=woven_pairs(mask), in_=rows_by_pairs(relu[:]), func=ACT.Sign)
+
+        def relu_and_mask(e, mask):
+            relu = make_relu(e)
+            make_mask(mask, relu)
             return relu
 
         def leave_bank(b):
             if b < 8:
                 turn(b + DH_BANKS)
-            if b in (6, 7, 8, 9):
+            if b in (6, 7):
                 turn(b + 6)
             if b + DH_BANKS + AHEAD < S // P:
                 first_product(b + DH_BANKS + AHEAD)
@@ -327,7 +338,9 @@ def tile_moe_bdx_glu_relu_kernel(
         mask4 = single([P, WIDE], BF16, "mask4")
         da3 = in_turn([P, 2 * WIDE], BF16, "da3_4", 16)
         unmasked4 = in_turn([P, WIDE], BF16, "unmasked4", 14)
-        products(4, mask4[:], part(da3, 0), unmasked4)
+        relu4 = make_relu(4)
+        for h in range(2):
+            times_dh(4, h, part(da3, 0), relu4)
         weave_relu(5, HELD_AT[2])
         mask_dh(5, HELD_AT[2])
         da1_5 = in_turn([P, WIDE], BF16, "da1_5", 8)
@@ -335,8 +348,21 @@ def tile_moe_bdx_glu_relu_kernel(
         for h, (slots, cols) in enumerate(blocks):
             nc.vector.tensor_tensor(woven(part(da3, 1)[:, cols]), rows_by_slot(dh[10 + h][:]),
                                     woven(relu_woven[5][:, cols]), MULT)
+            leave_bank(10 + h)
         before, last = E - 2, E - 1
-        mask, da3_last, unmasked = pair_of_products(before, 18, 20)
+        mask = single([P, 2 * WIDE], BF16, "mask6")
+        da3_last = in_turn([P, 2 * WIDE], BF16, "da3_6", 18)
+        unmasked = in_turn([P, 2 * WIDE], BF16, "unmasked6", 20)
+        for i, e in enumerate((before, last)):
+            relus[e] = make_relu(e)
+            for h in range(2):
+                times_dh(e, h, part(da3_last, i), relus[e])
+        make_mask(mask4[:], relu4)
+        for i, e in enumerate((before, last)):
+            make_mask(part(mask, i), relus[e])
+        for e, product in ((4, unmasked4[:]), (before, part(unmasked, 0)), (last, part(unmasked, 1))):
+            for h in range(2):
+                times_dh(e, h, product, a3_sb[e])
 
         operands[3] = quantise(in_turn([P, 2 * C], U32, "codes3", 11), da)
         for e in range(4):
@@ -349,7 +375,7 @@ def tile_moe_bdx_glu_relu_kernel(
             second_product(e, (quantise_one(codes[:, (e - 4) * C:(e - 3) * C], da1_one[:]), for_w3[e - 4]))
         da1 = in_turn([P, 2 * WIDE], BF16, "da1_last", 16)
         nc.vector.tensor_tensor(da1[:], unmasked[:], mask[:], MULT)
-        acc = {(e, kb): psum.tile([P, C], F32, name="acc", tag="bank%d" % (4 * (last - e) + kb))
+        acc = {(e, kb): psum.tile([P, C], F32, name="acc", tag="bank%d" % (4 + 2 * (e - before) + kb))
                for e in (before, last) for kb in range(K // P)}
         for_w3 = quantise(in_turn([P, 2 * C], U32, "codes3_last", 14), da3_last)
         for i, e in enumerate((before, last)):

@@ -25,14 +25,19 @@ MULT = mybir.AluOpType.mult
 ADD = mybir.AluOpType.add
 IS_GT = mybir.AluOpType.is_gt
 
-HELD_AT = (0, 4, 9)
-SCALES = 10
 EARLY = 2
-BY_GPSIMD = (0, 3)
 WIDE = R * C
 DH_BANKS = 4
+AHEAD = 6
+SCALE_PLANES = 10
 WINDOW = 2048
 OVERLAP = 64
+RELU_AT = {0: 0, 3: 4, 5: 9}
+MASKED_AT = {g: place + 2 for g, place in RELU_AT.items()}
+DA1_GPSIMD_AT = 8
+CODES_AT = 13
+UNMASKED_AT, DA3_AT = 14, 16
+LAST_DA3_AT, LAST_UNMASKED_AT = 18, 20
 
 
 def tile_moe_bdx_glu_relu_kernel(
@@ -139,16 +144,12 @@ def tile_moe_bdx_glu_relu_kernel(
                 out=w13w[:, at:at + n * K * 2].bitcast(I32).rearrange("p (e b) -> p e b", e=n),
                 in_=(w1_words, w3_words)[m][e0:e0 + n, 0].rearrange("e p b -> p e b").bitcast(I32))
 
-        load_w2_pair(2)
-        load_a1(2, 2)
-        load_a3(0, 2)
-        load_a3(2, 2)
-        load_w2_pair(4)
-        load_a1(4, 2)
-        load_w2_pair(6)
-        load_a1(6, 2)
-        load_a3(4, 2)
-        load_a3(6, 2)
+        for e0 in range(EARLY, E, 2):
+            load_w2_pair(e0)
+            load_a1(e0, 2)
+            if e0 != E // 2:
+                load_a3(e0 - 2, 2)
+                load_a3(e0, 2)
 
         g_words = {}
         for e0, n in ((0, 2), (2, 2), (4, 4)):
@@ -159,12 +160,15 @@ def tile_moe_bdx_glu_relu_kernel(
                 for e in range(n):
                     g_words[e0 + e, s] = words[:, e * C:(e + 1) * C]
 
-        operands = {}
-
         def quantise(codes, da):
-            scales = ring.tile([P, 2 * C], U8, name="scales", align_bytes=64, bufs=SCALES)
+            scales = ring.tile([P, 2 * C], U8, name="scales", align_bytes=64, bufs=SCALE_PLANES)
             nc.vector.quantize_mx(out=codes[:].bitcast(FP8X4), scales=scales[:], in_=da[:])
             return [(codes[:, i * C:(i + 1) * C], scales[:, i * C:(i + 1) * C]) for i in range(2)]
+
+        def quantise_one(codes, da_part):
+            scales = ring.tile([P, C], U8, name="scales", align_bytes=64, bufs=SCALE_PLANES)
+            nc.vector.quantize_mx(out=codes.bitcast(FP8X4), scales=scales[:], in_=da_part)
+            return codes, scales[:]
 
         def multiply(acc, e, kb, m, operand, start):
             col = (m * E + e) * K + kb * P
@@ -175,8 +179,8 @@ def tile_moe_bdx_glu_relu_kernel(
                 rhs=operand[0].bitcast(FP8X4), rhs_scale=operand[1],
                 start=start, stop=not start)
 
-        def second_product(e, operands):
-            acc = psum.tile([P, K // P, C], F32, name="acc%d" % e, tag="bank%d" % (2, 3, 0, 1, 3, 2)[e])
+        def second_product(e, operands, bank):
+            acc = psum.tile([P, K // P, C], F32, name="acc%d" % e, tag="bank%d" % bank)
             for kb in range(K // P):
                 for m in range(2):
                     multiply(acc[:, kb, :], e, kb, m, operands[m], m == 0)
@@ -195,12 +199,20 @@ def tile_moe_bdx_glu_relu_kernel(
         def rows_by_pairs(ap):
             return ap.rearrange("p r (c i) -> p c r i", i=2)
 
-        dh, turned = {}, {}
-        AHEAD = 6
+        dh, gated = {}, {}
+        n_blocks = S // P
+
+        def sums_bank(b):
+            return 7 - b % (4 if b < n_blocks // 2 else 2)
+
+        def dh_bank(b):
+            if b < n_blocks - 4:
+                return b % DH_BANKS
+            return DH_BANKS + b % 2 if b < n_blocks - 2 else sums_bank(b)
 
         def first_product(b):
             e, h = divmod(b, 2)
-            sums = psum.tile([P, H], F32, name="sums%d" % b, tag="bank%d" % (7 - b % (4 if b < 8 else 2)))
+            sums = psum.tile([P, H], F32, name="sums%d" % b, tag="bank%d" % sums_bank(b))
             for s in range(PASSES):
                 nc.tensor.matmul_mx(
                     out=sums[:],
@@ -209,52 +221,45 @@ def tile_moe_bdx_glu_relu_kernel(
                     rhs=w2w[e][:, s * H * 2:(s + 1) * H * 2].bitcast(FP4X4),
                     rhs_scale=w2s[:, (e * PASSES + s) * H:(e * PASSES + s + 1) * H],
                     start=(s == 0), stop=(s == PASSES - 1))
-            dh_t = ring.tile([P, R, P], F32, name="dh_t%d" % b, tag="dh_t", bufs=6)
-            nc.scalar.activation(out=dh_t[:],
-                                 in_=sums[:].rearrange("j (p r) -> j r p", r=R),
+            gated[b] = ring.tile([P, R, P], F32, name="gated%d" % b, tag="gated", bufs=AHEAD)
+            nc.scalar.activation(out=gated[b][:], in_=sums[:].rearrange("j (p r) -> j r p", r=R),
                                  func=ACT.Copy, scale=gate_col[:, b:b + 1])
-            turned[b] = dh_t
-            if b >= 14:
+            if b >= n_blocks - 2:
                 turn(b)
 
         def turn(b):
-            dh_t = turned[b]
-            dh[b] = psum.tile([P, R, P], F32, name="dh%d" % b, tag="bank%d" % (b % 4 if b < 12 else 4 + b % 2 if b < 14 else 7 - b % 2))
+            dh[b] = psum.tile([P, R, P], F32, name="dh%d" % b, tag="bank%d" % dh_bank(b))
             for r in range(R):
-                nc.tensor.transpose(dh[b][:, r, :], dh_t[:, r, :], ident[:])
+                nc.tensor.transpose(dh[b][:, r, :], gated[b][:, r, :], ident[:])
 
         blocks = [(slice(h * P, (h + 1) * P), slice(h * R * P, (h + 1) * R * P)) for h in range(C // P)]
 
         def single(shape, dtype, tag):
             return ring.tile(shape, dtype, name=tag, tag=tag, align_bytes=64, bufs=1)
 
-        relus = {}
-
         def make_relu(e):
-            relu = ring.tile([P, R, C], F32, name="relu%d" % e, tag="relu", bufs=4)
-            nc.scalar.activation(out=relu[:], in_=a1_sb[e], func=ACT.Relu)
+            relu = ring.tile([P, WIDE], F32, name="relu%d" % e, tag="relu", bufs=4)
+            nc.scalar.activation(out=woven_pairs(relu[:]), in_=rows_by_pairs(a1_sb[e]), func=ACT.Relu)
             return relu
 
         def make_mask(mask, relu):
-            nc.scalar.activation(out=woven_pairs(mask), in_=rows_by_pairs(relu[:]), func=ACT.Sign)
-
-        def relu_and_mask(e, mask):
-            relu = make_relu(e)
-            make_mask(mask, relu)
-            return relu
+            nc.scalar.activation(out=mask, in_=relu[:], func=ACT.Sign)
 
         def leave_bank(b):
-            if b < 8:
-                turn(b + DH_BANKS)
-            if b in (6, 7):
-                turn(b + 6)
-            if b + DH_BANKS + AHEAD < S // P:
+            turn(b + DH_BANKS)
+            if b + AHEAD in (n_blocks - 4, n_blocks - 3):
+                turn(b + AHEAD)
+            if b + DH_BANKS + AHEAD < n_blocks:
                 first_product(b + DH_BANKS + AHEAD)
 
         def times_dh(e, h, product, rows):
             slots, cols = blocks[h]
             nc.vector.tensor_tensor(woven_pairs(product[:, cols]), rows_by_pairs(dh[2 * e + h][:]),
                                     rows_by_pairs(rows[:, :, slots]), MULT)
+
+        def times_relu(e, h, da3, relu):
+            cols = blocks[h][1]
+            nc.vector.tensor_tensor(woven(da3[:, cols]), rows_by_slot(dh[2 * e + h][:]), woven(relu[:, cols]), MULT)
 
         def part(tile, i):
             return tile[:, i * WIDE:(i + 1) * WIDE]
@@ -273,115 +278,108 @@ def tile_moe_bdx_glu_relu_kernel(
                 load_w13_words(m, e0, E // 2)
 
         relu_woven, dh_masked = {}, {}
+        whole = (slice(0, C), slice(0, WIDE))
 
-        def weave_relu(g, place):
-            relu_woven[g] = in_turn([P, WIDE], F32, "relu_woven%d" % g, place)
+        def weave_relu(g):
+            relu_woven[g] = in_turn([P, WIDE], F32, "relu_woven%d" % g, RELU_AT[g])
             nc.scalar.activation(out=woven_pairs(relu_woven[g][:]), in_=rows_by_pairs(a1_sb[g]), func=ACT.Relu)
 
-        def mask_dh(g, place):
-            dh_masked[g] = in_turn([P, WIDE], F32, "dh_masked%d" % g, place + 2)
+        def mask_dh(g):
+            dh_masked[g] = in_turn([P, WIDE], F32, "dh_masked%d" % g, MASKED_AT[g])
             for h, (slots, cols) in enumerate(blocks):
                 nc.vector.scalar_tensor_tensor(woven(dh_masked[g][:, cols]), woven(relu_woven[g][:, cols]), 0.0,
                                                rows_by_slot(dh[2 * g + h][:]), IS_GT, MULT)
-                if g in BY_GPSIMD:
+                if g < E // 2:
                     leave_bank(2 * g + h)
 
-        def da1_on_gpsimd(g, da, slots, cols):
-            nc.gpsimd.tensor_tensor(woven(da[:, cols]), woven(dh_masked[g][:, cols]),
+        def da1_on_gpsimd(g, da1, slots, cols):
+            nc.gpsimd.tensor_tensor(woven(da1[:, cols]), woven(dh_masked[g][:, cols]),
                                     rows_by_slot(a3_sb[g][:, :, slots]), MULT)
 
-        for g, place in zip((0, 3), HELD_AT):
-            weave_relu(g, place)
-        mask_dh(0, 0)
+        def da3_on_gpsimd(g, da3, cols):
+            nc.gpsimd.tensor_tensor(da3[:, cols], dh_masked[g][:, cols], relu_woven[g][:, cols], MULT)
+
+        def codes_at(name, place):
+            return in_turn([P, 2 * C], U32, name, place)
+
+        weave_relu(0)
+        weave_relu(3)
+        mask_dh(0)
         da = single([P, 2 * WIDE], BF16, "da0")
-        whole = (slice(0, C), slice(0, WIDE))
-
-        def da3_on_gpsimd(g, da, slots, cols):
-            nc.gpsimd.tensor_tensor(part(da, 1)[:, cols], dh_masked[g][:, cols], relu_woven[g][:, cols], MULT)
-
-        def products(e, mask, da3, unmasked):
-            relu = relu_and_mask(e, mask)
+        for slots, cols in blocks:
+            da3_on_gpsimd(0, part(da, 1), cols)
+            da1_on_gpsimd(0, da, slots, cols)
+        mask = single([P, 2 * WIDE], BF16, "mask1")
+        da3 = in_turn([P, 2 * WIDE], BF16, "da3_1", DA3_AT)
+        unmasked = in_turn([P, 2 * WIDE], BF16, "unmasked1", UNMASKED_AT)
+        for i, e in enumerate((1, 2)):
+            relu = make_relu(e)
+            make_mask(part(mask, i), relu)
             for h in range(2):
-                times_dh(e, h, da3, relu)
-                times_dh(e, h, unmasked, a3_sb[e])
+                times_relu(e, h, part(da3, i), relu)
+                times_dh(e, h, part(unmasked, i), a3_sb[e])
                 leave_bank(2 * e + h)
+        mask_dh(3)
 
-        def pair_of_products(e0, da3_at, unmasked_at):
-            mask = single([P, 2 * WIDE], BF16, "mask%d" % e0)
-            da3 = in_turn([P, 2 * WIDE], BF16, "da3_%d" % e0, da3_at)
-            unmasked = in_turn([P, 2 * WIDE], BF16, "unmasked%d" % e0, unmasked_at)
-            for i in range(2):
-                products(e0 + i, part(mask, i), part(da3, i), part(unmasked, i))
-            return mask, da3, unmasked
-
-        def quantise_one(codes, da_one):
-            scales = ring.tile([P, C], U8, name="scales", align_bytes=64, bufs=SCALES)
-            nc.vector.quantize_mx(out=codes.bitcast(FP8X4), scales=scales[:], in_=da_one)
-            return codes, scales[:]
-
-        for block in blocks:
-            da3_on_gpsimd(0, da, *block)
-            da1_on_gpsimd(0, da, *block)
-        mask, da3, unmasked = pair_of_products(1, 16, 14)
-        mask_dh(3, HELD_AT[1])
-        for_w3 = quantise(in_turn([P, 2 * C], U32, "codes3_1", 0), da3)
-        da1 = in_turn([P, 2 * WIDE], BF16, "da1_1", 2)
+        for_w3 = quantise(codes_at("codes3_1", RELU_AT[0]), da3)
+        da1 = in_turn([P, 2 * WIDE], BF16, "da1_1", MASKED_AT[0])
         nc.vector.tensor_tensor(da1[:], unmasked[:], mask[:], MULT)
-        operands[0] = quantise(single([P, 2 * C], U32, "mask1"), da)
-        for_w1 = quantise(in_turn([P, 2 * C], U32, "codes1_1", 1), da1)
-        for i in range(2):
-            operands[1 + i] = (for_w1[i], for_w3[i])
+        operands = {0: quantise(single([P, 2 * C], U32, "mask1"), da)}
+        for_w1 = quantise(codes_at("codes1_1", RELU_AT[0] + 1), da1)
+        for i, e in enumerate((1, 2)):
+            operands[e] = (for_w1[i], for_w3[i])
 
-        da = in_turn([P, 2 * WIDE], BF16, "da3", 2)
-        da3_on_gpsimd(3, da, *whole)
+        before, last = E - 2, E - 1
+        da = in_turn([P, 2 * WIDE], BF16, "da3", MASKED_AT[0])
+        da3_on_gpsimd(3, part(da, 1), whole[1])
         da1_on_gpsimd(3, da, *whole)
         mask4 = single([P, WIDE], BF16, "mask4")
-        da3 = in_turn([P, 2 * WIDE], BF16, "da3_4", 16)
-        unmasked4 = in_turn([P, WIDE], BF16, "unmasked4", 14)
-        relu4 = make_relu(4)
+        da3 = in_turn([P, 2 * WIDE], BF16, "da3_4", DA3_AT)
+        unmasked4 = in_turn([P, WIDE], BF16, "unmasked4", UNMASKED_AT)
+        relus = {4: make_relu(4)}
         for h in range(2):
-            times_dh(4, h, part(da3, 0), relu4)
-        weave_relu(5, HELD_AT[2])
-        mask_dh(5, HELD_AT[2])
-        da1_5 = in_turn([P, WIDE], BF16, "da1_5", 8)
+            times_relu(4, h, part(da3, 0), relus[4])
+        weave_relu(5)
+        mask_dh(5)
+        da1_5 = in_turn([P, WIDE], BF16, "da1_5", DA1_GPSIMD_AT)
         da1_on_gpsimd(5, da1_5, *whole)
-        for h, (slots, cols) in enumerate(blocks):
-            nc.vector.tensor_tensor(woven(part(da3, 1)[:, cols]), rows_by_slot(dh[10 + h][:]),
-                                    woven(relu_woven[5][:, cols]), MULT)
-            leave_bank(10 + h)
-        before, last = E - 2, E - 1
+        for h in range(2):
+            times_relu(5, h, part(da3, 1), relu_woven[5])
         mask = single([P, 2 * WIDE], BF16, "mask6")
-        da3_last = in_turn([P, 2 * WIDE], BF16, "da3_6", 18)
-        unmasked = in_turn([P, 2 * WIDE], BF16, "unmasked6", 20)
+        da3_last = in_turn([P, 2 * WIDE], BF16, "da3_6", LAST_DA3_AT)
+        unmasked = in_turn([P, 2 * WIDE], BF16, "unmasked6", LAST_UNMASKED_AT)
         for i, e in enumerate((before, last)):
             relus[e] = make_relu(e)
             for h in range(2):
-                times_dh(e, h, part(da3_last, i), relus[e])
-        make_mask(mask4[:], relu4)
-        for i, e in enumerate((before, last)):
-            make_mask(part(mask, i), relus[e])
-        for e, product in ((4, unmasked4[:]), (before, part(unmasked, 0)), (last, part(unmasked, 1))):
+                times_relu(e, h, part(da3_last, i), relus[e])
+        rest = ((4, mask4[:], unmasked4[:]), (before, part(mask, 0), part(unmasked, 0)),
+                (last, part(mask, 1), part(unmasked, 1)))
+        for e, mask_part, _ in rest:
+            make_mask(mask_part, relus[e])
+        for e, _, product in rest:
             for h in range(2):
                 times_dh(e, h, product, a3_sb[e])
 
-        operands[3] = quantise(in_turn([P, 2 * C], U32, "codes3", 11), da)
-        for e in range(4):
-            second_product(e, operands[e])
-        for_w3 = quantise(in_turn([P, 2 * C], U32, "codes3_4", 2), da3)
-        da1_4 = in_turn([P, WIDE], BF16, "da1_4", 12)
+        operands[3] = quantise(codes_at("codes3", MASKED_AT[5]), da)
+        for e in range(E // 2):
+            second_product(e, operands[e], (e + 2) % DH_BANKS)
+        for_w3 = quantise(codes_at("codes3_4", MASKED_AT[0]), da3)
+        da1_4 = in_turn([P, WIDE], BF16, "da1_4", MASKED_AT[5] + 1)
         nc.vector.tensor_tensor(da1_4[:], unmasked4[:], mask4[:], MULT)
-        codes = in_turn([P, 2 * C], U32, "codes1_4", 13)
-        for e, da1_one in ((5, da1_5), (4, da1_4)):
-            second_product(e, (quantise_one(codes[:, (e - 4) * C:(e - 3) * C], da1_one[:]), for_w3[e - 4]))
-        da1 = in_turn([P, 2 * WIDE], BF16, "da1_last", 16)
+        codes = codes_at("codes1_4", CODES_AT)
+        for n, (e, da1_part) in enumerate(((5, da1_5), (4, da1_4))):
+            i = e - 4
+            second_product(e, (quantise_one(codes[:, i * C:(i + 1) * C], da1_part[:]), for_w3[i]), 2 + n)
+
+        da1 = in_turn([P, 2 * WIDE], BF16, "da1_last", DA3_AT)
         nc.vector.tensor_tensor(da1[:], unmasked[:], mask[:], MULT)
-        acc = {(e, kb): psum.tile([P, C], F32, name="acc", tag="bank%d" % (4 + 2 * (e - before) + kb))
+        acc = {(e, kb): psum.tile([P, C], F32, name="acc", tag="bank%d" % (DH_BANKS + 2 * (e - before) + kb))
                for e in (before, last) for kb in range(K // P)}
-        for_w3 = quantise(in_turn([P, 2 * C], U32, "codes3_last", 14), da3_last)
+        for_w3 = quantise(codes_at("codes3_last", UNMASKED_AT), da3_last)
         for i, e in enumerate((before, last)):
             for kb in range(K // P):
                 multiply(acc[e, kb][:], e, kb, 1, for_w3[i], True)
-        codes = in_turn([P, 2 * C], U32, "codes1_last", 4)
+        codes = codes_at("codes1_last", RELU_AT[3])
         for i, e in enumerate((before, last)):
             operand = quantise_one(codes[:, i * C:(i + 1) * C], part(da1, i))
             for kb in range(K // P):

from contextlib import ExitStack

import concourse.mybir as mybir
from concourse.masks import make_identity

K, T, E, C, H, N = 256, 512, 8, 256, 512, 1024
S = E * C
P = 128
R = 4
PASSES = N // (P * R)
FLOPS = 2 * S * (N * H + 2 * H * K)
BYTES = (N * T + N * T // 32 + 2 * H * S * 4 + E * (N * H + 2 * H * K) // 2 + E * (N * H + 2 * H * K) // 32
         + S * 4 + P * (S + 4 * T) // 16 * 2 + K * T * 4)

F32 = mybir.dt.float32
BF16 = mybir.dt.bfloat16
I32 = mybir.dt.int32
U32 = mybir.dt.uint32
U16 = mybir.dt.uint16
U8 = mybir.dt.uint8
FP8X4 = mybir.dt.float8_e4m3fn_x4
FP4X4 = mybir.dt.float4_e2m1fn_x4
ACT = mybir.ActivationFunctionType
MULT = mybir.AluOpType.mult
ADD = mybir.AluOpType.add
IS_GT = mybir.AluOpType.is_gt

EARLY = 2
WIDE = R * C
DH_BANKS = 4
AHEAD = 6
SCALE_PLANES = 10
WINDOW = 2048
OVERLAP = 64
RELU_AT = {0: 0, 3: 4, 5: 9}
MASKED_AT = {g: place + 2 for g, place in RELU_AT.items()}
DA1_GPSIMD_AT = 8
CODES_AT = 13
UNMASKED_AT, DA3_AT = 14, 16
LAST_DA3_AT, LAST_UNMASKED_AT = 18, 20


def tile_moe_bdx_glu_relu_kernel(
        tc, dy_words, dy_scales, a1, a3, w2_words, w2_scales, w1_words, w1_scales, w3_words, w3_scales,
        gate, offs, pos1, pos2, pos3, pos4, out):
    nc = tc.nc
    with ExitStack() as ctx:
        keep = ctx.enter_context(tc.tile_pool(name="keep", bufs=1))
        ring = ctx.enter_context(tc.tile_pool(name="ring", bufs=3))
        psum = ctx.enter_context(tc.psum_pool(name="psum", bufs=1))

        offs_sb = keep.tile([P, S // 16], U16, name="offs_sb")
        pos_sb = [keep.tile([P, T // 16], U16, name="pos_sb%d" % r) for r in range(4)]
        dyw = keep.tile([P, T + WINDOW], I32, name="dyw", align_bytes=64)
        share = ctx.enter_context(tc.tile_pool(name="share", bufs=1))
        late_bytes = (2 * E - EARLY) * WIDE * 4
        dys = share.tile([P, WINDOW], U8, name="dys", align_bytes=64, offset=late_bytes - OVERLAP)
        gs0 = keep.tile([P, S], U8, name="gs0", align_bytes=64)
        gs1 = keep.tile([P, S], U8, name="gs1", align_bytes=64)
        w2s = keep.tile([P, E * PASSES * H], U8, name="w2s", align_bytes=64)
        gate_rows = keep.tile([P, P], F32, name="gate_rows")
        gate_col = keep.tile([P, S // P], F32, name="gate_col")
        ident = keep.tile([P, P], F32, name="ident")
        dx = [keep.tile([P, S], F32, name="dx%d" % kb) for kb in range(K // P)]

        nc.vector.memset(dys[:, 0:T].bitcast(I32), 0)
        nc.vector.memset(dys[:, T:].bitcast(I32), 0)
        nc.vector.memset(dyw[:, PASSES * T:], 0)
        make_identity(nc, ident[:])

        w2w, a1_sb, a3_sb = {}, {}, {}
        w2_bytes = PASSES * H * 2
        w13w_bytes = 2 * E * K * 2
        turns = ctx.enter_context(tc.tile_pool(name="turns", bufs=1))

        def in_turn(shape, dtype, name, place):
            return turns.tile(shape, dtype, name=name, align_bytes=64, offset=place * WIDE * 2)

        def load_w2(dst, e0, n):
            nc.sync.dma_start(
                out=dst.bitcast(I32).rearrange("p (g b) -> p g b", g=n * PASSES),
                in_=w2_words[e0:e0 + n].rearrange("e s p b -> p (e s) b").bitcast(I32))
            for e in range(n):
                w2w[e0 + e] = dst[:, e * w2_bytes:(e + 1) * w2_bytes]

        def load_saved(src, held, dst, e0, n):
            rows = dst.rearrange("p (r j) -> p r j", r=R)
            nc.sync.dma_start(out=rows, in_=src[:, e0 * C:(e0 + n) * C].rearrange("(p r) j -> p r j", r=R))
            for e in range(n):
                held[e0 + e] = rows[:, :, e * C:(e + 1) * C]

        def load_scales(plane, rows, groups):
            for r in range(4):
                nc.sync.dma_start(
                    out=plane[r:P:32, :].bitcast(I32).rearrange("q (g i) -> q g i", g=groups),
                    in_=rows[r:16:4].bitcast(I32))

        early_w2 = keep.tile([P, EARLY * w2_bytes], U8, name="early_w2", tag="early_w2", align_bytes=64)

        nc.sync.dma_start(offs_sb[:], offs)
        nc.sync.dma_start(out=gate_rows[:], in_=gate[0:P * P // S, :].rearrange("h (b p) -> (h b) p", p=P))
        for q in range(4):
            nc.sync.dma_start(out=dys[32 * q:32 * q + 4 * PASSES, 0:T].bitcast(I32),
                              in_=dy_scales[:, 4 * q:4 * q + 4, :].bitcast(I32))
        nc.sync.dma_start(out=dyw[:, 0:PASSES * T].rearrange("p (o t) -> p o t", o=PASSES),
                          in_=dy_words.rearrange("o p t d -> p o (t d)").bitcast(I32))
        load_saved(a1, a1_sb, keep.tile([P, EARLY * WIDE], F32, name="early_a1")[:], 0, EARLY)
        load_w2(early_w2[:], 0, EARLY)
        for r, pos in enumerate((pos1, pos2, pos3, pos4)):
            nc.sync.dma_start(pos_sb[r][:], pos)
        load_scales(w2s, w2_scales.rearrange("e s f i -> f (e s) i"), E * PASSES)

        gate_ps = psum.tile([P, P], F32, name="gate_ps", tag="bank%d" % (DH_BANKS + 1))
        nc.tensor.transpose(gate_ps[:], gate_rows[:], ident[:])
        nc.scalar.copy(gate_col[:], gate_ps[:, 0:S // P])

        for half in range(2):
            nc.vector.tensor_copy(gs0[:, half * S // 2:(half + 1) * S // 2],
                                  dys[:].indirect(offs_sb[:, half * S // 32:(half + 1) * S // 32]))
        for r in range(4):
            nc.sync.dma_start(out=gs1[r:P:32, :].bitcast(I32), in_=gs0[4 + r:P:32, :].bitcast(I32))
        g_scales = (gs0, gs1)

        saved = share.tile([P, late_bytes // 4], F32, name="saved", align_bytes=64, offset=0)
        weights = share.tile([P, w13w_bytes + (E - EARLY) * w2_bytes], U8, name="weights",
                             align_bytes=64, offset=late_bytes + WINDOW - 2 * OVERLAP)
        w13w = weights[:, 0:w13w_bytes]

        def load_a1(e0, n):
            at = (e0 - EARLY) * WIDE
            load_saved(a1, a1_sb, saved[:, at:at + n * WIDE], e0, n)

        def load_a3(e0, n):
            at = (E - EARLY + e0) * WIDE
            load_saved(a3, a3_sb, saved[:, at:at + n * WIDE], e0, n)

        def load_w2_pair(e0):
            at = w13w_bytes + (e0 - EARLY) * w2_bytes
            load_w2(weights[:, at:at + 2 * w2_bytes], e0, 2)

        def load_w13_words(m, e0, n):
            at = (m * E + e0) * K * 2
            nc.sync.dma_start(
                out=w13w[:, at:at + n * K * 2].bitcast(I32).rearrange("p (e b) -> p e b", e=n),
                in_=(w1_words, w3_words)[m][e0:e0 + n, 0].rearrange("e p b -> p e b").bitcast(I32))

        for e0 in range(EARLY, E, 2):
            load_w2_pair(e0)
            load_a1(e0, 2)
            if e0 != E // 2:
                load_a3(e0 - 2, 2)
                load_a3(e0, 2)

        g_words = {}
        for e0, n in ((0, 2), (2, 2), (4, 4)):
            for s in range(PASSES):
                words = keep.tile([P, n * C], U32, name="g_words%d_%d" % (e0, s), align_bytes=64)
                nc.vector.tensor_copy(words[:], dyw[:, s * T:s * T + WINDOW].bitcast(U32).indirect(
                    offs_sb[:, e0 * C // 16:(e0 + n) * C // 16]))
                for e in range(n):
                    g_words[e0 + e, s] = words[:, e * C:(e + 1) * C]

        def quantise(codes, da):
            scales = ring.tile([P, 2 * C], U8, name="scales", align_bytes=64, bufs=SCALE_PLANES)
            nc.vector.quantize_mx(out=codes[:].bitcast(FP8X4), scales=scales[:], in_=da[:])
            return [(codes[:, i * C:(i + 1) * C], scales[:, i * C:(i + 1) * C]) for i in range(2)]

        def quantise_one(codes, da_part):
            scales = ring.tile([P, C], U8, name="scales", align_bytes=64, bufs=SCALE_PLANES)
            nc.vector.quantize_mx(out=codes.bitcast(FP8X4), scales=scales[:], in_=da_part)
            return codes, scales[:]

        def multiply(acc, e, kb, m, operand, start):
            col = (m * E + e) * K + kb * P
            nc.tensor.matmul_mx(
                out=acc,
                lhsT=w13w[:, col * 2:(col + P) * 2].bitcast(FP4X4),
                lhsT_scale=w13s[:, col:col + P],
                rhs=operand[0].bitcast(FP8X4), rhs_scale=operand[1],
                start=start, stop=not start)

        def second_product(e, operands, bank):
            acc = psum.tile([P, K // P, C], F32, name="acc%d" % e, tag="bank%d" % bank)
            for kb in range(K // P):
                for m in range(2):
                    multiply(acc[:, kb, :], e, kb, m, operands[m], m == 0)
            for kb in range(K // P):
                nc.scalar.copy(dx[kb][:, e * C:(e + 1) * C], acc[:, kb, :])

        def woven(ap):
            return ap.rearrange("p (j r) -> p j r", r=R)

        def rows_by_slot(ap):
            return ap.rearrange("p r j -> p j r")

        def woven_pairs(ap):
            return ap.rearrange("p (c i r) -> p c r i", i=2, r=R)

        def rows_by_pairs(ap):
            return ap.rearrange("p r (c i) -> p c r i", i=2)

        dh, gated = {}, {}
        n_blocks = S // P

        def sums_bank(b):
            return 7 - b % (4 if b < n_blocks // 2 else 2)

        def dh_bank(b):
            if b < n_blocks - 4:
                return b % DH_BANKS
            return DH_BANKS + b % 2 if b < n_blocks - 2 else sums_bank(b)

        def first_product(b):
            e, h = divmod(b, 2)
            sums = psum.tile([P, H], F32, name="sums%d" % b, tag="bank%d" % sums_bank(b))
            for s in range(PASSES):
                nc.tensor.matmul_mx(
                    out=sums[:],
                    lhsT=g_words[e, s][:, h * P:(h + 1) * P].bitcast(FP8X4),
                    lhsT_scale=g_scales[s][:, b * P:(b + 1) * P],
                    rhs=w2w[e][:, s * H * 2:(s + 1) * H * 2].bitcast(FP4X4),
                    rhs_scale=w2s[:, (e * PASSES + s) * H:(e * PASSES + s + 1) * H],
                    start=(s == 0), stop=(s == PASSES - 1))
            gated[b] = ring.tile([P, R, P], F32, name="gated%d" % b, tag="gated", bufs=AHEAD)
            nc.scalar.activation(out=gated[b][:], in_=sums[:].rearrange("j (p r) -> j r p", r=R),
                                 func=ACT.Copy, scale=gate_col[:, b:b + 1])
            if b >= n_blocks - 2:
                turn(b)

        def turn(b):
            dh[b] = psum.tile([P, R, P], F32, name="dh%d" % b, tag="bank%d" % dh_bank(b))
            for r in range(R):
                nc.tensor.transpose(dh[b][:, r, :], gated[b][:, r, :], ident[:])

        blocks = [(slice(h * P, (h + 1) * P), slice(h * R * P, (h + 1) * R * P)) for h in range(C // P)]

        def single(shape, dtype, tag):
            return ring.tile(shape, dtype, name=tag, tag=tag, align_bytes=64, bufs=1)

        def make_relu(e):
            relu = ring.tile([P, WIDE], F32, name="relu%d" % e, tag="relu", bufs=4)
            nc.scalar.activation(out=woven_pairs(relu[:]), in_=rows_by_pairs(a1_sb[e]), func=ACT.Relu)
            return relu

        def make_mask(mask, relu):
            nc.scalar.activation(out=mask, in_=relu[:], func=ACT.Sign)

        def leave_bank(b):
            turn(b + DH_BANKS)
            if b + AHEAD in (n_blocks - 4, n_blocks - 3):
                turn(b + AHEAD)
            if b + DH_BANKS + AHEAD < n_blocks:
                first_product(b + DH_BANKS + AHEAD)

        def times_dh(e, h, product, rows):
            slots, cols = blocks[h]
            nc.vector.tensor_tensor(woven_pairs(product[:, cols]), rows_by_pairs(dh[2 * e + h][:]),
                                    rows_by_pairs(rows[:, :, slots]), MULT)

        def times_relu(e, h, da3, relu):
            cols = blocks[h][1]
            nc.vector.tensor_tensor(woven(da3[:, cols]), rows_by_slot(dh[2 * e + h][:]), woven(relu[:, cols]), MULT)

        def part(tile, i):
            return tile[:, i * WIDE:(i + 1) * WIDE]

        for b in range(DH_BANKS):
            first_product(b)
            turn(b)
        for b in range(DH_BANKS, DH_BANKS + AHEAD):
            first_product(b)

        w13s = keep.tile([P, 2 * E * K], U8, name="w13s", tag="early_w2", align_bytes=64)
        for m, w_scales in enumerate((w1_scales, w3_scales)):
            load_scales(w13s[:, m * E * K:(m + 1) * E * K], w_scales[:, 0].rearrange("e f k -> f e k"), E)
        for e0 in (0, E // 2):
            for m in range(2):
                load_w13_words(m, e0, E // 2)

        relu_woven, dh_masked = {}, {}
        whole = (slice(0, C), slice(0, WIDE))

        def weave_relu(g):
            relu_woven[g] = in_turn([P, WIDE], F32, "relu_woven%d" % g, RELU_AT[g])
            nc.scalar.activation(out=woven_pairs(relu_woven[g][:]), in_=rows_by_pairs(a1_sb[g]), func=ACT.Relu)

        def mask_dh(g):
            dh_masked[g] = in_turn([P, WIDE], F32, "dh_masked%d" % g, MASKED_AT[g])
            for h, (slots, cols) in enumerate(blocks):
                nc.vector.scalar_tensor_tensor(woven(dh_masked[g][:, cols]), woven(relu_woven[g][:, cols]), 0.0,
                                               rows_by_slot(dh[2 * g + h][:]), IS_GT, MULT)
                if g < E // 2:
                    leave_bank(2 * g + h)

        def da1_on_gpsimd(g, da1, slots, cols):
            nc.gpsimd.tensor_tensor(woven(da1[:, cols]), woven(dh_masked[g][:, cols]),
                                    rows_by_slot(a3_sb[g][:, :, slots]), MULT)

        def da3_on_gpsimd(g, da3, cols):
            nc.gpsimd.tensor_tensor(da3[:, cols], dh_masked[g][:, cols], relu_woven[g][:, cols], MULT)

        def codes_at(name, place):
            return in_turn([P, 2 * C], U32, name, place)

        weave_relu(0)
        weave_relu(3)
        mask_dh(0)
        da = single([P, 2 * WIDE], BF16, "da0")
        for slots, cols in blocks:
            da3_on_gpsimd(0, part(da, 1), cols)
            da1_on_gpsimd(0, da, slots, cols)
        mask = single([P, 2 * WIDE], BF16, "mask1")
        da3 = in_turn([P, 2 * WIDE], BF16, "da3_1", DA3_AT)
        unmasked = in_turn([P, 2 * WIDE], BF16, "unmasked1", UNMASKED_AT)
        for i, e in enumerate((1, 2)):
            relu = make_relu(e)
            make_mask(part(mask, i), relu)
            for h in range(2):
                times_relu(e, h, part(da3, i), relu)
                times_dh(e, h, part(unmasked, i), a3_sb[e])
                leave_bank(2 * e + h)
        mask_dh(3)

        for_w3 = quantise(codes_at("codes3_1", RELU_AT[0]), da3)
        da1 = in_turn([P, 2 * WIDE], BF16, "da1_1", MASKED_AT[0])
        nc.vector.tensor_tensor(da1[:], unmasked[:], mask[:], MULT)
        operands = {0: quantise(single([P, 2 * C], U32, "mask1"), da)}
        for_w1 = quantise(codes_at("codes1_1", RELU_AT[0] + 1), da1)
        for i, e in enumerate((1, 2)):
            operands[e] = (for_w1[i], for_w3[i])

        before, last = E - 2, E - 1
        da = in_turn([P, 2 * WIDE], BF16, "da3", MASKED_AT[0])
        da3_on_gpsimd(3, part(da, 1), whole[1])
        da1_on_gpsimd(3, da, *whole)
        mask4 = single([P, WIDE], BF16, "mask4")
        da3 = in_turn([P, 2 * WIDE], BF16, "da3_4", DA3_AT)
        unmasked4 = in_turn([P, WIDE], BF16, "unmasked4", UNMASKED_AT)
        relus = {4: make_relu(4)}
        for h in range(2):
            times_relu(4, h, part(da3, 0), relus[4])
        weave_relu(5)
        mask_dh(5)
        da1_5 = in_turn([P, WIDE], BF16, "da1_5", DA1_GPSIMD_AT)
        da1_on_gpsimd(5, da1_5, *whole)
        for h in range(2):
            times_relu(5, h, part(da3, 1), relu_woven[5])
        mask = single([P, 2 * WIDE], BF16, "mask6")
        da3_last = in_turn([P, 2 * WIDE], BF16, "da3_6", LAST_DA3_AT)
        unmasked = in_turn([P, 2 * WIDE], BF16, "unmasked6", LAST_UNMASKED_AT)
        for i, e in enumerate((before, last)):
            relus[e] = make_relu(e)
            for h in range(2):
                times_relu(e, h, part(da3_last, i), relus[e])
        rest = ((4, mask4[:], unmasked4[:]), (before, part(mask, 0), part(unmasked, 0)),
                (last, part(mask, 1), part(unmasked, 1)))
        for e, mask_part, _ in rest:
            make_mask(mask_part, relus[e])
        for e, _, product in rest:
            for h in range(2):
                times_dh(e, h, product, a3_sb[e])

        operands[3] = quantise(codes_at("codes3", MASKED_AT[5]), da)
        for e in range(E // 2):
            second_product(e, operands[e], (e + 2) % DH_BANKS)
        for_w3 = quantise(codes_at("codes3_4", MASKED_AT[0]), da3)
        da1_4 = in_turn([P, WIDE], BF16, "da1_4", MASKED_AT[5] + 1)
        nc.vector.tensor_tensor(da1_4[:], unmasked4[:], mask4[:], MULT)
        codes = codes_at("codes1_4", CODES_AT)
        for n, (e, da1_part) in enumerate(((5, da1_5), (4, da1_4))):
            i = e - 4
            second_product(e, (quantise_one(codes[:, i * C:(i + 1) * C], da1_part[:]), for_w3[i]), 2 + n)

        da1 = in_turn([P, 2 * WIDE], BF16, "da1_last", DA3_AT)
        nc.vector.tensor_tensor(da1[:], unmasked[:], mask[:], MULT)
        acc = {(e, kb): psum.tile([P, C], F32, name="acc", tag="bank%d" % (DH_BANKS + 2 * (e - before) + kb))
               for e in (before, last) for kb in range(K // P)}
        for_w3 = quantise(codes_at("codes3_last", UNMASKED_AT), da3_last)
        for i, e in enumerate((before, last)):
            for kb in range(K // P):
                multiply(acc[e, kb][:], e, kb, 1, for_w3[i], True)
        codes = codes_at("codes1_last", RELU_AT[3])
        for i, e in enumerate((before, last)):
            operand = quantise_one(codes[:, i * C:(i + 1) * C], part(da1, i))
            for kb in range(K // P):
                multiply(acc[e, kb][:], e, kb, 0, operand, False)
        for kb in range(K // P):
            nc.scalar.copy(dx[kb][:, before * C:last * C], acc[before, kb][:])
        for kb in range(K // P):
            nc.vector.tensor_copy(dx[kb][:, last * C:], acc[last, kb][:])

        half_t = T // 2
        used = []

        def fresh():
            used.append(share.tile([P, half_t], F32, name="value%d" % len(used), offset=len(used) * half_t * 4))
            return used[-1][:]

        def picked(piece, r):
            kb, h = divmod(piece, 2)
            return dx[kb][:].indirect(pos_sb[r][:, h * half_t // 16:(h + 1) * half_t // 16])

        def fetch(piece, r):
            value = fresh()
            nc.scalar.activation(out=value, in_=picked(piece, r), func=ACT.Copy)
            return value

        def add(first, second):
            value = fresh()
            nc.vector.tensor_tensor(value, first, second, ADD)
            return value

        def store(piece, value):
            kb, h = divmod(piece, 2)
            nc.sync.dma_start(out=out[kb * P:(kb + 1) * P, h * half_t:(h + 1) * half_t], in_=value)

        fetched = {(0, 1): fresh()}
        nc.vector.tensor_copy(fetched[0, 1], picked(0, 1))
        fetched[0, 0] = fetch(0, 0)
        for r in range(2):
            fetched[1, r] = fetch(1, r)
        for r in range(3):
            for piece in (2, 3):
                fetched[piece, r] = fetch(piece, r)
        sums0 = [add(picked(0, 2 + r), fetched[0, r]) for r in range(2)]
        sums1 = [add(picked(1, 2), fetched[1, 0])]
        store(0, add(*sums0))
        sums1.append(add(picked(1, 3), fetched[1, 1]))
        running = [add(picked(2, 3), fetched[2, 0])]
        store(1, add(*sums1))
        running.append(add(picked(3, 3), fetched[3, 0]))
        running = [add(running[h], fetched[2 + h, 1]) for h in range(2)]
        for h in range(2):
            store(2 + h, add(running[h], fetched[2 + h, 2]))
